import numpy as np
import ml_dtypes


def mxq(x, axis, fmt="e4m3"):
    dtype, down = {"e4m3": (ml_dtypes.float8_e4m3fn, 7), "e5m2": (ml_dtypes.float8_e5m2, 14)}[fmt]
    v = np.moveaxis(np.asarray(x, np.float32).astype(ml_dtypes.bfloat16).astype(np.float64), axis, -1)
    blocks = v.reshape(v.shape[:-1] + (-1, 32))
    amax = np.abs(blocks).max(-1, keepdims=True)
    byte = np.maximum(np.where(amax > 0, np.frexp(amax)[1] - 1 + 127, 0) - down, 1)
    scale = np.exp2(byte - 127.0)
    codes = (blocks / scale).astype(np.float32).astype(dtype).astype(np.float64)
    return np.moveaxis((codes * scale).reshape(v.shape), -1, axis)


WIDE = False


def mx_kscale(k):
    if not WIDE:
        return np.ones(k)
    levels = np.array([10, -10, 5, -5, 0])
    if k % 512:
        return np.exp2(np.random.permutation(np.resize(levels, k // 32))).repeat(32)
    a = np.empty((k // 512, 16))
    for p in range(k // 512):
        a[p, :8] = np.random.permutation(np.resize(levels, 8))
        for g in range(8):
            far = levels[np.abs(levels - a[p, g]) >= 10]
            a[p, g + 8] = far[np.random.randint(len(far))]
    return np.exp2(a.ravel()).repeat(32)


BF16 = ml_dtypes.bfloat16


def bf(x):
    return np.asarray(x, np.float32).astype(BF16)


def f64(x):
    return np.asarray(x).astype(np.float64)


E2M1 = np.array([0.0, 0.5, 1.0, 1.5, 2.0, 3.0, 4.0, 6.0, -0.0, -0.5, -1.0, -1.5, -2.0, -3.0, -4.0, -6.0])


def pack_weight(w, fmt):
    k, n = w.shape
    w = f64(bf(w)).reshape(k // 32, 32, n)
    amax = np.abs(w).max(1)
    if fmt == "e4m3":
        byte = np.frexp(amax)[1] - 1 + 127 - 7
    else:
        mant, ex = np.frexp(amax / 6.0)
        byte = np.where(mant > 0.5, ex, ex - 1) + 127
    byte = np.clip(np.where(amax > 0, byte, 1), 1, 254)
    scaled = (w * np.exp2(127.0 - byte)[:, None, :]).reshape(k, n).astype(np.float32)
    by_word = np.ascontiguousarray(scaled.reshape(k // 512, 128, 4, n).transpose(0, 1, 3, 2))
    if fmt == "e4m3":
        words = by_word.astype(ml_dtypes.float8_e4m3fn).view(np.uint8)
    else:
        c = by_word.astype(ml_dtypes.float4_e2m1fn).view(np.uint8) & 0xF
        words = c[..., 0::2] | (c[..., 1::2] << 4)
    return np.ascontiguousarray(words), np.ascontiguousarray(byte.astype(np.uint8).reshape(k // 512, 16, n))


def unpack_weight(words, scales, fmt):
    g, p, n, _ = words.shape
    if fmt == "e4m3":
        vals = np.ascontiguousarray(words).view(ml_dtypes.float8_e4m3fn).astype(np.float64)
    else:
        nib = np.empty((g, p, n, 4), np.uint8)
        nib[..., 0::2] = words & 0xF
        nib[..., 1::2] = words >> 4
        vals = E2M1[nib]
    vals = vals * np.repeat(np.exp2(scales.astype(np.float64) - 127.0), 8, axis=1)[..., None]
    return vals.transpose(0, 1, 3, 2).reshape(g * 512, n)
def pack4(w):
    words, scales = pack_weight(w, "e2m1")
    return words.reshape(words.shape[0], 128, -1), scales


def unpack4(words, scales):
    return unpack_weight(words.reshape(words.shape[0], 128, -1, 2), scales, "e2m1")


def planes(Y):
    n, m = Y.shape
    b = f64(bf(Y)).reshape(n // 32, 32, m)
    amax = np.abs(b).max(1)
    byte = np.clip(np.where(amax > 0, np.frexp(amax)[1] - 1 + 127 - 7, 1), 1, 254)
    codes = (b * np.exp2(127.0 - byte)[:, None, :]).reshape(n, m).astype(np.float32).astype(ml_dtypes.float8_e4m3fn).view(np.uint8)
    words = codes.reshape(n // 512, 128, 4, m).transpose(0, 1, 3, 2)
    return np.ascontiguousarray(words), np.ascontiguousarray(byte.astype(np.uint8).reshape(n // 512, 16, m))


I, J, D, N = 512, 1536, 1024, 1024

def sigmoid(v):
    return 1.0 / (1.0 + np.exp(-v))

def setup_inputs():
    sd, sj = mx_kscale(D), mx_kscale(J)
    x_words, x_scales = pack_weight(np.random.randn(D, I) / np.sqrt(D) / sd[:, None], "e4m3")
    U = bf(np.random.randn(J, D) * sd[None, :] * sj[:, None])
    w_words, w_scales = pack4(np.random.randn(D, N) / np.sqrt(D) / sd[:, None])
    Z = bf(np.sign(np.random.randn(I, J) - 0.5))
    c = bf(np.exp(0.3 * np.random.randn(J)) / sj)
    b = bf(0.5 * np.random.randn(J) - 0.5)
    a = bf(2.0 / np.sqrt(J) * np.exp(0.3 * np.random.randn(I)))
    gain = bf(np.exp(0.8 * np.random.randn(N)))
    return {"x_words": x_words, "x_scales": x_scales, "U": U, "w_words": w_words, "w_scales": w_scales,
            "Z": Z, "c": c, "b": b, "a": a, "gain": gain}

def reference(x_words, x_scales, U, w_words, w_scales, Z, c, b, a, gain):
    X = unpack_weight(x_words, x_scales, "e4m3")
    W = unpack4(w_words, w_scales)
    Uq = mxq(f64(U), 1, "e4m3")
    Z, c = f64(Z), f64(c)
    logits = (X.T @ Uq.T) * c + f64(b)
    R = -Z * sigmoid(-Z * logits) * c
    B = Uq @ W
    y = (mxq(R, 1, "e4m3") @ mxq(B, 0, "e4m3")) * f64(a)[:, None] * f64(gain)
    Y = y.T
    words, scales = planes(Y)
    return y, words, scales

@@ -1,0 +1,395 @@
+from contextlib import ExitStack
+
+import concourse.mybir as mybir
+from concourse.masks import make_identity
+
+I, J, D, N = 512, 1536, 1024, 1024
+FLOPS = 2 * I * J * D + 2 * J * D * N + 2 * I * J * N
+
+F32 = mybir.dt.float32
+BF16 = mybir.dt.bfloat16
+I32 = mybir.dt.int32
+U32 = mybir.dt.uint32
+U8 = mybir.dt.uint8
+FP8X4 = mybir.dt.float8_e4m3fn_x4
+FP4X4 = mybir.dt.float4_e2m1fn_x4
+ALU = mybir.AluOpType
+ACT = mybir.ActivationFunctionType
+
+P = 128
+G = J // 512
+DG = D // 512
+NH = N // 512
+IT = I // P
+
+
+def tile_siglip_image_feature_gradient_k4_kernel(
+    tc, x_words, x_scales, U, w_words, w_scales, Z, c, b, a, gain, out_0, out_1, out_2
+):
+    nc = tc.nc
+    with ExitStack() as ctx:
+        keep = ctx.enter_context(tc.tile_pool(name="keep", bufs=1))
+        work = ctx.enter_context(tc.tile_pool(name="work", bufs=2))
+        psum = ctx.enter_context(tc.psum_pool(name="psum", bufs=8))
+        ctx.enter_context(tc.manual_schedule())
+
+        def kept(name, shape, dtype):
+            return keep.tile(shape, dtype, name=name, align_bytes=64)
+
+        def bank(name):
+            return psum.tile([P, 512], F32, name=name, tag="bank")
+
+        ident = kept("ident", [P, P], F32)
+        warm = kept("warm", [P, 16], F32)
+        c_sb = kept("c_sb", [P, G, 4], BF16)
+        b_sb = kept("b_sb", [P, G, 4], BF16)
+        a_sb = kept("a_sb", [P, IT, 2], BF16)
+        c_neg = kept("c_neg", [P, G, 4], BF16)
+        c_safe = kept("c_safe", [P, G * 4], F32)
+        c_inv = kept("c_inv", [P, G * 4], F32)
+        b_over_c = kept("b_over_c", [P, G * 4], F32)
+        gain_sb = kept("gain_sb", [P, N], BF16)
+        xw = kept("xw", [P, DG, I], U32)
+        xs = kept("xs", [P, DG, I], U8)
+        ww = [kept("ww%d" % h, [P, DG, 1024], U8) for h in range(NH)]
+        ws = kept("ws", [P, DG, N], U8)
+        u_raw = [kept("u_raw%d" % g, [P, 4, D], BF16) for g in range(G)]
+        z_raw = [kept("z_raw%d" % g, [P, IT, 512], BF16) for g in range(G)]
+        uc = [[kept("uc%d_%d" % (g, t), [P, DG * P], U32) for t in range(4)] for g in range(G)]
+        us = [[kept("us%d_%d" % (g, t), [P, DG * P], U8) for t in range(4)] for g in range(G)]
+        zc = [kept("zc%d" % g, [P, I, 4], BF16) for g in range(G)]
+        rc = [kept("rc%d" % g, [P, I], U32) for g in range(G)]
+        rs = [kept("rs%d" % g, [P, I], U8) for g in range(G)]
+        bc = [[kept("bc%d_%d" % (g, h), [P, 512], U32) for h in range(NH)] for g in range(G)]
+        bs = [[kept("bs%d_%d" % (g, h), [P, 512], U8) for h in range(NH)] for g in range(G)]
+        yg = [kept("yg%d" % h, [P, I, 4], BF16) for h in range(NH)]
+        yc = [kept("yc%d" % h, [P, I], U32) for h in range(NH)]
+        ys = [kept("ys%d" % h, [P, I], U8) for h in range(NH)]
+        live = {}
+
+        def load_u(g, t0, t1):
+            rows = U[512 * g : 512 * (g + 1), :].rearrange("(m t) k -> m t k", t=4)
+            nc.sync.dma_start(out=u_raw[g][:, t0:t1, :], in_=rows[:, t0:t1, :])
+
+        def load_z(g):
+            nc.sync.dma_start(
+                out=z_raw[g][:], in_=Z[:, 512 * g : 512 * (g + 1)].rearrange("(r p) j -> p r j", p=P)
+            )
+
+        def load_w(h):
+            src = w_words.rearrange("g p n -> p g n")[:, :, 1024 * h : 1024 * (h + 1)]
+            nc.sync.dma_start(out=ww[h][:].bitcast(I32), in_=src.bitcast(I32))
+
+        def load_scales(plane, src):
+            for q in range(4):
+                nc.sync.dma_start(
+                    out=plane[32 * q : 32 * q + 4, :, :].bitcast(I32),
+                    in_=src[:, 4 * q : 4 * q + 4, :].rearrange("g r n -> r g n").bitcast(I32),
+                )
+
+        def u_turn(g, t):
+            bk = bank("bk_u")
+            words = u_raw[g][:, t, :].bitcast(F32)
+            for d in range(DG):
+                for u in range(2):
+                    s = 2 * d + u
+                    nc.tensor.transpose(
+                        bk[:, P * s : P * (s + 1)], words[:, 256 * d + u : 256 * (d + 1) : 2], ident[:]
+                    )
+            live["u_bank", g, t] = bk
+
+        def u_copy(g, t):
+            ug = work.tile([P, 1024], BF16, name="ug", tag="ug", bufs=4, align_bytes=64)
+            nc.scalar.copy(
+                out=ug[:].bitcast(F32).rearrange("p (d m u) -> p d m u", d=DG, u=2),
+                in_=live["u_bank", g, t][:].rearrange("p (d u m) -> p d m u", d=DG, u=2),
+            )
+            live["ug", g, t] = ug
+
+        def u_quant(g, t):
+            nc.vector.quantize_mx(out=uc[g][t][:].bitcast(FP8X4), scales=us[g][t][:], in_=live["ug", g, t][:])
+
+        def z_turn(g, ih):
+            bk = bank("bk_z")
+            for r in range(2):
+                words = z_raw[g][:, 2 * ih + r, :].bitcast(F32)
+                for u in range(2):
+                    col = 256 * u + P * r
+                    nc.tensor.transpose(bk[:, col : col + P], words[:, u:256:2], ident[:])
+            live["z_bank", g, ih] = bk
+
+        def z_scale(g, ih):
+            nc.vector.tensor_tensor(
+                out=zc[g][:, 256 * ih : 256 * (ih + 1), :].rearrange("p i (u e) -> p i u e", u=2),
+                in0=live["z_bank", g, ih][:].bitcast(BF16).rearrange("p (u i e) -> p i u e", u=2, e=2),
+                in1=c_neg[:, g, :].rearrange("p (u e) -> p u e", u=2).unsqueeze(1).broadcast_to([P, 256, 2, 2]),
+                op=ALU.mult,
+            )
+
+        def logits(g, t):
+            bk = bank("bk_l")
+            for d in range(DG):
+                nc.tensor.matmul_mx(
+                    out=bk[:],
+                    lhsT=uc[g][t][:, P * d : P * (d + 1)].bitcast(FP8X4),
+                    lhsT_scale=us[g][t][:, P * d : P * (d + 1)],
+                    rhs=xw[:, d, :].bitcast(FP8X4),
+                    rhs_scale=xs[:, d, :],
+                    start=(d == 0),
+                    stop=(d == DG - 1),
+                )
+            live["l_bank", g, t] = bk
+
+        def margin(g, t):
+            mg = work.tile([P, I], F32, name="mg", tag="mg", bufs=3, align_bytes=64)
+            nc.vector.scalar_tensor_tensor(
+                out=mg[:],
+                in0=live["l_bank", g, t][:],
+                scalar=b_over_c[:, 4 * g + t : 4 * g + t + 1],
+                in1=zc[g][:, :, t],
+                op0=ALU.add,
+                op1=ALU.mult,
+            )
+            live["mg", g, t] = mg
+
+        def sigmoid(g, t):
+            if t == 0:
+                live["sg", g] = work.tile([P, 4, I], F32, name="sg", tag="sg", align_bytes=64)
+            nc.scalar.activation(out=live["sg", g][:, t, :], in_=live["mg", g, t][:], func=ACT.Sigmoid)
+
+        def r_make(g, ih):
+            if ih == 0:
+                live["rb", g] = work.tile([P, I, 4], BF16, name="rb", tag="rb", align_bytes=64)
+            cols = slice(256 * ih, 256 * (ih + 1))
+            nc.vector.tensor_tensor(
+                out=live["rb", g][:, cols, :].rearrange("p (x i) t -> p x t i", i=4),
+                in0=live["sg", g][:, :, cols].rearrange("p t (x i) -> p x t i", i=4),
+                in1=zc[g][:, cols, :].rearrange("p (x i) t -> p x t i", i=4),
+                op=ALU.mult,
+            )
+
+        def r_quant(g):
+            nc.vector.quantize_mx(
+                out=rc[g][:].bitcast(FP8X4), scales=rs[g][:], in_=live["rb", g][:].rearrange("p i t -> p (i t)")
+            )
+
+        def b_mul(g, h, s):
+            bk = bank("bk_b")
+            for t in range(4):
+                for d in range(DG):
+                    nc.tensor.matmul_mx(
+                        out=bk[:, P * t : P * (t + 1)],
+                        lhsT=uc[g][t][:, P * d : P * (d + 1)].bitcast(FP8X4),
+                        lhsT_scale=us[g][t][:, P * d : P * (d + 1)],
+                        rhs=ww[h][:, d, 256 * s : 256 * (s + 1)].bitcast(FP4X4),
+                        rhs_scale=ws[:, d, 512 * h + P * s : 512 * h + P * (s + 1)],
+                        start=(d == 0),
+                        stop=(d == DG - 1),
+                    )
+            live["b_bank", g, h, s] = bk
+
+        def b_copy(g, h, s):
+            if s % 2 == 0:
+                live["bb", g, h, s // 2] = work.tile([P, 256, 4], BF16, name="bb", tag="bb", bufs=3, align_bytes=64)
+            dst = live["bb", g, h, s // 2][:, P * (s % 2) : P * (s % 2 + 1), :]
+            nc.scalar.copy(out=dst, in_=live["b_bank", g, h, s][:].rearrange("p (t n) -> p n t", t=4))
+
+        def b_pair(g, h, sp):
+            for s in (2 * sp, 2 * sp + 1):
+                b_mul(g, h, s)
+                b_copy(g, h, s)
+
+        def b_quant(g, h, sp):
+            cols = slice(256 * sp, 256 * (sp + 1))
+            nc.vector.quantize_mx(
+                out=bc[g][h][:, cols].bitcast(FP8X4),
+                scales=bs[g][h][:, cols],
+                in_=live["bb", g, h, sp][:].rearrange("p n t -> p (n t)"),
+            )
+
+        def y_mul(h, r):
+            bk = bank("bk_y")
+            for g in range(G):
+                nc.tensor.matmul_mx(
+                    out=bk[:],
+                    lhsT=rc[g][:, P * r : P * (r + 1)].bitcast(FP8X4),
+                    lhsT_scale=rs[g][:, P * r : P * (r + 1)],
+                    rhs=bc[g][h][:].bitcast(FP8X4),
+                    rhs_scale=bs[g][h][:],
+                    start=(g == 0),
+                    stop=(g == G - 1),
+                )
+            live["y_bank", h, r] = bk
+
+        def y_scale(h, r):
+            yf = work.tile([P, 512], F32, name="yf", tag="yf", bufs=8, align_bytes=64)
+            nc.vector.scalar_tensor_tensor(
+                out=yf[:],
+                in0=live["y_bank", h, r][:],
+                scalar=a_sb[:, r, 0:1],
+                in1=gain_sb[:, 512 * h : 512 * (h + 1)],
+                op0=ALU.mult,
+                op1=ALU.mult,
+            )
+            nc.sync.dma_start(out=out_0[P * r : P * (r + 1), 512 * h : 512 * (h + 1)], in_=yf[:])
+            live["yf", h, r] = yf
+
+        def y_round(h, r, on_scalar):
+            yb = work.tile([P, 512], BF16, name="yb", tag="yb", bufs=4, align_bytes=64)
+            dst = yb[:].rearrange("q (u p e) -> q u p e", u=2, e=2)
+            src = live["yf", h, r][:].rearrange("q (p u e) -> q u p e", u=2, e=2)
+            if on_scalar:
+                nc.scalar.copy(out=dst, in_=src)
+            else:
+                nc.vector.tensor_copy(out=dst, in_=src)
+            live["yb", h, r] = yb
+
+        def y_turn(h, rows):
+            bk = bank("bk_t")
+            for k, r in enumerate(rows):
+                words = live["yb", h, r][:].bitcast(F32)
+                for u in range(2):
+                    col = P * (2 * k + u)
+                    nc.tensor.transpose(bk[:, col : col + P], words[:, P * u : P * (u + 1)], ident[:])
+            live["t_bank", h, rows[0]] = bk
+
+        def y_copy(h, rows):
+            n = len(rows)
+            dst = yg[h][:, P * rows[0] : P * (rows[0] + n), :].rearrange("p i t -> p (i t)").bitcast(F32)
+            nc.scalar.copy(
+                out=dst.rearrange("p (k i u) -> p k i u", k=n, u=2),
+                in_=live["t_bank", h, rows[0]][:, 0 : 256 * n].rearrange("p (k u i) -> p k i u", k=n, u=2),
+            )
+
+        def y_quant(h, rows):
+            cols = slice(P * rows[0], P * (rows[0] + len(rows)))
+            nc.vector.quantize_mx(
+                out=yc[h][:, cols].bitcast(FP8X4),
+                scales=ys[h][:, cols],
+                in_=yg[h][:, cols, :].rearrange("p i t -> p (i t)"),
+            )
+
+        def store_words(h, rows):
+            cols = slice(P * rows[0], P * (rows[0] + len(rows)))
+            dst = out_1[h].rearrange("p m t -> p (m t)").bitcast(I32)
+            nc.sync.dma_start(out=dst[:, cols], in_=yc[h][:, cols].bitcast(I32))
+
+        def store_scales(h, queues):
+            for q in range(4):
+                queues[q % len(queues)].dma_start(
+                    out=out_2[h, 4 * q : 4 * q + 4, :].bitcast(I32), in_=ys[h][32 * q : 32 * q + 4, :].bitcast(I32)
+                )
+
+        nc.vector.memset(xs[:].rearrange("p g n -> p (g n)").bitcast(I32), 0)
+        nc.vector.memset(ws[:].rearrange("p g n -> p (g n)").bitcast(I32), 0)
+        nc.vector.memset(warm[:, 0:8], 0.0)
+        nc.scalar.activation(out=warm[:, 8:16], in_=warm[:, 0:8], func=ACT.Sigmoid)
+        make_identity(nc, ident[:])
+        nc.gpsimd.dma_start(out=c_sb[:], in_=c.rearrange("(g p t) -> p g t", g=G, t=4))
+        nc.gpsimd.dma_start(out=b_sb[:], in_=b.rearrange("(g p t) -> p g t", g=G, t=4))
+        with nc.allow_non_contiguous_dma(reason="one value of a to each partition"):
+            nc.gpsimd.dma_start(out=a_sb[:, :, 0], in_=a.rearrange("(r p) -> p r", p=P))
+        load_u(0, 0, 1)
+        load_u(0, 1, 2)
+        load_u(0, 2, 4)
+        load_z(0)
+        nc.sync.dma_start(
+            out=xw[:].bitcast(I32), in_=x_words.rearrange("g p n t -> p g (n t)").bitcast(I32)
+        )
+        load_scales(xs, x_scales)
+        load_scales(ws, w_scales)
+        load_w(0)
+        for g in range(1, G):
+            load_z(g)
+            load_u(g, 0, 2)
+            load_u(g, 2, 4)
+        load_w(1)
+        nc.sync.dma_start(out=gain_sb[:], in_=gain.partition_broadcast(P))
+
+        c_flat = c_sb[:].rearrange("p g t -> p (g t)")
+        nc.vector.tensor_scalar(
+            out=c_neg[:].rearrange("p g t -> p (g t)"), in0=c_flat, scalar1=-1.0, scalar2=None, op0=ALU.mult
+        )
+        nc.vector.scalar_tensor_tensor(
+            out=c_safe[:], in0=c_flat, scalar=0.0, in1=c_flat, op0=ALU.is_equal, op1=ALU.add
+        )
+        nc.vector.reciprocal(out=c_inv[:], in_=c_safe[:])
+        nc.vector.tensor_tensor(
+            out=b_over_c[:], in0=c_inv[:], in1=b_sb[:].rearrange("p g t -> p (g t)"), op=ALU.mult
+        )
+
+        for t in range(4):
+            u_turn(0, t)
+            u_copy(0, t)
+            u_quant(0, t)
+        for ih in range(2):
+            z_turn(0, ih)
+            z_scale(0, ih)
+
+        for g in range(G):
+            more = g + 1 < G
+            for t in range(4):
+                logits(g, t)
+                margin(g, t)
+                sigmoid(g, t)
+                if t == 0 and g > 0:
+                    b_quant(g - 1, 0, 1)
+            if more:
+                for ih in range(2):
+                    z_turn(g + 1, ih)
+                    z_scale(g + 1, ih)
+            b_pair(g, 0, 0)
+            r_make(g, 0)
+            r_make(g, 1)
+            b_quant(g, 0, 0)
+            if more:
+                for t in range(4):
+                    u_turn(g + 1, t)
+                    u_copy(g + 1, t)
+                    u_quant(g + 1, t)
+                    if t == 0:
+                        r_quant(g)
+            else:
+                r_quant(g)
+            b_pair(g, 0, 1)
+
+        b_pair(0, 1, 0)
+        b_quant(G - 1, 0, 1)
+        b_pair(0, 1, 1)
+        b_quant(0, 1, 0)
+        pairs = [(g, sp) for g in range(1, G) for sp in range(2)]
+        done = (0, 1)
+        for r in range(IT):
+            y_mul(0, r)
+            b_pair(pairs[r][0], 1, pairs[r][1])
+            y_scale(0, r)
+            b_quant(done[0], 1, done[1])
+            y_round(0, r, False)
+            done = pairs[r]
+        y_turn(0, [0, 1])
+        y_turn(0, [2, 3])
+        b_quant(done[0], 1, done[1])
+        y_copy(0, [0, 1])
+        y_copy(0, [2, 3])
+        y_mul(1, 0)
+        y_quant(0, [0, 1, 2, 3])
+        store_words(0, [0, 1, 2, 3])
+        store_scales(0, [nc.sync])
+        y_scale(1, 0)
+        y_round(1, 0, True)
+        for r in range(1, IT):
+            y_mul(1, r)
+            y_scale(1, r)
+            y_round(1, r, True)
+        y_turn(1, [0, 1])
+        y_copy(1, [0, 1])
+        y_turn(1, [2])
+        y_turn(1, [3])
+        y_quant(1, [0, 1])
+        y_copy(1, [2])
+        y_copy(1, [3])
+        store_words(1, [0, 1])
+        y_quant(1, [2])
+        y_quant(1, [3])
+        store_words(1, [2, 3])
+        store_scales(1, [nc.scalar, nc.sync])

@@ -51,7 +51,7 @@ def tile_siglip_image_feature_gradient_k4_kernel(
         gain_sb = kept("gain_sb", [P, N], BF16)
         xw = kept("xw", [P, DG, I], U32)
         xs = kept("xs", [P, DG, I], U8)
-        ww = [kept("ww%d" % h, [P, DG, 1024], U8) for h in range(NH)]
+        ww = kept("ww", [P, DG, 2 * N], U8)
         ws = kept("ws", [P, DG, N], U8)
         u_raw = [kept("u_raw%d" % g, [P, 4, D], BF16) for g in range(G)]
         z_raw = [kept("z_raw%d" % g, [P, IT, 512], BF16) for g in range(G)]
@@ -64,7 +64,7 @@ def tile_siglip_image_feature_gradient_k4_kernel(
         bs = [[kept("bs%d_%d" % (g, h), [P, 512], U8) for h in range(NH)] for g in range(G)]
         yg = [kept("yg%d" % h, [P, I, 4], BF16) for h in range(NH)]
         yc = [kept("yc%d" % h, [P, I], U32) for h in range(NH)]
-        ys = [kept("ys%d" % h, [P, I], U8) for h in range(NH)]
+        ys = kept("ys", [P, I], U8)
         live = {}
 
         def load_u(g, t0, t1):
@@ -75,10 +75,6 @@ def tile_siglip_image_feature_gradient_k4_kernel(
             nc.sync.dma_start(
                 out=z_raw[g][:], in_=Z[:, 512 * g : 512 * (g + 1)].rearrange("(r p) j -> p r j", p=P)
             )
-
-        def load_w(h):
-            src = w_words.rearrange("g p n -> p g n")[:, :, 1024 * h : 1024 * (h + 1)]
-            nc.sync.dma_start(out=ww[h][:].bitcast(I32), in_=src.bitcast(I32))
 
         def load_scales(plane, src):
             for q in range(4):
@@ -168,9 +164,12 @@ def tile_siglip_image_feature_gradient_k4_kernel(
                 op=ALU.mult,
             )
 
-        def r_quant(g):
+        def r_quant(g, ih):
+            cols = slice(256 * ih, 256 * (ih + 1))
             nc.vector.quantize_mx(
-                out=rc[g][:].bitcast(FP8X4), scales=rs[g][:], in_=live["rb", g][:].rearrange("p i t -> p (i t)")
+                out=rc[g][:, cols].bitcast(FP8X4),
+                scales=rs[g][:, cols],
+                in_=live["rb", g][:, cols, :].rearrange("p i t -> p (i t)"),
             )
 
         def b_mul(g, h, s):
@@ -181,7 +180,7 @@ def tile_siglip_image_feature_gradient_k4_kernel(
                         out=bk[:, P * t : P * (t + 1)],
                         lhsT=uc[g][t][:, P * d : P * (d + 1)].bitcast(FP8X4),
                         lhsT_scale=us[g][t][:, P * d : P * (d + 1)],
-                        rhs=ww[h][:, d, 256 * s : 256 * (s + 1)].bitcast(FP4X4),
+                        rhs=ww[:, d, 1024 * h + 256 * s : 1024 * h + 256 * (s + 1)].bitcast(FP4X4),
                         rhs_scale=ws[:, d, 512 * h + P * s : 512 * h + P * (s + 1)],
                         start=(d == 0),
                         stop=(d == DG - 1),
@@ -190,7 +189,7 @@ def tile_siglip_image_feature_gradient_k4_kernel(
 
         def b_copy(g, h, s):
             if s % 2 == 0:
-                live["bb", g, h, s // 2] = work.tile([P, 256, 4], BF16, name="bb", tag="bb", bufs=3, align_bytes=64)
+                live["bb", g, h, s // 2] = work.tile([P, 256, 4], BF16, name="bb", tag="bb", bufs=4, align_bytes=64)
             dst = live["bb", g, h, s // 2][:, P * (s % 2) : P * (s % 2 + 1), :]
             nc.scalar.copy(out=dst, in_=live["b_bank", g, h, s][:].rearrange("p (t n) -> p n t", t=4))
 
@@ -244,6 +243,21 @@ def tile_siglip_image_feature_gradient_k4_kernel(
                 nc.vector.tensor_copy(out=dst, in_=src)
             live["yb", h, r] = yb
 
+        def y_round_from_bank(h, r):
+            yb = work.tile([P, 512], BF16, name="yb", tag="yb", bufs=4, align_bytes=64)
+            src = live["y_bank", h, r][:].rearrange("q (p u e) -> q u p e", u=2, e=2)
+            gn = gain_sb[:, 512 * h : 512 * (h + 1)].rearrange("q (p u e) -> q u p e", u=2, e=2)
+            for u in range(2):
+                nc.vector.scalar_tensor_tensor(
+                    out=yb[:, 256 * u : 256 * (u + 1)].rearrange("q (p e) -> q p e", e=2),
+                    in0=src[:, u],
+                    scalar=a_sb[:, r, 0:1],
+                    in1=gn[:, u],
+                    op0=ALU.mult,
+                    op1=ALU.mult,
+                )
+            live["yb", h, r] = yb
+
         def y_turn(h, rows):
             bk = bank("bk_t")
             for k, r in enumerate(rows):
@@ -253,10 +267,11 @@ def tile_siglip_image_feature_gradient_k4_kernel(
                     nc.tensor.transpose(bk[:, col : col + P], words[:, P * u : P * (u + 1)], ident[:])
             live["t_bank", h, rows[0]] = bk
 
-        def y_copy(h, rows):
+        def y_copy(h, rows, on_scalar=True):
             n = len(rows)
+            copy = nc.scalar.copy if on_scalar else nc.vector.tensor_copy
             dst = yg[h][:, P * rows[0] : P * (rows[0] + n), :].rearrange("p i t -> p (i t)").bitcast(F32)
-            nc.scalar.copy(
+            copy(
                 out=dst.rearrange("p (k i u) -> p k i u", k=n, u=2),
                 in_=live["t_bank", h, rows[0]][:, 0 : 256 * n].rearrange("p (k u i) -> p k i u", k=n, u=2),
             )
@@ -265,7 +280,7 @@ def tile_siglip_image_feature_gradient_k4_kernel(
             cols = slice(P * rows[0], P * (rows[0] + len(rows)))
             nc.vector.quantize_mx(
                 out=yc[h][:, cols].bitcast(FP8X4),
-                scales=ys[h][:, cols],
+                scales=ys[4 * h :, cols],
                 in_=yg[h][:, cols, :].rearrange("p i t -> p (i t)"),
             )
 
@@ -274,38 +289,44 @@ def tile_siglip_image_feature_gradient_k4_kernel(
             dst = out_1[h].rearrange("p m t -> p (m t)").bitcast(I32)
             nc.sync.dma_start(out=dst[:, cols], in_=yc[h][:, cols].bitcast(I32))
 
-        def store_scales(h, queues):
+        def store_scales():
             for q in range(4):
-                queues[q % len(queues)].dma_start(
-                    out=out_2[h, 4 * q : 4 * q + 4, :].bitcast(I32), in_=ys[h][32 * q : 32 * q + 4, :].bitcast(I32)
+                queue = nc.scalar if q % 2 == 0 else nc.sync
+                queue.dma_start(
+                    out=out_2[:, 4 * q : 4 * q + 4, :].bitcast(I32), in_=ys[32 * q : 32 * q + 8, :].bitcast(I32)
                 )
 
         nc.vector.memset(xs[:].rearrange("p g n -> p (g n)").bitcast(I32), 0)
         nc.vector.memset(ws[:].rearrange("p g n -> p (g n)").bitcast(I32), 0)
         nc.vector.memset(warm[:, 0:8], 0.0)
-        nc.scalar.activation(out=warm[:, 8:16], in_=warm[:, 0:8], func=ACT.Sigmoid)
         make_identity(nc, ident[:])
         nc.gpsimd.dma_start(out=c_sb[:], in_=c.rearrange("(g p t) -> p g t", g=G, t=4))
         nc.gpsimd.dma_start(out=b_sb[:], in_=b.rearrange("(g p t) -> p g t", g=G, t=4))
-        with nc.allow_non_contiguous_dma(reason="one value of a to each partition"):
-            nc.gpsimd.dma_start(out=a_sb[:, :, 0], in_=a.rearrange("(r p) -> p r", p=P))
+        nc.scalar.activation(out=warm[:, 8:16], in_=warm[:, 0:8], func=ACT.Sigmoid)
         load_u(0, 0, 1)
         load_u(0, 1, 2)
         load_u(0, 2, 4)
         load_z(0)
+        load_scales(xs, x_scales)
         nc.sync.dma_start(
             out=xw[:].bitcast(I32), in_=x_words.rearrange("g p n t -> p g (n t)").bitcast(I32)
         )
-        load_scales(xs, x_scales)
+        load_z(1)
         load_scales(ws, w_scales)
-        load_w(0)
-        for g in range(1, G):
-            load_z(g)
-            load_u(g, 0, 2)
-            load_u(g, 2, 4)
-        load_w(1)
+        nc.sync.dma_start(out=ww[:].bitcast(I32), in_=w_words.rearrange("g p n -> p g n").bitcast(I32))
+        load_u(1, 0, 2)
+        load_u(1, 2, 4)
+        load_z(2)
+        load_u(2, 0, 2)
+        load_u(2, 2, 4)
+        with nc.allow_non_contiguous_dma(reason="one value of a to each partition"):
+            nc.sync.dma_start(out=a_sb[:, :, 0], in_=a.rearrange("(r p) -> p r", p=P))
         nc.sync.dma_start(out=gain_sb[:], in_=gain.partition_broadcast(P))
 
+        for t in range(2):
+            u_turn(0, t)
+            u_copy(0, t)
+            u_quant(0, t)
         c_flat = c_sb[:].rearrange("p g t -> p (g t)")
         nc.vector.tensor_scalar(
             out=c_neg[:].rearrange("p g t -> p (g t)"), in0=c_flat, scalar1=-1.0, scalar2=None, op0=ALU.mult
@@ -318,7 +339,7 @@ def tile_siglip_image_feature_gradient_k4_kernel(
             out=b_over_c[:], in0=c_inv[:], in1=b_sb[:].rearrange("p g t -> p (g t)"), op=ALU.mult
         )
 
-        for t in range(4):
+        for t in range(2, 4):
             u_turn(0, t)
             u_copy(0, t)
             u_quant(0, t)
@@ -333,63 +354,65 @@ def tile_siglip_image_feature_gradient_k4_kernel(
                 margin(g, t)
                 sigmoid(g, t)
                 if t == 0 and g > 0:
-                    b_quant(g - 1, 0, 1)
+                    b_quant(g - 1, 1, 1)
             if more:
                 for ih in range(2):
                     z_turn(g + 1, ih)
                     z_scale(g + 1, ih)
             b_pair(g, 0, 0)
             r_make(g, 0)
-            r_make(g, 1)
+            b_pair(g, 0, 1)
             b_quant(g, 0, 0)
+            r_quant(g, 0)
+            r_make(g, 1)
+            b_quant(g, 0, 1)
+            r_quant(g, 1)
             if more:
                 for t in range(4):
                     u_turn(g + 1, t)
                     u_copy(g + 1, t)
                     u_quant(g + 1, t)
-                    if t == 0:
-                        r_quant(g)
-            else:
-                r_quant(g)
-            b_pair(g, 0, 1)
+            b_pair(g, 1, 0)
+            b_pair(g, 1, 1)
+            b_quant(g, 1, 0)
 
-        b_pair(0, 1, 0)
-        b_quant(G - 1, 0, 1)
-        b_pair(0, 1, 1)
-        b_quant(0, 1, 0)
-        pairs = [(g, sp) for g in range(1, G) for sp in range(2)]
-        done = (0, 1)
-        for r in range(IT):
+        y_mul(0, 0)
+        b_quant(G - 1, 1, 1)
+        y_scale(0, 0)
+        y_round(0, 0, True)
+        for r in range(1, IT):
             y_mul(0, r)
-            b_pair(pairs[r][0], 1, pairs[r][1])
             y_scale(0, r)
-            b_quant(done[0], 1, done[1])
-            y_round(0, r, False)
-            done = pairs[r]
+            y_round(0, r, True)
+        y_mul(1, 0)
+        y_scale(1, 0)
+        y_mul(1, 1)
+        y_round(1, 0, False)
         y_turn(0, [0, 1])
         y_turn(0, [2, 3])
-        b_quant(done[0], 1, done[1])
+        y_turn(1, [0])
+        y_scale(1, 1)
         y_copy(0, [0, 1])
         y_copy(0, [2, 3])
-        y_mul(1, 0)
-        y_quant(0, [0, 1, 2, 3])
+        y_mul(1, 2)
+        y_quant(0, [0, 1])
+        y_round(1, 1, True)
+        y_scale(1, 2)
+        y_copy(1, [0])
+        y_quant(0, [2, 3])
         store_words(0, [0, 1, 2, 3])
-        store_scales(0, [nc.sync])
-        y_scale(1, 0)
-        y_round(1, 0, True)
-        for r in range(1, IT):
-            y_mul(1, r)
-            y_scale(1, r)
-            y_round(1, r, True)
-        y_turn(1, [0, 1])
-        y_copy(1, [0, 1])
+        y_mul(1, 3)
+        y_round(1, 2, True)
+        y_round_from_bank(1, 3)
+        y_turn(1, [1])
         y_turn(1, [2])
         y_turn(1, [3])
-        y_quant(1, [0, 1])
+        y_scale(1, 3)
+        y_copy(1, [1])
         y_copy(1, [2])
-        y_copy(1, [3])
+        y_copy(1, [3], False)
+        y_quant(1, [0, 1])
         store_words(1, [0, 1])
-        y_quant(1, [2])
-        y_quant(1, [3])
+        y_quant(1, [2, 3])
         store_words(1, [2, 3])
-        store_scales(1, [nc.scalar, nc.sync])
+        store_scales()

@@ -40,7 +40,6 @@ def tile_siglip_image_feature_gradient_k4_kernel(
             return psum.tile([P, 512], F32, name=name, tag="bank")
 
         ident = kept("ident", [P, P], F32)
-        warm = kept("warm", [P, 16], F32)
         c_sb = kept("c_sb", [P, G, 4], BF16)
         b_sb = kept("b_sb", [P, G, 4], BF16)
         a_sb = kept("a_sb", [P, IT, 2], BF16)
@@ -55,8 +54,8 @@ def tile_siglip_image_feature_gradient_k4_kernel(
         ws = kept("ws", [P, DG, N], U8)
         u_raw = [kept("u_raw%d" % g, [P, 4, D], BF16) for g in range(G)]
         z_raw = [kept("z_raw%d" % g, [P, IT, 512], BF16) for g in range(G)]
-        uc = [[kept("uc%d_%d" % (g, t), [P, DG * P], U32) for t in range(4)] for g in range(G)]
-        us = [[kept("us%d_%d" % (g, t), [P, DG * P], U8) for t in range(4)] for g in range(G)]
+        uc = [kept("uc%d" % g, [P, 4, DG * P], U32) for g in range(G)]
+        us = [kept("us%d" % g, [P, 4, DG * P], U8) for g in range(G)]
         zc = [kept("zc%d" % g, [P, I, 4], BF16) for g in range(G)]
         rc = [kept("rc%d" % g, [P, I], U32) for g in range(G)]
         rs = [kept("rs%d" % g, [P, I], U8) for g in range(G)]
@@ -76,8 +75,8 @@ def tile_siglip_image_feature_gradient_k4_kernel(
                 out=z_raw[g][:], in_=Z[:, 512 * g : 512 * (g + 1)].rearrange("(r p) j -> p r j", p=P)
             )
 
-        def load_scales(plane, src):
-            for q in range(4):
+        def load_scales(plane, src, quadrants):
+            for q in quadrants:
                 nc.sync.dma_start(
                     out=plane[32 * q : 32 * q + 4, :, :].bitcast(I32),
                     in_=src[:, 4 * q : 4 * q + 4, :].rearrange("g r n -> r g n").bitcast(I32),
@@ -95,15 +94,25 @@ def tile_siglip_image_feature_gradient_k4_kernel(
             live["u_bank", g, t] = bk
 
         def u_copy(g, t):
-            ug = work.tile([P, 1024], BF16, name="ug", tag="ug", bufs=4, align_bytes=64)
+            if t == 0:
+                live["ug", g] = work.tile([P, 4, D], BF16, name="ug", tag="ug", align_bytes=64)
             nc.scalar.copy(
-                out=ug[:].bitcast(F32).rearrange("p (d m u) -> p d m u", d=DG, u=2),
+                out=live["ug", g][:, t, :].bitcast(F32).rearrange("p (d m u) -> p d m u", d=DG, u=2),
                 in_=live["u_bank", g, t][:].rearrange("p (d u m) -> p d m u", d=DG, u=2),
             )
-            live["ug", g, t] = ug
 
-        def u_quant(g, t):
-            nc.vector.quantize_mx(out=uc[g][t][:].bitcast(FP8X4), scales=us[g][t][:], in_=live["ug", g, t][:])
+        def u_quant(g, t0, t1):
+            nc.vector.quantize_mx(
+                out=uc[g][:, t0:t1, :].rearrange("p t m -> p (t m)").bitcast(FP8X4),
+                scales=us[g][:, t0:t1, :].rearrange("p t m -> p (t m)"),
+                in_=live["ug", g][:, t0:t1, :].rearrange("p t k -> p (t k)"),
+            )
+
+        def z_sort(g):
+            zs = work.tile([P, IT, 2, P], F32, name="zs", tag="zs", bufs=1, align_bytes=64)
+            words = z_raw[g][:].rearrange("q r j -> q (r j)").bitcast(F32)
+            nc.vector.tensor_copy(out=zs[:], in_=words.rearrange("q (r p u) -> q r u p", r=IT, u=2))
+            live["zs", g] = zs
 
         def z_turn(g, ih):
             bk = bank("bk_z")
@@ -111,7 +120,8 @@ def tile_siglip_image_feature_gradient_k4_kernel(
                 words = z_raw[g][:, 2 * ih + r, :].bitcast(F32)
                 for u in range(2):
                     col = 256 * u + P * r
-                    nc.tensor.transpose(bk[:, col : col + P], words[:, u:256:2], ident[:])
+                    src = words[:, u:256:2] if g == 0 else live["zs", g][:, 2 * ih + r, u, :]
+                    nc.tensor.transpose(bk[:, col : col + P], src, ident[:])
             live["z_bank", g, ih] = bk
 
         def z_scale(g, ih):
@@ -127,8 +137,8 @@ def tile_siglip_image_feature_gradient_k4_kernel(
             for d in range(DG):
                 nc.tensor.matmul_mx(
                     out=bk[:],
-                    lhsT=uc[g][t][:, P * d : P * (d + 1)].bitcast(FP8X4),
-                    lhsT_scale=us[g][t][:, P * d : P * (d + 1)],
+                    lhsT=uc[g][:, t, P * d : P * (d + 1)].bitcast(FP8X4),
+                    lhsT_scale=us[g][:, t, P * d : P * (d + 1)],
                     rhs=xw[:, d, :].bitcast(FP8X4),
                     rhs_scale=xs[:, d, :],
                     start=(d == 0),
@@ -153,10 +163,9 @@ def tile_siglip_image_feature_gradient_k4_kernel(
                 live["sg", g] = work.tile([P, 4, I], F32, name="sg", tag="sg", align_bytes=64)
             nc.scalar.activation(out=live["sg", g][:, t, :], in_=live["mg", g, t][:], func=ACT.Sigmoid)
 
-        def r_make(g, ih):
-            if ih == 0:
+        def r_make(g, cols):
+            if cols.start == 0:
                 live["rb", g] = work.tile([P, I, 4], BF16, name="rb", tag="rb", align_bytes=64)
-            cols = slice(256 * ih, 256 * (ih + 1))
             nc.vector.tensor_tensor(
                 out=live["rb", g][:, cols, :].rearrange("p (x i) t -> p x t i", i=4),
                 in0=live["sg", g][:, :, cols].rearrange("p t (x i) -> p x t i", i=4),
@@ -164,8 +173,7 @@ def tile_siglip_image_feature_gradient_k4_kernel(
                 op=ALU.mult,
             )
 
-        def r_quant(g, ih):
-            cols = slice(256 * ih, 256 * (ih + 1))
+        def r_quant(g, cols):
             nc.vector.quantize_mx(
                 out=rc[g][:, cols].bitcast(FP8X4),
                 scales=rs[g][:, cols],
@@ -178,8 +186,8 @@ def tile_siglip_image_feature_gradient_k4_kernel(
                 for d in range(DG):
                     nc.tensor.matmul_mx(
                         out=bk[:, P * t : P * (t + 1)],
-                        lhsT=uc[g][t][:, P * d : P * (d + 1)].bitcast(FP8X4),
-                        lhsT_scale=us[g][t][:, P * d : P * (d + 1)],
+                        lhsT=uc[g][:, t, P * d : P * (d + 1)].bitcast(FP8X4),
+                        lhsT_scale=us[g][:, t, P * d : P * (d + 1)],
                         rhs=ww[:, d, 1024 * h + 256 * s : 1024 * h + 256 * (s + 1)].bitcast(FP4X4),
                         rhs_scale=ws[:, d, 512 * h + P * s : 512 * h + P * (s + 1)],
                         start=(d == 0),
@@ -188,22 +196,21 @@ def tile_siglip_image_feature_gradient_k4_kernel(
             live["b_bank", g, h, s] = bk
 
         def b_copy(g, h, s):
-            if s % 2 == 0:
-                live["bb", g, h, s // 2] = work.tile([P, 256, 4], BF16, name="bb", tag="bb", bufs=4, align_bytes=64)
-            dst = live["bb", g, h, s // 2][:, P * (s % 2) : P * (s % 2 + 1), :]
+            if s == 0:
+                live["bb", g, h] = work.tile([P, 512, 4], BF16, name="bb", tag="bb", bufs=3, align_bytes=64)
+            dst = live["bb", g, h][:, P * s : P * (s + 1), :]
             nc.scalar.copy(out=dst, in_=live["b_bank", g, h, s][:].rearrange("p (t n) -> p n t", t=4))
 
-        def b_pair(g, h, sp):
-            for s in (2 * sp, 2 * sp + 1):
+        def b_half(g, h):
+            for s in range(4):
                 b_mul(g, h, s)
                 b_copy(g, h, s)
 
-        def b_quant(g, h, sp):
-            cols = slice(256 * sp, 256 * (sp + 1))
+        def b_quant(g, h):
             nc.vector.quantize_mx(
-                out=bc[g][h][:, cols].bitcast(FP8X4),
-                scales=bs[g][h][:, cols],
-                in_=live["bb", g, h, sp][:].rearrange("p n t -> p (n t)"),
+                out=bc[g][h][:].bitcast(FP8X4),
+                scales=bs[g][h][:],
+                in_=live["bb", g, h][:].rearrange("p n t -> p (n t)"),
             )
 
         def y_mul(h, r):
@@ -298,22 +305,21 @@ def tile_siglip_image_feature_gradient_k4_kernel(
 
         nc.vector.memset(xs[:].rearrange("p g n -> p (g n)").bitcast(I32), 0)
         nc.vector.memset(ws[:].rearrange("p g n -> p (g n)").bitcast(I32), 0)
-        nc.vector.memset(warm[:, 0:8], 0.0)
         make_identity(nc, ident[:])
-        nc.gpsimd.dma_start(out=c_sb[:], in_=c.rearrange("(g p t) -> p g t", g=G, t=4))
-        nc.gpsimd.dma_start(out=b_sb[:], in_=b.rearrange("(g p t) -> p g t", g=G, t=4))
-        nc.scalar.activation(out=warm[:, 8:16], in_=warm[:, 0:8], func=ACT.Sigmoid)
         load_u(0, 0, 1)
         load_u(0, 1, 2)
         load_u(0, 2, 4)
+        nc.scalar.dma_start(out=c_sb[:], in_=c.rearrange("(g p t) -> p g t", g=G, t=4))
+        nc.scalar.dma_start(out=b_sb[:], in_=b.rearrange("(g p t) -> p g t", g=G, t=4))
+        load_scales(xs, x_scales, range(0, 2))
         load_z(0)
-        load_scales(xs, x_scales)
         nc.sync.dma_start(
             out=xw[:].bitcast(I32), in_=x_words.rearrange("g p n t -> p g (n t)").bitcast(I32)
         )
-        load_z(1)
-        load_scales(ws, w_scales)
+        load_scales(xs, x_scales, range(2, 4))
+        load_scales(ws, w_scales, range(4))
         nc.sync.dma_start(out=ww[:].bitcast(I32), in_=w_words.rearrange("g p n -> p g n").bitcast(I32))
+        load_z(1)
         load_u(1, 0, 2)
         load_u(1, 2, 4)
         load_z(2)
@@ -323,10 +329,6 @@ def tile_siglip_image_feature_gradient_k4_kernel(
             nc.sync.dma_start(out=a_sb[:, :, 0], in_=a.rearrange("(r p) -> p r", p=P))
         nc.sync.dma_start(out=gain_sb[:], in_=gain.partition_broadcast(P))
 
-        for t in range(2):
-            u_turn(0, t)
-            u_copy(0, t)
-            u_quant(0, t)
         c_flat = c_sb[:].rearrange("p g t -> p (g t)")
         nc.vector.tensor_scalar(
             out=c_neg[:].rearrange("p g t -> p (g t)"), in0=c_flat, scalar1=-1.0, scalar2=None, op0=ALU.mult
@@ -339,46 +341,57 @@ def tile_siglip_image_feature_gradient_k4_kernel(
             out=b_over_c[:], in0=c_inv[:], in1=b_sb[:].rearrange("p g t -> p (g t)"), op=ALU.mult
         )
 
-        for t in range(2, 4):
+        for t in range(4):
             u_turn(0, t)
             u_copy(0, t)
-            u_quant(0, t)
+            u_quant(0, t, t + 1)
         for ih in range(2):
             z_turn(0, ih)
             z_scale(0, ih)
 
-        for g in range(G):
-            more = g + 1 < G
+        every = slice(0, I)
+        for g in range(G - 1):
             for t in range(4):
                 logits(g, t)
                 margin(g, t)
                 sigmoid(g, t)
                 if t == 0 and g > 0:
-                    b_quant(g - 1, 1, 1)
-            if more:
-                for ih in range(2):
-                    z_turn(g + 1, ih)
-                    z_scale(g + 1, ih)
-            b_pair(g, 0, 0)
-            r_make(g, 0)
-            b_pair(g, 0, 1)
-            b_quant(g, 0, 0)
-            r_quant(g, 0)
-            r_make(g, 1)
-            b_quant(g, 0, 1)
-            r_quant(g, 1)
-            if more:
-                for t in range(4):
-                    u_turn(g + 1, t)
-                    u_copy(g + 1, t)
-                    u_quant(g + 1, t)
-            b_pair(g, 1, 0)
-            b_pair(g, 1, 1)
-            b_quant(g, 1, 0)
+                    b_quant(g - 1, 1)
+            z_sort(g + 1)
+            b_half(g, 0)
+            r_make(g, every)
+            for t in range(2):
+                u_turn(g + 1, t)
+                u_copy(g + 1, t)
+            b_quant(g, 0)
+            for ih in range(2):
+                z_turn(g + 1, ih)
+                z_scale(g + 1, ih)
+            u_quant(g + 1, 0, 2)
+            r_quant(g, every)
+            for t in range(2, 4):
+                u_turn(g + 1, t)
+                u_copy(g + 1, t)
+            u_quant(g + 1, 2, 4)
+            b_half(g, 1)
+
+        last = G - 1
+        for t in range(4):
+            logits(last, t)
+            margin(last, t)
+            sigmoid(last, t)
+        b_quant(last - 1, 1)
+        b_half(last, 0)
+        r_make(last, slice(0, 256))
+        r_make(last, slice(256, I))
+        r_quant(last, slice(0, 256))
+        b_quant(last, 0)
+        b_half(last, 1)
+        r_quant(last, slice(256, I))
 
         y_mul(0, 0)
-        b_quant(G - 1, 1, 1)
         y_scale(0, 0)
+        b_quant(last, 1)
         y_round(0, 0, True)
         for r in range(1, IT):
             y_mul(0, r)

@@ -21,6 +21,7 @@ G = J // 512
 DG = D // 512
 NH = N // 512
 IT = I // P
+NSORT = 2
 
 
 def tile_siglip_image_feature_gradient_k4_kernel(
@@ -40,13 +41,12 @@ def tile_siglip_image_feature_gradient_k4_kernel(
             return psum.tile([P, 512], F32, name=name, tag="bank")
 
         ident = kept("ident", [P, P], F32)
-        c_sb = kept("c_sb", [P, G, 4], BF16)
-        b_sb = kept("b_sb", [P, G, 4], BF16)
+        cb_rows = kept("cb_rows", [P, 512], BF16)
         a_sb = kept("a_sb", [P, IT, 2], BF16)
         c_neg = kept("c_neg", [P, G, 4], BF16)
-        c_safe = kept("c_safe", [P, G * 4], F32)
-        c_inv = kept("c_inv", [P, G * 4], F32)
-        b_over_c = kept("b_over_c", [P, G * 4], F32)
+        c_safe = kept("c_safe", [P, G, 4], F32)
+        c_inv = kept("c_inv", [P, G, 4], F32)
+        b_over_c = kept("b_over_c", [P, G, 4], F32)
         gain_sb = kept("gain_sb", [P, N], BF16)
         xw = kept("xw", [P, DG, I], U32)
         xs = kept("xs", [P, DG, I], U8)
@@ -82,15 +82,23 @@ def tile_siglip_image_feature_gradient_k4_kernel(
                     in_=src[:, 4 * q : 4 * q + 4, :].rearrange("g r n -> r g n").bitcast(I32),
                 )
 
+        def u_sort(g):
+            srt = work.tile([P, NSORT * DG, 2, P], F32, name="srt", tag="srt", bufs=1, align_bytes=64)
+            words = u_raw[g][:, 0:NSORT, :].rearrange("q t k -> q (t k)").bitcast(F32)
+            nc.vector.tensor_copy(out=srt[:], in_=words.rearrange("q (s p u) -> q s u p", p=P, u=2))
+            live["srt", g] = srt
+
         def u_turn(g, t):
             bk = bank("bk_u")
             words = u_raw[g][:, t, :].bitcast(F32)
             for d in range(DG):
                 for u in range(2):
                     s = 2 * d + u
-                    nc.tensor.transpose(
-                        bk[:, P * s : P * (s + 1)], words[:, 256 * d + u : 256 * (d + 1) : 2], ident[:]
-                    )
+                    if g > 0 and t < NSORT:
+                        src = live["srt", g][:, DG * t + d, u, :]
+                    else:
+                        src = words[:, 256 * d + u : 256 * (d + 1) : 2]
+                    nc.tensor.transpose(bk[:, P * s : P * (s + 1)], src, ident[:])
             live["u_bank", g, t] = bk
 
         def u_copy(g, t):
@@ -151,9 +159,9 @@ def tile_siglip_image_feature_gradient_k4_kernel(
             nc.vector.scalar_tensor_tensor(
                 out=mg[:],
                 in0=live["l_bank", g, t][:],
-                scalar=b_over_c[:, 4 * g + t : 4 * g + t + 1],
+                scalar=b_over_c[:, g, t : t + 1],
                 in1=zc[g][:, :, t],
-                op0=ALU.add,
+                op0=ALU.subtract,
                 op1=ALU.mult,
             )
             live["mg", g, t] = mg
@@ -303,14 +311,14 @@ def tile_siglip_image_feature_gradient_k4_kernel(
                     out=out_2[:, 4 * q : 4 * q + 4, :].bitcast(I32), in_=ys[32 * q : 32 * q + 8, :].bitcast(I32)
                 )
 
+        nc.vector.memset(cb_rows[:].bitcast(I32), 0)
         nc.vector.memset(xs[:].rearrange("p g n -> p (g n)").bitcast(I32), 0)
         nc.vector.memset(ws[:].rearrange("p g n -> p (g n)").bitcast(I32), 0)
         make_identity(nc, ident[:])
-        load_u(0, 0, 1)
-        load_u(0, 1, 2)
-        load_u(0, 2, 4)
-        nc.scalar.dma_start(out=c_sb[:], in_=c.rearrange("(g p t) -> p g t", g=G, t=4))
-        nc.scalar.dma_start(out=b_sb[:], in_=b.rearrange("(g p t) -> p g t", g=G, t=4))
+        for t in range(4):
+            load_u(0, t, t + 1)
+        nc.scalar.dma_start(out=cb_rows[0:G, :], in_=c.rearrange("(g j) -> g j", g=G))
+        nc.scalar.dma_start(out=cb_rows[G : 2 * G, :], in_=b.rearrange("(g j) -> g j", g=G))
         load_scales(xs, x_scales, range(0, 2))
         load_z(0)
         nc.sync.dma_start(
@@ -319,32 +327,41 @@ def tile_siglip_image_feature_gradient_k4_kernel(
         load_scales(xs, x_scales, range(2, 4))
         load_scales(ws, w_scales, range(4))
         nc.sync.dma_start(out=ww[:].bitcast(I32), in_=w_words.rearrange("g p n -> p g n").bitcast(I32))
-        load_z(1)
-        load_u(1, 0, 2)
-        load_u(1, 2, 4)
-        load_z(2)
-        load_u(2, 0, 2)
-        load_u(2, 2, 4)
+        for g in range(1, G):
+            load_u(g, 0, 2)
+            load_z(g)
+            load_u(g, 2, 4)
         with nc.allow_non_contiguous_dma(reason="one value of a to each partition"):
             nc.sync.dma_start(out=a_sb[:, :, 0], in_=a.rearrange("(r p) -> p r", p=P))
         nc.sync.dma_start(out=gain_sb[:], in_=gain.partition_broadcast(P))
 
-        c_flat = c_sb[:].rearrange("p g t -> p (g t)")
-        nc.vector.tensor_scalar(
-            out=c_neg[:].rearrange("p g t -> p (g t)"), in0=c_flat, scalar1=-1.0, scalar2=None, op0=ALU.mult
-        )
-        nc.vector.scalar_tensor_tensor(
-            out=c_safe[:], in0=c_flat, scalar=0.0, in1=c_flat, op0=ALU.is_equal, op1=ALU.add
-        )
-        nc.vector.reciprocal(out=c_inv[:], in_=c_safe[:])
-        nc.vector.tensor_tensor(
-            out=b_over_c[:], in0=c_inv[:], in1=b_sb[:].rearrange("p g t -> p (g t)"), op=ALU.mult
-        )
+        def text_constants():
+            bk = bank("bk_c")
+            words = cb_rows[:].bitcast(F32)
+            for u in range(2):
+                nc.tensor.transpose(bk[:, P * u : P * (u + 1)], words[:, u:256:2], ident[:])
+            turned = bk[:, 0 : 2 * P].bitcast(BF16).rearrange("p (u r e) -> p r u e", u=2, e=2)
+            split = "p g (u e) -> p g u e"
+            nc.vector.tensor_scalar(
+                out=c_neg[:].rearrange(split, u=2), in0=turned[:, 0:G], scalar1=-1.0, scalar2=None, op0=ALU.mult
+            )
+            nc.vector.scalar_tensor_tensor(
+                out=c_safe[:], in0=c_neg[:], scalar=0.0, in1=c_neg[:], op0=ALU.is_equal, op1=ALU.add
+            )
+            nc.vector.reciprocal(out=c_inv[:], in_=c_safe[:])
+            nc.vector.tensor_tensor(
+                out=b_over_c[:].rearrange(split, u=2),
+                in0=turned[:, G : 2 * G],
+                in1=c_inv[:].rearrange(split, u=2),
+                op=ALU.mult,
+            )
 
         for t in range(4):
             u_turn(0, t)
             u_copy(0, t)
             u_quant(0, t, t + 1)
+            if t == 1:
+                text_constants()
         for ih in range(2):
             z_turn(0, ih)
             z_scale(0, ih)
@@ -357,6 +374,7 @@ def tile_siglip_image_feature_gradient_k4_kernel(
                 sigmoid(g, t)
                 if t == 0 and g > 0:
                     b_quant(g - 1, 1)
+            u_sort(g + 1)
             z_sort(g + 1)
             b_half(g, 0)
             r_make(g, every)

@@ -21,7 +21,6 @@ G = J // 512
 DG = D // 512
 NH = N // 512
 IT = I // P
-NSORT = 2
 
 
 def tile_siglip_image_feature_gradient_k4_kernel(
@@ -50,9 +49,9 @@ def tile_siglip_image_feature_gradient_k4_kernel(
         gain_sb = kept("gain_sb", [P, N], BF16)
         xw = kept("xw", [P, DG, I], U32)
         xs = kept("xs", [P, DG, I], U8)
-        ww = kept("ww", [P, DG, 2 * N], U8)
+        ww = [kept("ww%d" % h, [P, DG, N], U8) for h in range(NH)]
         ws = kept("ws", [P, DG, N], U8)
-        u_raw = [kept("u_raw%d" % g, [P, 4, D], BF16) for g in range(G)]
+        u_raw = [[kept("u_raw%d_%d" % (g, t), [P, D], BF16) for t in range(4)] for g in range(G)]
         z_raw = [kept("z_raw%d" % g, [P, IT, 512], BF16) for g in range(G)]
         uc = [kept("uc%d" % g, [P, 4, DG * P], U32) for g in range(G)]
         us = [kept("us%d" % g, [P, 4, DG * P], U8) for g in range(G)]
@@ -66,9 +65,13 @@ def tile_siglip_image_feature_gradient_k4_kernel(
         ys = kept("ys", [P, I], U8)
         live = {}
 
-        def load_u(g, t0, t1):
+        def load_u(g, t):
             rows = U[512 * g : 512 * (g + 1), :].rearrange("(m t) k -> m t k", t=4)
-            nc.sync.dma_start(out=u_raw[g][:, t0:t1, :], in_=rows[:, t0:t1, :])
+            nc.sync.dma_start(out=u_raw[g][t][:], in_=rows[:, t, :])
+
+        def load_w(h):
+            src = w_words[:, :, N * h : N * (h + 1)].rearrange("g p n -> p g n")
+            nc.sync.dma_start(out=ww[h][:].bitcast(I32), in_=src.bitcast(I32))
 
         def load_z(g):
             nc.sync.dma_start(
@@ -82,20 +85,20 @@ def tile_siglip_image_feature_gradient_k4_kernel(
                     in_=src[:, 4 * q : 4 * q + 4, :].rearrange("g r n -> r g n").bitcast(I32),
                 )
 
-        def u_sort(g):
-            srt = work.tile([P, NSORT * DG, 2, P], F32, name="srt", tag="srt", bufs=1, align_bytes=64)
-            words = u_raw[g][:, 0:NSORT, :].rearrange("q t k -> q (t k)").bitcast(F32)
-            nc.vector.tensor_copy(out=srt[:], in_=words.rearrange("q (s p u) -> q s u p", p=P, u=2))
-            live["srt", g] = srt
+        def u_sort(g, t):
+            srt = work.tile([P, DG, 2, P], F32, name="srt", tag="srt", bufs=4, align_bytes=64)
+            words = u_raw[g][t][:].bitcast(F32)
+            nc.vector.tensor_copy(out=srt[:], in_=words.rearrange("q (d p u) -> q d u p", p=P, u=2))
+            live["srt", g, t] = srt
 
         def u_turn(g, t):
             bk = bank("bk_u")
-            words = u_raw[g][:, t, :].bitcast(F32)
+            words = u_raw[g][t][:].bitcast(F32)
             for d in range(DG):
                 for u in range(2):
                     s = 2 * d + u
-                    if g > 0 and t < NSORT:
-                        src = live["srt", g][:, DG * t + d, u, :]
+                    if ("srt", g, t) in live:
+                        src = live["srt", g, t][:, d, u, :]
                     else:
                         src = words[:, 256 * d + u : 256 * (d + 1) : 2]
                     nc.tensor.transpose(bk[:, P * s : P * (s + 1)], src, ident[:])
@@ -116,19 +119,22 @@ def tile_siglip_image_feature_gradient_k4_kernel(
                 in_=live["ug", g][:, t0:t1, :].rearrange("p t k -> p (t k)"),
             )
 
-        def z_sort(g):
+        def z_sort(g, on_scalar):
             zs = work.tile([P, IT, 2, P], F32, name="zs", tag="zs", bufs=1, align_bytes=64)
             words = z_raw[g][:].rearrange("q r j -> q (r j)").bitcast(F32)
-            nc.vector.tensor_copy(out=zs[:], in_=words.rearrange("q (r p u) -> q r u p", r=IT, u=2))
+            copy = nc.scalar.copy if on_scalar else nc.vector.tensor_copy
+            copy(out=zs[:], in_=words.rearrange("q (r p u) -> q r u p", r=IT, u=2))
             live["zs", g] = zs
 
         def z_turn(g, ih):
             bk = bank("bk_z")
             for r in range(2):
-                words = z_raw[g][:, 2 * ih + r, :].bitcast(F32)
                 for u in range(2):
                     col = 256 * u + P * r
-                    src = words[:, u:256:2] if g == 0 else live["zs", g][:, 2 * ih + r, u, :]
+                    if ("zs", g) in live:
+                        src = live["zs", g][:, 2 * ih + r, u, :]
+                    else:
+                        src = z_raw[g][:, 2 * ih + r, :].bitcast(F32)[:, u:256:2]
                     nc.tensor.transpose(bk[:, col : col + P], src, ident[:])
             live["z_bank", g, ih] = bk
 
@@ -168,7 +174,7 @@ def tile_siglip_image_feature_gradient_k4_kernel(
 
         def sigmoid(g, t):
             if t == 0:
-                live["sg", g] = work.tile([P, 4, I], F32, name="sg", tag="sg", align_bytes=64)
+                live["sg", g] = work.tile([P, 4, I], F32, name="sg", tag="sg", bufs=2, align_bytes=64)
             nc.scalar.activation(out=live["sg", g][:, t, :], in_=live["mg", g, t][:], func=ACT.Sigmoid)
 
         def r_make(g, cols):
@@ -188,31 +194,40 @@ def tile_siglip_image_feature_gradient_k4_kernel(
                 in_=live["rb", g][:, cols, :].rearrange("p i t -> p (i t)"),
             )
 
+        def b_pass(bk, g, h, s, t, d):
+            nc.tensor.matmul_mx(
+                out=bk[:, P * t : P * (t + 1)],
+                lhsT=uc[g][:, t, P * d : P * (d + 1)].bitcast(FP8X4),
+                lhsT_scale=us[g][:, t, P * d : P * (d + 1)],
+                rhs=ww[h][:, d, 256 * s : 256 * (s + 1)].bitcast(FP4X4),
+                rhs_scale=ws[:, d, 512 * h + P * s : 512 * h + P * (s + 1)],
+                start=(d == 0),
+                stop=(d == DG - 1),
+            )
+
         def b_mul(g, h, s):
             bk = bank("bk_b")
             for t in range(4):
                 for d in range(DG):
-                    nc.tensor.matmul_mx(
-                        out=bk[:, P * t : P * (t + 1)],
-                        lhsT=uc[g][:, t, P * d : P * (d + 1)].bitcast(FP8X4),
-                        lhsT_scale=us[g][:, t, P * d : P * (d + 1)],
-                        rhs=ww[:, d, 1024 * h + 256 * s : 1024 * h + 256 * (s + 1)].bitcast(FP4X4),
-                        rhs_scale=ws[:, d, 512 * h + P * s : 512 * h + P * (s + 1)],
-                        start=(d == 0),
-                        stop=(d == DG - 1),
-                    )
+                    b_pass(bk, g, h, s, t, d)
             live["b_bank", g, h, s] = bk
+
+        def b_slot(g, h, t):
+            for d in range(DG):
+                for s in range(4):
+                    if t == 0 and d == 0:
+                        live["b_bank", g, h, s] = bank("bk_b")
+                    b_pass(live["b_bank", g, h, s], g, h, s, t, d)
 
         def b_copy(g, h, s):
             if s == 0:
-                live["bb", g, h] = work.tile([P, 512, 4], BF16, name="bb", tag="bb", bufs=3, align_bytes=64)
+                live["bb", g, h] = work.tile([P, 512, 4], BF16, name="bb", tag="bb", bufs=5, align_bytes=64)
             dst = live["bb", g, h][:, P * s : P * (s + 1), :]
             nc.scalar.copy(out=dst, in_=live["b_bank", g, h, s][:].rearrange("p (t n) -> p n t", t=4))
 
-        def b_half(g, h):
-            for s in range(4):
-                b_mul(g, h, s)
-                b_copy(g, h, s)
+        def b_bank(g, h, s):
+            b_mul(g, h, s)
+            b_copy(g, h, s)
 
         def b_quant(g, h):
             nc.vector.quantize_mx(
@@ -249,7 +264,7 @@ def tile_siglip_image_feature_gradient_k4_kernel(
             live["yf", h, r] = yf
 
         def y_round(h, r, on_scalar):
-            yb = work.tile([P, 512], BF16, name="yb", tag="yb", bufs=4, align_bytes=64)
+            yb = work.tile([P, 512], BF16, name="yb", tag="yb", bufs=8, align_bytes=64)
             dst = yb[:].rearrange("q (u p e) -> q u p e", u=2, e=2)
             src = live["yf", h, r][:].rearrange("q (p u e) -> q u p e", u=2, e=2)
             if on_scalar:
@@ -259,7 +274,7 @@ def tile_siglip_image_feature_gradient_k4_kernel(
             live["yb", h, r] = yb
 
         def y_round_from_bank(h, r):
-            yb = work.tile([P, 512], BF16, name="yb", tag="yb", bufs=4, align_bytes=64)
+            yb = work.tile([P, 512], BF16, name="yb", tag="yb", bufs=8, align_bytes=64)
             src = live["y_bank", h, r][:].rearrange("q (p u e) -> q u p e", u=2, e=2)
             gn = gain_sb[:, 512 * h : 512 * (h + 1)].rearrange("q (p u e) -> q u p e", u=2, e=2)
             for u in range(2):
@@ -311,72 +326,99 @@ def tile_siglip_image_feature_gradient_k4_kernel(
                     out=out_2[:, 4 * q : 4 * q + 4, :].bitcast(I32), in_=ys[32 * q : 32 * q + 8, :].bitcast(I32)
                 )
 
+        split = "p g (u e) -> p g u e"
+
+        def c_turn():
+            bk = bank("bk_c")
+            words = cb_rows[:].bitcast(F32)
+            for u in range(2):
+                nc.tensor.transpose(bk[:, P * u : P * (u + 1)], words[:, u:256:2], ident[:])
+            live["cb"] = bk[:, 0 : 2 * P].bitcast(BF16).rearrange("p (u r e) -> p r u e", u=2, e=2)
+
+        def c_negate():
+            nc.vector.tensor_scalar(
+                out=c_neg[:].rearrange(split, u=2), in0=live["cb"][:, 0:G], scalar1=-1.0, scalar2=None, op0=ALU.mult
+            )
+
+        def c_guard():
+            nc.vector.scalar_tensor_tensor(
+                out=c_safe[:], in0=c_neg[:], scalar=0.0, in1=c_neg[:], op0=ALU.is_equal, op1=ALU.add
+            )
+
+        def c_invert():
+            nc.vector.reciprocal(out=c_inv[:], in_=c_safe[:])
+
+        def b_divide():
+            nc.vector.tensor_tensor(
+                out=b_over_c[:].rearrange(split, u=2),
+                in0=live["cb"][:, G : 2 * G],
+                in1=c_inv[:].rearrange(split, u=2),
+                op=ALU.mult,
+            )
+
         nc.vector.memset(cb_rows[:].bitcast(I32), 0)
         nc.vector.memset(xs[:].rearrange("p g n -> p (g n)").bitcast(I32), 0)
         nc.vector.memset(ws[:].rearrange("p g n -> p (g n)").bitcast(I32), 0)
         make_identity(nc, ident[:])
         for t in range(4):
-            load_u(0, t, t + 1)
+            load_u(0, t)
+        load_z(0)
         nc.scalar.dma_start(out=cb_rows[0:G, :], in_=c.rearrange("(g j) -> g j", g=G))
         nc.scalar.dma_start(out=cb_rows[G : 2 * G, :], in_=b.rearrange("(g j) -> g j", g=G))
-        load_scales(xs, x_scales, range(0, 2))
-        load_z(0)
+        load_scales(xs, x_scales, range(4))
         nc.sync.dma_start(
             out=xw[:].bitcast(I32), in_=x_words.rearrange("g p n t -> p g (n t)").bitcast(I32)
         )
-        load_scales(xs, x_scales, range(2, 4))
         load_scales(ws, w_scales, range(4))
-        nc.sync.dma_start(out=ww[:].bitcast(I32), in_=w_words.rearrange("g p n -> p g n").bitcast(I32))
+        load_w(0)
+        load_w(1)
         for g in range(1, G):
-            load_u(g, 0, 2)
+            load_u(g, 0)
+            load_u(g, 1)
             load_z(g)
-            load_u(g, 2, 4)
+            load_u(g, 2)
+            load_u(g, 3)
         with nc.allow_non_contiguous_dma(reason="one value of a to each partition"):
             nc.sync.dma_start(out=a_sb[:, :, 0], in_=a.rearrange("(r p) -> p r", p=P))
         nc.sync.dma_start(out=gain_sb[:], in_=gain.partition_broadcast(P))
 
-        def text_constants():
-            bk = bank("bk_c")
-            words = cb_rows[:].bitcast(F32)
-            for u in range(2):
-                nc.tensor.transpose(bk[:, P * u : P * (u + 1)], words[:, u:256:2], ident[:])
-            turned = bk[:, 0 : 2 * P].bitcast(BF16).rearrange("p (u r e) -> p r u e", u=2, e=2)
-            split = "p g (u e) -> p g u e"
-            nc.vector.tensor_scalar(
-                out=c_neg[:].rearrange(split, u=2), in0=turned[:, 0:G], scalar1=-1.0, scalar2=None, op0=ALU.mult
-            )
-            nc.vector.scalar_tensor_tensor(
-                out=c_safe[:], in0=c_neg[:], scalar=0.0, in1=c_neg[:], op0=ALU.is_equal, op1=ALU.add
-            )
-            nc.vector.reciprocal(out=c_inv[:], in_=c_safe[:])
-            nc.vector.tensor_tensor(
-                out=b_over_c[:].rearrange(split, u=2),
-                in0=turned[:, G : 2 * G],
-                in1=c_inv[:].rearrange(split, u=2),
-                op=ALU.mult,
-            )
-
-        for t in range(4):
+        u_turn(0, 0)
+        u_copy(0, 0)
+        for t in range(1, 4):
+            u_sort(0, t)
             u_turn(0, t)
             u_copy(0, t)
-            u_quant(0, t, t + 1)
-            if t == 1:
-                text_constants()
+        c_turn()
+        u_quant(0, 0, 1)
+        z_sort(0, False)
+        c_negate()
+        u_quant(0, 1, 2)
+        c_guard()
+        u_quant(0, 2, 3)
+        c_invert()
         for ih in range(2):
             z_turn(0, ih)
-            z_scale(0, ih)
+        z_scale(0, 0)
+        b_divide()
+        z_scale(0, 1)
+        u_quant(0, 3, 4)
 
         every = slice(0, I)
-        for g in range(G - 1):
+        lo, hi = slice(0, 256), slice(256, I)
+
+        def r_front(g):
             for t in range(4):
                 logits(g, t)
                 margin(g, t)
                 sigmoid(g, t)
-                if t == 0 and g > 0:
-                    b_quant(g - 1, 1)
-            u_sort(g + 1)
-            z_sort(g + 1)
-            b_half(g, 0)
+
+        for g in range(G - 1):
+            r_front(g)
+            u_sort(g + 1, 0)
+            u_sort(g + 1, 1)
+            z_sort(g + 1, False)
+            for s in range(4):
+                b_bank(g, 0, s)
             r_make(g, every)
             for t in range(2):
                 u_turn(g + 1, t)
@@ -391,21 +433,21 @@ def tile_siglip_image_feature_gradient_k4_kernel(
                 u_turn(g + 1, t)
                 u_copy(g + 1, t)
             u_quant(g + 1, 2, 4)
-            b_half(g, 1)
-
+            for s in range(4):
+                b_bank(g, 1, s)
         last = G - 1
-        for t in range(4):
-            logits(last, t)
-            margin(last, t)
-            sigmoid(last, t)
-        b_quant(last - 1, 1)
-        b_half(last, 0)
-        r_make(last, slice(0, 256))
-        r_make(last, slice(256, I))
-        r_quant(last, slice(0, 256))
+        r_front(last)
+        for s in range(4):
+            b_bank(last, 0, s)
+        b_quant(0, 1)
+        r_make(last, lo)
+        r_make(last, hi)
+        r_quant(last, lo)
         b_quant(last, 0)
-        b_half(last, 1)
-        r_quant(last, slice(256, I))
+        for s in range(4):
+            b_bank(last, 1, s)
+        r_quant(last, hi)
+        b_quant(1, 1)
 
         y_mul(0, 0)
         y_scale(0, 0)
@@ -421,27 +463,25 @@ def tile_siglip_image_feature_gradient_k4_kernel(
         y_round(1, 0, False)
         y_turn(0, [0, 1])
         y_turn(0, [2, 3])
-        y_turn(1, [0])
         y_scale(1, 1)
         y_copy(0, [0, 1])
         y_copy(0, [2, 3])
         y_mul(1, 2)
+        y_round(1, 1, False)
         y_quant(0, [0, 1])
-        y_round(1, 1, True)
         y_scale(1, 2)
-        y_copy(1, [0])
+        y_mul(1, 3)
+        y_turn(1, [0, 1])
+        y_round(1, 2, True)
+        y_copy(1, [0, 1])
         y_quant(0, [2, 3])
         store_words(0, [0, 1, 2, 3])
-        y_mul(1, 3)
-        y_round(1, 2, True)
         y_round_from_bank(1, 3)
-        y_turn(1, [1])
         y_turn(1, [2])
         y_turn(1, [3])
         y_scale(1, 3)
-        y_copy(1, [1])
         y_copy(1, [2])
-        y_copy(1, [3], False)
+        y_copy(1, [3])
         y_quant(1, [0, 1])
         store_words(1, [0, 1])
         y_quant(1, [2, 3])

@@ -49,9 +49,9 @@ def tile_siglip_image_feature_gradient_k4_kernel(
         gain_sb = kept("gain_sb", [P, N], BF16)
         xw = kept("xw", [P, DG, I], U32)
         xs = kept("xs", [P, DG, I], U8)
-        ww = [kept("ww%d" % h, [P, DG, N], U8) for h in range(NH)]
+        ww = {}
         ws = kept("ws", [P, DG, N], U8)
-        u_raw = [[kept("u_raw%d_%d" % (g, t), [P, D], BF16) for t in range(4)] for g in range(G)]
+        u_raw = {}
         z_raw = [kept("z_raw%d" % g, [P, IT, 512], BF16) for g in range(G)]
         uc = [kept("uc%d" % g, [P, 4, DG * P], U32) for g in range(G)]
         us = [kept("us%d" % g, [P, 4, DG * P], U8) for g in range(G)]
@@ -65,35 +65,51 @@ def tile_siglip_image_feature_gradient_k4_kernel(
         ys = kept("ys", [P, I], U8)
         live = {}
 
-        def load_u(g, t):
+        def load_u(g, t0, t1):
             rows = U[512 * g : 512 * (g + 1), :].rearrange("(m t) k -> m t k", t=4)
-            nc.sync.dma_start(out=u_raw[g][t][:], in_=rows[:, t, :])
+            raw = kept("u_raw%d_%d" % (g, t0), [P, t1 - t0, D], BF16)
+            nc.sync.dma_start(out=raw[:], in_=rows[:, t0:t1, :])
+            for t in range(t0, t1):
+                u_raw[g, t] = raw[:, t - t0, :]
 
-        def load_w(h):
-            src = w_words[:, :, N * h : N * (h + 1)].rearrange("g p n -> p g n")
-            nc.sync.dma_start(out=ww[h][:].bitcast(I32), in_=src.bitcast(I32))
+        def load_w(h0, h1):
+            src = w_words[:, :, N * h0 : N * h1].rearrange("g p n -> p g n")
+            raw = kept("ww%d" % h0, [P, DG, N * (h1 - h0)], U8)
+            nc.sync.dma_start(out=raw[:].bitcast(I32), in_=src.bitcast(I32))
+            for h in range(h0, h1):
+                ww[h] = raw[:, :, N * (h - h0) : N * (h - h0 + 1)]
 
         def load_z(g):
             nc.sync.dma_start(
                 out=z_raw[g][:], in_=Z[:, 512 * g : 512 * (g + 1)].rearrange("(r p) j -> p r j", p=P)
             )
 
-        def load_scales(plane, src, quadrants):
-            for q in quadrants:
+        def load_scales(plane, src):
+            for r in range(4):
                 nc.sync.dma_start(
-                    out=plane[32 * q : 32 * q + 4, :, :].bitcast(I32),
-                    in_=src[:, 4 * q : 4 * q + 4, :].rearrange("g r n -> r g n").bitcast(I32),
+                    out=plane[r:P:32, :, :].bitcast(I32),
+                    in_=src[:, r:16:4, :].rearrange("g q n -> q g n").bitcast(I32),
                 )
+
+        def load_x():
+            load_scales(xs, x_scales)
+            nc.sync.dma_start(
+                out=xw[:].bitcast(I32), in_=x_words.rearrange("g p n t -> p g (n t)").bitcast(I32)
+            )
+
+        def load_cb():
+            nc.scalar.dma_start(out=cb_rows[0:G, :], in_=c.rearrange("(g j) -> g j", g=G))
+            nc.scalar.dma_start(out=cb_rows[G : 2 * G, :], in_=b.rearrange("(g j) -> g j", g=G))
 
         def u_sort(g, t):
             srt = work.tile([P, DG, 2, P], F32, name="srt", tag="srt", bufs=4, align_bytes=64)
-            words = u_raw[g][t][:].bitcast(F32)
+            words = u_raw[g, t].bitcast(F32)
             nc.vector.tensor_copy(out=srt[:], in_=words.rearrange("q (d p u) -> q d u p", p=P, u=2))
             live["srt", g, t] = srt
 
         def u_turn(g, t):
             bk = bank("bk_u")
-            words = u_raw[g][t][:].bitcast(F32)
+            words = u_raw[g, t].bitcast(F32)
             for d in range(DG):
                 for u in range(2):
                     s = 2 * d + u
@@ -360,27 +376,33 @@ def tile_siglip_image_feature_gradient_k4_kernel(
         nc.vector.memset(xs[:].rearrange("p g n -> p (g n)").bitcast(I32), 0)
         nc.vector.memset(ws[:].rearrange("p g n -> p (g n)").bitcast(I32), 0)
         make_identity(nc, ident[:])
-        for t in range(4):
-            load_u(0, t)
+        load_u(0, 0, 1)
+        load_u(0, 1, 2)
+        load_u(0, 2, 3)
+        load_u(0, 3, 4)
         load_z(0)
-        nc.scalar.dma_start(out=cb_rows[0:G, :], in_=c.rearrange("(g j) -> g j", g=G))
-        nc.scalar.dma_start(out=cb_rows[G : 2 * G, :], in_=b.rearrange("(g j) -> g j", g=G))
-        load_scales(xs, x_scales, range(4))
-        nc.sync.dma_start(
-            out=xw[:].bitcast(I32), in_=x_words.rearrange("g p n t -> p g (n t)").bitcast(I32)
-        )
-        load_scales(ws, w_scales, range(4))
-        load_w(0)
-        load_w(1)
-        for g in range(1, G):
-            load_u(g, 0)
-            load_u(g, 1)
-            load_z(g)
-            load_u(g, 2)
-            load_u(g, 3)
+        load_cb()
+        load_x()
+        load_scales(ws, w_scales)
+        load_w(0, 2)
+        load_u(1, 0, 2)
+        load_z(1)
+        load_u(1, 2, 4)
+        load_u(2, 0, 2)
+        load_z(2)
+        load_u(2, 2, 4)
         with nc.allow_non_contiguous_dma(reason="one value of a to each partition"):
             nc.sync.dma_start(out=a_sb[:, :, 0], in_=a.rearrange("(r p) -> p r", p=P))
         nc.sync.dma_start(out=gain_sb[:], in_=gain.partition_broadcast(P))
+
+        every = slice(0, I)
+        lo, hi = slice(0, 256), slice(256, I)
+
+        def r_front(g):
+            for t in range(4):
+                logits(g, t)
+                margin(g, t)
+                sigmoid(g, t)
 
         u_turn(0, 0)
         u_copy(0, 0)
@@ -402,16 +424,6 @@ def tile_siglip_image_feature_gradient_k4_kernel(
         b_divide()
         z_scale(0, 1)
         u_quant(0, 3, 4)
-
-        every = slice(0, I)
-        lo, hi = slice(0, 256), slice(256, I)
-
-        def r_front(g):
-            for t in range(4):
-                logits(g, t)
-                margin(g, t)
-                sigmoid(g, t)
-
         for g in range(G - 1):
             r_front(g)
             u_sort(g + 1, 0)

@@ -52,6 +52,7 @@ def tile_siglip_image_feature_gradient_k4_kernel(
         ww = {}
         ws = kept("ws", [P, DG, N], U8)
         u_raw = {}
+        u_pack = {}
         z_raw = [kept("z_raw%d" % g, [P, IT, 512], BF16) for g in range(G)]
         uc = [kept("uc%d" % g, [P, 4, DG * P], U32) for g in range(G)]
         us = [kept("us%d" % g, [P, 4, DG * P], U8) for g in range(G)]
@@ -69,6 +70,7 @@ def tile_siglip_image_feature_gradient_k4_kernel(
             rows = U[512 * g : 512 * (g + 1), :].rearrange("(m t) k -> m t k", t=4)
             raw = kept("u_raw%d_%d" % (g, t0), [P, t1 - t0, D], BF16)
             nc.sync.dma_start(out=raw[:], in_=rows[:, t0:t1, :])
+            u_pack[g, t0] = raw
             for t in range(t0, t1):
                 u_raw[g, t] = raw[:, t - t0, :]
 
@@ -101,11 +103,13 @@ def tile_siglip_image_feature_gradient_k4_kernel(
             nc.scalar.dma_start(out=cb_rows[0:G, :], in_=c.rearrange("(g j) -> g j", g=G))
             nc.scalar.dma_start(out=cb_rows[G : 2 * G, :], in_=b.rearrange("(g j) -> g j", g=G))
 
-        def u_sort(g, t):
-            srt = work.tile([P, DG, 2, P], F32, name="srt", tag="srt", bufs=4, align_bytes=64)
-            words = u_raw[g, t].bitcast(F32)
-            nc.vector.tensor_copy(out=srt[:], in_=words.rearrange("q (d p u) -> q d u p", p=P, u=2))
-            live["srt", g, t] = srt
+        def u_sort(g, t0, t1):
+            n = t1 - t0
+            srt = work.tile([P, n * DG, 2, P], F32, name="srt", tag="srt", bufs=3, align_bytes=64)
+            words = u_pack[g, t0][:, 0:n, :].rearrange("q t k -> q (t k)").bitcast(F32)
+            nc.vector.tensor_copy(out=srt[:], in_=words.rearrange("q (s p u) -> q s u p", p=P, u=2))
+            for t in range(t0, t1):
+                live["srt", g, t] = srt[:, DG * (t - t0) : DG * (t - t0 + 1)]
 
         def u_turn(g, t):
             bk = bank("bk_u")
@@ -121,10 +125,10 @@ def tile_siglip_image_feature_gradient_k4_kernel(
             live["u_bank", g, t] = bk
 
         def u_copy(g, t):
-            if t == 0:
-                live["ug", g] = work.tile([P, 4, D], BF16, name="ug", tag="ug", align_bytes=64)
+            if t % 2 == 0:
+                live["ug", g, t // 2] = work.tile([P, 2, D], BF16, name="ug", tag="ug", bufs=2, align_bytes=64)
             nc.scalar.copy(
-                out=live["ug", g][:, t, :].bitcast(F32).rearrange("p (d m u) -> p d m u", d=DG, u=2),
+                out=live["ug", g, t // 2][:, t % 2, :].bitcast(F32).rearrange("p (d m u) -> p d m u", d=DG, u=2),
                 in_=live["u_bank", g, t][:].rearrange("p (d u m) -> p d m u", d=DG, u=2),
             )
 
@@ -132,7 +136,7 @@ def tile_siglip_image_feature_gradient_k4_kernel(
             nc.vector.quantize_mx(
                 out=uc[g][:, t0:t1, :].rearrange("p t m -> p (t m)").bitcast(FP8X4),
                 scales=us[g][:, t0:t1, :].rearrange("p t m -> p (t m)"),
-                in_=live["ug", g][:, t0:t1, :].rearrange("p t k -> p (t k)"),
+                in_=live["ug", g, t0 // 2][:, t0 % 2 : t0 % 2 + t1 - t0, :].rearrange("p t k -> p (t k)"),
             )
 
         def z_sort(g, on_scalar):
@@ -177,7 +181,7 @@ def tile_siglip_image_feature_gradient_k4_kernel(
             live["l_bank", g, t] = bk
 
         def margin(g, t):
-            mg = work.tile([P, I], F32, name="mg", tag="mg", bufs=3, align_bytes=64)
+            mg = work.tile([P, I], F32, name="mg", tag="mg", bufs=4, align_bytes=64)
             nc.vector.scalar_tensor_tensor(
                 out=mg[:],
                 in0=live["l_bank", g, t][:],
@@ -193,21 +197,24 @@ def tile_siglip_image_feature_gradient_k4_kernel(
                 live["sg", g] = work.tile([P, 4, I], F32, name="sg", tag="sg", bufs=2, align_bytes=64)
             nc.scalar.activation(out=live["sg", g][:, t, :], in_=live["mg", g, t][:], func=ACT.Sigmoid)
 
-        def r_make(g, cols):
-            if cols.start == 0:
-                live["rb", g] = work.tile([P, I, 4], BF16, name="rb", tag="rb", align_bytes=64)
-            nc.vector.tensor_tensor(
-                out=live["rb", g][:, cols, :].rearrange("p (x i) t -> p x t i", i=4),
+        def r_make(g, half, engine=nc.vector, tag="rb", part=slice(0, 256)):
+            cols = slice(256 * half + part.start, 256 * half + part.stop)
+            if part.start == 0:
+                bufs = 1 if tag == "bb_first" else 2
+                live["rb", g, half] = work.tile([P, 256, 4], BF16, name="rb", tag=tag, bufs=bufs, align_bytes=64)
+            engine.tensor_tensor(
+                out=live["rb", g, half][:, part, :].rearrange("p (x i) t -> p x t i", i=4),
                 in0=live["sg", g][:, :, cols].rearrange("p t (x i) -> p x t i", i=4),
                 in1=zc[g][:, cols, :].rearrange("p (x i) t -> p x t i", i=4),
                 op=ALU.mult,
             )
 
-        def r_quant(g, cols):
+        def r_quant(g, half):
+            cols = slice(256 * half, 256 * (half + 1))
             nc.vector.quantize_mx(
                 out=rc[g][:, cols].bitcast(FP8X4),
                 scales=rs[g][:, cols],
-                in_=live["rb", g][:, cols, :].rearrange("p i t -> p (i t)"),
+                in_=live["rb", g, half][:].rearrange("p i t -> p (i t)"),
             )
 
         def b_pass(bk, g, h, s, t, d):
@@ -228,16 +235,20 @@ def tile_siglip_image_feature_gradient_k4_kernel(
                     b_pass(bk, g, h, s, t, d)
             live["b_bank", g, h, s] = bk
 
-        def b_slot(g, h, t):
-            for d in range(DG):
-                for s in range(4):
-                    if t == 0 and d == 0:
-                        live["b_bank", g, h, s] = bank("bk_b")
-                    b_pass(live["b_bank", g, h, s], g, h, s, t, d)
+        def b_group(g, h, banks):
+            for s in banks:
+                live["b_bank", g, h, s] = bank("bk_b")
+            for t in range(4):
+                for d in range(DG):
+                    for s in banks:
+                        b_pass(live["b_bank", g, h, s], g, h, s, t, d)
+            for s in banks:
+                b_copy(g, h, s)
 
         def b_copy(g, h, s):
             if s == 0:
-                live["bb", g, h] = work.tile([P, 512, 4], BF16, name="bb", tag="bb", bufs=5, align_bytes=64)
+                tag, bufs = ("bb_first", 1) if h == 0 else ("bb_second", 3)
+                live["bb", g, h] = work.tile([P, 512, 4], BF16, name="bb", tag=tag, bufs=bufs, align_bytes=64)
             dst = live["bb", g, h][:, P * s : P * (s + 1), :]
             nc.scalar.copy(out=dst, in_=live["b_bank", g, h, s][:].rearrange("p (t n) -> p n t", t=4))
 
@@ -386,8 +397,8 @@ def tile_siglip_image_feature_gradient_k4_kernel(
         load_scales(ws, w_scales)
         load_w(0, 2)
         load_u(1, 0, 2)
-        load_z(1)
         load_u(1, 2, 4)
+        load_z(1)
         load_u(2, 0, 2)
         load_z(2)
         load_u(2, 2, 4)
@@ -406,13 +417,16 @@ def tile_siglip_image_feature_gradient_k4_kernel(
 
         u_turn(0, 0)
         u_copy(0, 0)
-        for t in range(1, 4):
-            u_sort(0, t)
-            u_turn(0, t)
-            u_copy(0, t)
+        u_sort(0, 1, 2)
+        u_turn(0, 1)
+        u_copy(0, 1)
+        u_sort(0, 2, 3)
         c_turn()
         u_quant(0, 0, 1)
-        z_sort(0, False)
+        u_sort(0, 3, 4)
+        for t in range(2, 4):
+            u_turn(0, t)
+            u_copy(0, t)
         c_negate()
         u_quant(0, 1, 2)
         c_guard()
@@ -420,46 +434,64 @@ def tile_siglip_image_feature_gradient_k4_kernel(
         c_invert()
         for ih in range(2):
             z_turn(0, ih)
-        z_scale(0, 0)
-        b_divide()
-        z_scale(0, 1)
         u_quant(0, 3, 4)
-        for g in range(G - 1):
-            r_front(g)
-            u_sort(g + 1, 0)
-            u_sort(g + 1, 1)
-            z_sort(g + 1, False)
-            for s in range(4):
-                b_bank(g, 0, s)
-            r_make(g, every)
-            for t in range(2):
-                u_turn(g + 1, t)
-                u_copy(g + 1, t)
-            b_quant(g, 0)
-            for ih in range(2):
-                z_turn(g + 1, ih)
-                z_scale(g + 1, ih)
-            u_quant(g + 1, 0, 2)
-            r_quant(g, every)
-            for t in range(2, 4):
-                u_turn(g + 1, t)
-                u_copy(g + 1, t)
-            u_quant(g + 1, 2, 4)
-            for s in range(4):
-                b_bank(g, 1, s)
+        b_divide()
+        for ih in range(2):
+            z_scale(0, ih)
+        r_front(0)
+        u_sort(1, 0, 2)
+        u_sort(1, 2, 4)
+        for s in range(4):
+            b_bank(0, 0, s)
+        r_make(0, 0)
+        for t in range(4):
+            u_turn(1, t)
+            u_copy(1, t)
+        for ih in range(2):
+            z_turn(1, ih)
+        r_quant(0, 0)
+        z_scale(1, 0)
+        u_sort(2, 0, 2)
+        u_quant(1, 0, 2)
+        z_scale(1, 1)
+        u_quant(1, 2, 4)
+        b_quant(0, 0)
+        r_make(0, 1, nc.gpsimd, "bb_first")
+        for s in range(4):
+            b_bank(0, 1, s)
+        r_front(1)
+        for ih in range(2):
+            z_turn(2, ih)
+            z_scale(2, ih)
+        for t in range(4):
+            u_turn(2, t)
+            u_copy(2, t)
+        r_make(1, 0)
+        r_quant(0, 1)
+        u_quant(2, 0, 2)
+        r_quant(1, 0)
+        u_quant(2, 2, 4)
+        b_quant(0, 1)
+        for s in range(4):
+            b_bank(1, 0, s)
+        b_quant(1, 0)
+        r_make(1, 1, nc.gpsimd, "bb_first")
+        for s in range(4):
+            b_bank(1, 1, s)
         last = G - 1
         r_front(last)
+        r_quant(1, 1)
         for s in range(4):
             b_bank(last, 0, s)
-        b_quant(0, 1)
-        r_make(last, lo)
-        r_make(last, hi)
-        r_quant(last, lo)
+        b_quant(1, 1)
+        r_make(last, 0)
+        r_make(last, 1, part=slice(0, P))
+        r_quant(last, 0)
         b_quant(last, 0)
+        r_make(last, 1, part=slice(P, 256))
         for s in range(4):
             b_bank(last, 1, s)
-        r_quant(last, hi)
-        b_quant(1, 1)
+        r_quant(last, 1)
 
         y_mul(0, 0)
         y_scale(0, 0)
@@ -479,21 +511,21 @@ def tile_siglip_image_feature_gradient_k4_kernel(
         y_copy(0, [0, 1])
         y_copy(0, [2, 3])
         y_mul(1, 2)
-        y_round(1, 1, False)
+        y_round(1, 1, True)
         y_quant(0, [0, 1])
         y_scale(1, 2)
         y_mul(1, 3)
         y_turn(1, [0, 1])
         y_round(1, 2, True)
-        y_copy(1, [0, 1])
         y_quant(0, [2, 3])
         store_words(0, [0, 1, 2, 3])
         y_round_from_bank(1, 3)
+        y_copy(1, [0, 1])
         y_turn(1, [2])
         y_turn(1, [3])
         y_scale(1, 3)
         y_copy(1, [2])
-        y_copy(1, [3])
+        y_copy(1, [3], False)
         y_quant(1, [0, 1])
         store_words(1, [0, 1])
         y_quant(1, [2, 3])

@@ -247,7 +247,7 @@ def tile_siglip_image_feature_gradient_k4_kernel(
 
         def b_copy(g, h, s):
             if s == 0:
-                tag, bufs = ("bb_first", 1) if h == 0 else ("bb_second", 3)
+                tag, bufs = ("bb_first", 1) if h == 0 and g < G - 1 else ("bb", 3)
                 live["bb", g, h] = work.tile([P, 512, 4], BF16, name="bb", tag=tag, bufs=bufs, align_bytes=64)
             dst = live["bb", g, h][:, P * s : P * (s + 1), :]
             nc.scalar.copy(out=dst, in_=live["b_bank", g, h, s][:].rearrange("p (t n) -> p n t", t=4))
@@ -395,10 +395,11 @@ def tile_siglip_image_feature_gradient_k4_kernel(
         load_cb()
         load_x()
         load_scales(ws, w_scales)
-        load_w(0, 2)
+        load_w(0, 1)
         load_u(1, 0, 2)
-        load_u(1, 2, 4)
         load_z(1)
+        load_u(1, 2, 4)
+        load_w(1, 2)
         load_u(2, 0, 2)
         load_z(2)
         load_u(2, 2, 4)
@@ -440,20 +441,24 @@ def tile_siglip_image_feature_gradient_k4_kernel(
             z_scale(0, ih)
         r_front(0)
         u_sort(1, 0, 2)
+        z_sort(1, False)
         u_sort(1, 2, 4)
         for s in range(4):
             b_bank(0, 0, s)
-        r_make(0, 0)
-        for t in range(4):
+        for t in range(2):
             u_turn(1, t)
             u_copy(1, t)
         for ih in range(2):
             z_turn(1, ih)
-        r_quant(0, 0)
+        for t in range(2, 4):
+            u_turn(1, t)
+            u_copy(1, t)
+        r_make(0, 0, part=slice(0, P))
         z_scale(1, 0)
+        z_scale(1, 1)
         u_sort(2, 0, 2)
         u_quant(1, 0, 2)
-        z_scale(1, 1)
+        z_sort(2, False)
         u_quant(1, 2, 4)
         b_quant(0, 0)
         r_make(0, 1, nc.gpsimd, "bb_first")
@@ -466,8 +471,10 @@ def tile_siglip_image_feature_gradient_k4_kernel(
         for t in range(4):
             u_turn(2, t)
             u_copy(2, t)
-        r_make(1, 0)
+        r_make(0, 0, part=slice(P, 256))
         r_quant(0, 1)
+        r_make(1, 0)
+        r_quant(0, 0)
         u_quant(2, 0, 2)
         r_quant(1, 0)
         u_quant(2, 2, 4)
@@ -475,15 +482,16 @@ def tile_siglip_image_feature_gradient_k4_kernel(
         for s in range(4):
             b_bank(1, 0, s)
         b_quant(1, 0)
-        r_make(1, 1, nc.gpsimd, "bb_first")
+        r_make(1, 1, nc.gpsimd, "bb_first", slice(0, P))
         for s in range(4):
             b_bank(1, 1, s)
         last = G - 1
         r_front(last)
+        r_make(1, 1, part=slice(P, 256))
+        b_quant(1, 1)
         r_quant(1, 1)
         for s in range(4):
             b_bank(last, 0, s)
-        b_quant(1, 1)
         r_make(last, 0)
         r_make(last, 1, part=slice(0, P))
         r_quant(last, 0)

@@ -87,10 +87,10 @@ def tile_siglip_image_feature_gradient_k4_kernel(
             )
 
         def load_scales(plane, src):
-            for r in range(4):
+            for q in range(4):
                 nc.sync.dma_start(
-                    out=plane[r:P:32, :, :].bitcast(I32),
-                    in_=src[:, r:16:4, :].rearrange("g q n -> q g n").bitcast(I32),
+                    out=plane[32 * q : 32 * q + 4, :, :].bitcast(I32),
+                    in_=src[:, 4 * q : 4 * q + 4, :].rearrange("g r n -> r g n").bitcast(I32),
                 )
 
         def load_x():

@@ -56,7 +56,7 @@ def tile_siglip_image_feature_gradient_k4_kernel(
         z_raw = [kept("z_raw%d" % g, [P, IT, 512], BF16) for g in range(G)]
         uc = [kept("uc%d" % g, [P, 4, DG * P], U32) for g in range(G)]
         us = [kept("us%d" % g, [P, 4, DG * P], U8) for g in range(G)]
-        zc = [kept("zc%d" % g, [P, I, 4], BF16) for g in range(G)]
+        zc = [kept("zc%d" % g, [P, 2, I, 2], BF16) for g in range(G)]
         rc = [kept("rc%d" % g, [P, I], U32) for g in range(G)]
         rs = [kept("rs%d" % g, [P, I], U8) for g in range(G)]
         bc = [[kept("bc%d_%d" % (g, h), [P, 512], U32) for h in range(NH)] for g in range(G)]
@@ -160,9 +160,9 @@ def tile_siglip_image_feature_gradient_k4_kernel(
 
         def z_scale(g, ih):
             nc.vector.tensor_tensor(
-                out=zc[g][:, 256 * ih : 256 * (ih + 1), :].rearrange("p i (u e) -> p i u e", u=2),
-                in0=live["z_bank", g, ih][:].bitcast(BF16).rearrange("p (u i e) -> p i u e", u=2, e=2),
-                in1=c_neg[:, g, :].rearrange("p (u e) -> p u e", u=2).unsqueeze(1).broadcast_to([P, 256, 2, 2]),
+                out=zc[g][:, :, 256 * ih : 256 * (ih + 1), :],
+                in0=live["z_bank", g, ih][:].bitcast(BF16).rearrange("p (u i e) -> p u i e", u=2, e=2),
+                in1=c_neg[:, g, :].rearrange("p (u e) -> p u e", u=2).unsqueeze(2).broadcast_to([P, 2, 256, 2]),
                 op=ALU.mult,
             )
 
@@ -181,21 +181,27 @@ def tile_siglip_image_feature_gradient_k4_kernel(
             live["l_bank", g, t] = bk
 
         def margin(g, t):
-            mg = work.tile([P, I], F32, name="mg", tag="mg", bufs=4, align_bytes=64)
+            u, e = divmod(t, 2)
+            if e == 0:
+                live["mg", g, u] = work.tile([P, 2, I], F32, name="mg", tag="mg", bufs=2, align_bytes=64)
             nc.vector.scalar_tensor_tensor(
-                out=mg[:],
+                out=live["mg", g, u][:, e, :],
                 in0=live["l_bank", g, t][:],
                 scalar=b_over_c[:, g, t : t + 1],
-                in1=zc[g][:, :, t],
+                in1=zc[g][:, u, :, e],
                 op0=ALU.subtract,
                 op1=ALU.mult,
             )
-            live["mg", g, t] = mg
 
-        def sigmoid(g, t):
-            if t == 0:
-                live["sg", g] = work.tile([P, 4, I], F32, name="sg", tag="sg", bufs=2, align_bytes=64)
-            nc.scalar.activation(out=live["sg", g][:, t, :], in_=live["mg", g, t][:], func=ACT.Sigmoid)
+        def sigmoid(g, u, half):
+            cols = slice(256 * half, 256 * (half + 1))
+            if u == 0 and half == 0:
+                live["sg", g] = work.tile([P, 2, I, 2], F32, name="sg", tag="sg", bufs=2, align_bytes=64)
+            nc.scalar.activation(
+                out=live["sg", g][:, u, cols, :],
+                in_=live["mg", g, u][:, :, cols].rearrange("p e i -> p i e"),
+                func=ACT.Sigmoid,
+            )
 
         def r_make(g, half, engine=nc.vector, tag="rb", part=slice(0, 256)):
             cols = slice(256 * half + part.start, 256 * half + part.stop)
@@ -203,9 +209,9 @@ def tile_siglip_image_feature_gradient_k4_kernel(
                 bufs = 1 if tag == "bb_first" else 2
                 live["rb", g, half] = work.tile([P, 256, 4], BF16, name="rb", tag=tag, bufs=bufs, align_bytes=64)
             engine.tensor_tensor(
-                out=live["rb", g, half][:, part, :].rearrange("p (x i) t -> p x t i", i=4),
-                in0=live["sg", g][:, :, cols].rearrange("p t (x i) -> p x t i", i=4),
-                in1=zc[g][:, cols, :].rearrange("p (x i) t -> p x t i", i=4),
+                out=live["rb", g, half][:, part, :].rearrange("p i (u e) -> p i u e", u=2),
+                in0=live["sg", g][:, :, cols, :].rearrange("p u i e -> p i u e"),
+                in1=zc[g][:, :, cols, :].rearrange("p u i e -> p i u e"),
                 op=ALU.mult,
             )
 
@@ -263,11 +269,12 @@ def tile_siglip_image_feature_gradient_k4_kernel(
                 in_=live["bb", g, h][:].rearrange("p n t -> p (n t)"),
             )
 
-        def y_mul(h, r):
-            bk = bank("bk_y")
-            for g in range(G):
+        def y_mul(h, r, groups=range(G)):
+            if groups[0] == 0:
+                live["y_bank", h, r] = bank("bk_y")
+            for g in groups:
                 nc.tensor.matmul_mx(
-                    out=bk[:],
+                    out=live["y_bank", h, r][:],
                     lhsT=rc[g][:, P * r : P * (r + 1)].bitcast(FP8X4),
                     lhsT_scale=rs[g][:, P * r : P * (r + 1)],
                     rhs=bc[g][h][:].bitcast(FP8X4),
@@ -275,7 +282,6 @@ def tile_siglip_image_feature_gradient_k4_kernel(
                     start=(g == 0),
                     stop=(g == G - 1),
                 )
-            live["y_bank", h, r] = bk
 
         def y_scale(h, r):
             yf = work.tile([P, 512], F32, name="yf", tag="yf", bufs=8, align_bytes=64)
@@ -414,31 +420,29 @@ def tile_siglip_image_feature_gradient_k4_kernel(
             for t in range(4):
                 logits(g, t)
                 margin(g, t)
-                sigmoid(g, t)
+                if t % 2:
+                    sigmoid(g, t // 2, 0)
+                    sigmoid(g, t // 2, 1)
 
         u_turn(0, 0)
         u_copy(0, 0)
-        u_sort(0, 1, 2)
-        u_turn(0, 1)
-        u_copy(0, 1)
-        u_sort(0, 2, 3)
-        c_turn()
-        u_quant(0, 0, 1)
-        u_sort(0, 3, 4)
-        for t in range(2, 4):
+        for t in range(1, 4):
+            u_sort(0, t, t + 1)
             u_turn(0, t)
             u_copy(0, t)
-        c_negate()
-        u_quant(0, 1, 2)
-        c_guard()
-        u_quant(0, 2, 3)
-        c_invert()
+        c_turn()
         for ih in range(2):
             z_turn(0, ih)
-        u_quant(0, 3, 4)
+        u_quant(0, 0, 1)
+        u_quant(0, 1, 2)
+        c_negate()
+        u_quant(0, 2, 3)
+        c_guard()
+        z_scale(0, 0)
+        c_invert()
+        z_scale(0, 1)
         b_divide()
-        for ih in range(2):
-            z_scale(0, ih)
+        u_quant(0, 3, 4)
         r_front(0)
         u_sort(1, 0, 2)
         z_sort(1, False)
@@ -501,13 +505,13 @@ def tile_siglip_image_feature_gradient_k4_kernel(
             b_bank(last, 1, s)
         r_quant(last, 1)
 
-        y_mul(0, 0)
-        y_scale(0, 0)
-        b_quant(last, 1)
-        y_round(0, 0, True)
-        for r in range(1, IT):
-            y_mul(0, r)
+        y_mul(0, 0, range(last))
+        y_mul(0, 1, range(last))
+        for r in range(IT):
+            y_mul(0, r, range(last, G) if r < 2 else range(G))
             y_scale(0, r)
+            if r == 1:
+                b_quant(last, 1)
             y_round(0, r, True)
         y_mul(1, 0)
         y_scale(1, 0)

@@ -107,7 +107,10 @@ def tile_siglip_image_feature_gradient_k4_kernel(
             n = t1 - t0
             srt = work.tile([P, n * DG, 2, P], F32, name="srt", tag="srt", bufs=3, align_bytes=64)
             words = u_pack[g, t0][:, 0:n, :].rearrange("q t k -> q (t k)").bitcast(F32)
-            nc.vector.tensor_copy(out=srt[:], in_=words.rearrange("q (s p u) -> q s u p", p=P, u=2))
+            nc.vector.tensor_copy(
+                out=srt[:].rearrange("q s u (x i) -> q s x u i", i=4),
+                in_=words.rearrange("q (s x i u) -> q s x u i", x=P // 4, i=4, u=2),
+            )
             for t in range(t0, t1):
                 live["srt", g, t] = srt[:, DG * (t - t0) : DG * (t - t0 + 1)]
 
@@ -124,10 +127,10 @@ def tile_siglip_image_feature_gradient_k4_kernel(
                     nc.tensor.transpose(bk[:, P * s : P * (s + 1)], src, ident[:])
             live["u_bank", g, t] = bk
 
-        def u_copy(g, t):
+        def u_copy(g, t, copy=nc.scalar.copy):
             if t % 2 == 0:
                 live["ug", g, t // 2] = work.tile([P, 2, D], BF16, name="ug", tag="ug", bufs=2, align_bytes=64)
-            nc.scalar.copy(
+            copy(
                 out=live["ug", g, t // 2][:, t % 2, :].bitcast(F32).rearrange("p (d m u) -> p d m u", d=DG, u=2),
                 in_=live["u_bank", g, t][:].rearrange("p (d u m) -> p d m u", d=DG, u=2),
             )
@@ -143,7 +146,10 @@ def tile_siglip_image_feature_gradient_k4_kernel(
             zs = work.tile([P, IT, 2, P], F32, name="zs", tag="zs", bufs=1, align_bytes=64)
             words = z_raw[g][:].rearrange("q r j -> q (r j)").bitcast(F32)
             copy = nc.scalar.copy if on_scalar else nc.vector.tensor_copy
-            copy(out=zs[:], in_=words.rearrange("q (r p u) -> q r u p", r=IT, u=2))
+            copy(
+                out=zs[:].rearrange("q r u (x i) -> q r x u i", i=4),
+                in_=words.rearrange("q (r x i u) -> q r x u i", r=IT, i=4, u=2),
+            )
             live["zs", g] = zs
 
         def z_turn(g, ih):
@@ -180,15 +186,15 @@ def tile_siglip_image_feature_gradient_k4_kernel(
                 )
             live["l_bank", g, t] = bk
 
-        def margin(g, t):
+        def margin(g, t, cols=slice(0, I)):
             u, e = divmod(t, 2)
             if e == 0:
                 live["mg", g, u] = work.tile([P, 2, I], F32, name="mg", tag="mg", bufs=2, align_bytes=64)
             nc.vector.scalar_tensor_tensor(
-                out=live["mg", g, u][:, e, :],
-                in0=live["l_bank", g, t][:],
+                out=live["mg", g, u][:, e, cols],
+                in0=live["l_bank", g, t][:, cols],
                 scalar=b_over_c[:, g, t : t + 1],
-                in1=zc[g][:, u, :, e],
+                in1=zc[g][:, u, cols, e],
                 op0=ALU.subtract,
                 op1=ALU.mult,
             )
@@ -205,7 +211,7 @@ def tile_siglip_image_feature_gradient_k4_kernel(
 
         def r_make(g, half, engine=nc.vector, tag="rb", part=slice(0, 256)):
             cols = slice(256 * half + part.start, 256 * half + part.stop)
-            if part.start == 0:
+            if ("rb", g, half) not in live:
                 bufs = 1 if tag == "bb_first" else 2
                 live["rb", g, half] = work.tile([P, 256, 4], BF16, name="rb", tag=tag, bufs=bufs, align_bytes=64)
             engine.tensor_tensor(
@@ -251,12 +257,12 @@ def tile_siglip_image_feature_gradient_k4_kernel(
             for s in banks:
                 b_copy(g, h, s)
 
-        def b_copy(g, h, s):
+        def b_copy(g, h, s, copy=nc.scalar.copy):
             if s == 0:
                 tag, bufs = ("bb_first", 1) if h == 0 and g < G - 1 else ("bb", 3)
                 live["bb", g, h] = work.tile([P, 512, 4], BF16, name="bb", tag=tag, bufs=bufs, align_bytes=64)
             dst = live["bb", g, h][:, P * s : P * (s + 1), :]
-            nc.scalar.copy(out=dst, in_=live["b_bank", g, h, s][:].rearrange("p (t n) -> p n t", t=4))
+            copy(out=dst, in_=live["b_bank", g, h, s][:].rearrange("p (t n) -> p n t", t=4))
 
         def b_bank(g, h, s):
             b_mul(g, h, s)
@@ -298,8 +304,8 @@ def tile_siglip_image_feature_gradient_k4_kernel(
 
         def y_round(h, r, on_scalar):
             yb = work.tile([P, 512], BF16, name="yb", tag="yb", bufs=8, align_bytes=64)
-            dst = yb[:].rearrange("q (u p e) -> q u p e", u=2, e=2)
-            src = live["yf", h, r][:].rearrange("q (p u e) -> q u p e", u=2, e=2)
+            dst = yb[:].rearrange("q (u x p e) -> q x u p e", u=2, p=4, e=2)
+            src = live["yf", h, r][:].rearrange("q (x p u e) -> q x u p e", p=4, u=2, e=2)
             if on_scalar:
                 nc.scalar.copy(out=dst, in_=src)
             else:
@@ -419,10 +425,12 @@ def tile_siglip_image_feature_gradient_k4_kernel(
         def r_front(g):
             for t in range(4):
                 logits(g, t)
-                margin(g, t)
-                if t % 2:
-                    sigmoid(g, t // 2, 0)
-                    sigmoid(g, t // 2, 1)
+                if t % 2 == 0:
+                    margin(g, t)
+                else:
+                    for half in range(2):
+                        margin(g, t, slice(256 * half, 256 * (half + 1)))
+                        sigmoid(g, t // 2, half)
 
         u_turn(0, 0)
         u_copy(0, 0)
@@ -446,9 +454,11 @@ def tile_siglip_image_feature_gradient_k4_kernel(
         r_front(0)
         u_sort(1, 0, 2)
         z_sort(1, False)
+        r_make(0, 0, part=slice(0, P))
         u_sort(1, 2, 4)
         for s in range(4):
-            b_bank(0, 0, s)
+            b_mul(0, 0, s)
+            b_copy(0, 0, s, nc.vector.tensor_copy if s == 2 else nc.scalar.copy)
         for t in range(2):
             u_turn(1, t)
             u_copy(1, t)
@@ -457,13 +467,12 @@ def tile_siglip_image_feature_gradient_k4_kernel(
         for t in range(2, 4):
             u_turn(1, t)
             u_copy(1, t)
-        r_make(0, 0, part=slice(0, P))
         z_scale(1, 0)
         z_scale(1, 1)
         u_sort(2, 0, 2)
         u_quant(1, 0, 2)
-        z_sort(2, False)
         u_quant(1, 2, 4)
+        z_sort(2, False)
         b_quant(0, 0)
         r_make(0, 1, nc.gpsimd, "bb_first")
         for s in range(4):
@@ -475,8 +484,8 @@ def tile_siglip_image_feature_gradient_k4_kernel(
         for t in range(4):
             u_turn(2, t)
             u_copy(2, t)
-        r_make(0, 0, part=slice(P, 256))
         r_quant(0, 1)
+        r_make(0, 0, part=slice(P, 256))
         r_make(1, 0)
         r_quant(0, 0)
         u_quant(2, 0, 2)
@@ -486,17 +495,18 @@ def tile_siglip_image_feature_gradient_k4_kernel(
         for s in range(4):
             b_bank(1, 0, s)
         b_quant(1, 0)
-        r_make(1, 1, nc.gpsimd, "bb_first", slice(0, P))
+        r_make(1, 1, nc.gpsimd, "bb_first")
         for s in range(4):
             b_bank(1, 1, s)
         last = G - 1
         r_front(last)
-        r_make(1, 1, part=slice(P, 256))
         b_quant(1, 1)
         r_quant(1, 1)
         for s in range(4):
-            b_bank(last, 0, s)
+            b_mul(last, 0, s)
         r_make(last, 0)
+        for s in range(4):
+            b_copy(last, 0, s, nc.vector.tensor_copy if s == 9 else nc.scalar.copy)
         r_make(last, 1, part=slice(0, P))
         r_quant(last, 0)
         b_quant(last, 0)

@@ -42,6 +42,7 @@ def tile_siglip_image_feature_gradient_k4_kernel(
         ident = kept("ident", [P, P], F32)
         cb_rows = kept("cb_rows", [P, 512], BF16)
         a_sb = kept("a_sb", [P, IT, 2], BF16)
+        warm = kept("warm", [P, 1], F32)
         c_neg = kept("c_neg", [P, G, 4], BF16)
         c_safe = kept("c_safe", [P, G, 4], F32)
         c_inv = kept("c_inv", [P, G, 4], F32)
@@ -100,14 +101,14 @@ def tile_siglip_image_feature_gradient_k4_kernel(
             )
 
         def load_cb():
-            nc.scalar.dma_start(out=cb_rows[0:G, :], in_=c.rearrange("(g j) -> g j", g=G))
-            nc.scalar.dma_start(out=cb_rows[G : 2 * G, :], in_=b.rearrange("(g j) -> g j", g=G))
+            nc.gpsimd.dma_start(out=cb_rows[0:G, :], in_=c.rearrange("(g j) -> g j", g=G))
+            nc.gpsimd.dma_start(out=cb_rows[G : 2 * G, :], in_=b.rearrange("(g j) -> g j", g=G))
 
-        def u_sort(g, t0, t1):
+        def u_sort(g, t0, t1, copy=nc.vector.tensor_copy):
             n = t1 - t0
             srt = work.tile([P, n * DG, 2, P], F32, name="srt", tag="srt", bufs=3, align_bytes=64)
             words = u_pack[g, t0][:, 0:n, :].rearrange("q t k -> q (t k)").bitcast(F32)
-            nc.vector.tensor_copy(
+            copy(
                 out=srt[:].rearrange("q s u (x i) -> q s x u i", i=4),
                 in_=words.rearrange("q (s x i u) -> q s x u i", x=P // 4, i=4, u=2),
             )
@@ -212,8 +213,10 @@ def tile_siglip_image_feature_gradient_k4_kernel(
         def r_make(g, half, engine=nc.vector, tag="rb", part=slice(0, 256)):
             cols = slice(256 * half + part.start, 256 * half + part.stop)
             if ("rb", g, half) not in live:
-                bufs = 1 if tag == "bb_first" else 2
-                live["rb", g, half] = work.tile([P, 256, 4], BF16, name="rb", tag=tag, bufs=bufs, align_bytes=64)
+                if tag == "rb":
+                    live["rb", g, half] = work.tile([P, 256, 4], BF16, name="rb", tag=tag, bufs=3, align_bytes=64)
+                else:
+                    live["rb", g, half] = kept(tag, [P, 256, 4], BF16)
             engine.tensor_tensor(
                 out=live["rb", g, half][:, part, :].rearrange("p i (u e) -> p i u e", u=2),
                 in0=live["sg", g][:, :, cols, :].rearrange("p u i e -> p i u e"),
@@ -257,10 +260,19 @@ def tile_siglip_image_feature_gradient_k4_kernel(
             for s in banks:
                 b_copy(g, h, s)
 
+        def b_slice(g, h, t):
+            for s in range(4):
+                if t == 0:
+                    live["b_bank", g, h, s] = bank("bk_b")
+                for d in range(DG):
+                    b_pass(live["b_bank", g, h, s], g, h, s, t, d)
+
         def b_copy(g, h, s, copy=nc.scalar.copy):
             if s == 0:
-                tag, bufs = ("bb_first", 1) if h == 0 and g < G - 1 else ("bb", 3)
-                live["bb", g, h] = work.tile([P, 512, 4], BF16, name="bb", tag=tag, bufs=bufs, align_bytes=64)
+                if h == 0 and g < G - 1:
+                    live["bb", g, h] = kept("bb_first", [P, 512, 4], BF16)
+                else:
+                    live["bb", g, h] = work.tile([P, 512, 4], BF16, name="bb", tag="bb", bufs=3, align_bytes=64)
             dst = live["bb", g, h][:, P * s : P * (s + 1), :]
             copy(out=dst, in_=live["b_bank", g, h, s][:].rearrange("p (t n) -> p n t", t=4))
 
@@ -403,15 +415,15 @@ def tile_siglip_image_feature_gradient_k4_kernel(
         load_u(0, 1, 2)
         load_u(0, 2, 3)
         load_u(0, 3, 4)
-        load_z(0)
         load_cb()
-        load_x()
         load_scales(ws, w_scales)
         load_w(0, 1)
-        load_u(1, 0, 2)
-        load_z(1)
-        load_u(1, 2, 4)
+        load_z(0)
+        load_x()
         load_w(1, 2)
+        load_u(1, 0, 2)
+        load_u(1, 2, 4)
+        load_z(1)
         load_u(2, 0, 2)
         load_z(2)
         load_u(2, 2, 4)
@@ -432,51 +444,55 @@ def tile_siglip_image_feature_gradient_k4_kernel(
                         margin(g, t, slice(256 * half, 256 * (half + 1)))
                         sigmoid(g, t // 2, half)
 
+        nc.scalar.activation(out=warm[:], in_=ident[:, 0:1], func=ACT.Sigmoid)
         u_turn(0, 0)
         u_copy(0, 0)
         for t in range(1, 4):
             u_sort(0, t, t + 1)
             u_turn(0, t)
             u_copy(0, t)
+        for t in range(3):
+            u_quant(0, t, t + 1)
+            b_slice(0, 0, t)
+        u_quant(0, 3, 4)
+        z_sort(0, False)
         c_turn()
         for ih in range(2):
             z_turn(0, ih)
-        u_quant(0, 0, 1)
-        u_quant(0, 1, 2)
+        b_slice(0, 0, 3)
+        for s in range(4):
+            b_copy(0, 0, s)
         c_negate()
-        u_quant(0, 2, 3)
         c_guard()
         z_scale(0, 0)
         c_invert()
         z_scale(0, 1)
         b_divide()
-        u_quant(0, 3, 4)
         r_front(0)
-        u_sort(1, 0, 2)
-        z_sort(1, False)
-        r_make(0, 0, part=slice(0, P))
         u_sort(1, 2, 4)
-        for s in range(4):
-            b_mul(0, 0, s)
-            b_copy(0, 0, s, nc.vector.tensor_copy if s == 2 else nc.scalar.copy)
-        for t in range(2):
+        b_mul(0, 1, 0)
+        b_mul(0, 1, 1)
+        for t in range(4):
             u_turn(1, t)
             u_copy(1, t)
+        z_sort(1, False)
+        b_copy(0, 1, 0, nc.vector.tensor_copy)
+        b_copy(0, 1, 1, nc.vector.tensor_copy)
         for ih in range(2):
             z_turn(1, ih)
-        for t in range(2, 4):
-            u_turn(1, t)
-            u_copy(1, t)
+        b_mul(0, 1, 2)
+        b_mul(0, 1, 3)
+        r_make(0, 0, nc.gpsimd, "z_raw1", slice(0, P))
         z_scale(1, 0)
-        z_scale(1, 1)
-        u_sort(2, 0, 2)
         u_quant(1, 0, 2)
+        z_scale(1, 1)
         u_quant(1, 2, 4)
-        z_sort(2, False)
         b_quant(0, 0)
         r_make(0, 1, nc.gpsimd, "bb_first")
-        for s in range(4):
-            b_bank(0, 1, s)
+        b_copy(0, 1, 2)
+        b_copy(0, 1, 3)
+        u_sort(2, 0, 2, nc.scalar.copy)
+        u_sort(2, 2, 4, nc.scalar.copy)
         r_front(1)
         for ih in range(2):
             z_turn(2, ih)

@@ -468,6 +468,7 @@ def tile_siglip_image_feature_gradient_k4_kernel(
         c_invert()
         z_scale(0, 1)
         b_divide()
+        u_sort(1, 0, 2, nc.gpsimd.tensor_copy)
         r_front(0)
         u_sort(1, 2, 4)
         b_mul(0, 1, 0)

@@ -21,6 +21,7 @@ G = J // 512
 DG = D // 512
 NH = N // 512
 IT = I // P
+HALF = I // 2
 
 
 def tile_siglip_image_feature_gradient_k4_kernel(
@@ -48,24 +49,25 @@ def tile_siglip_image_feature_gradient_k4_kernel(
         c_inv = kept("c_inv", [P, G, 4], F32)
         b_over_c = kept("b_over_c", [P, G, 4], F32)
         gain_sb = kept("gain_sb", [P, N], BF16)
-        xw = kept("xw", [P, DG, I], U32)
+        xw = [kept("xw%d" % ih, [P, DG, HALF], U32) for ih in range(2)]
         xs = kept("xs", [P, DG, I], U8)
         ww = {}
-        ws = kept("ws", [P, DG, N], U8)
+        ws = [kept("ws%d" % h, [P, DG, 512], U8) for h in range(NH)]
         u_raw = {}
         u_pack = {}
-        z_raw = [kept("z_raw%d" % g, [P, IT, 512], BF16) for g in range(G)]
+        z_raw = {}
         uc = [kept("uc%d" % g, [P, 4, DG * P], U32) for g in range(G)]
         us = [kept("us%d" % g, [P, 4, DG * P], U8) for g in range(G)]
-        zc = [kept("zc%d" % g, [P, 2, I, 2], BF16) for g in range(G)]
+        zc = [[kept("zc%d_%d" % (g, ih), [P, 2, HALF, 2], BF16) for ih in range(2)] for g in range(G)]
         rc = [kept("rc%d" % g, [P, I], U32) for g in range(G)]
         rs = [kept("rs%d" % g, [P, I], U8) for g in range(G)]
         bc = [[kept("bc%d_%d" % (g, h), [P, 512], U32) for h in range(NH)] for g in range(G)]
         bs = [[kept("bs%d_%d" % (g, h), [P, 512], U8) for h in range(NH)] for g in range(G)]
         yg = [kept("yg%d" % h, [P, I, 4], BF16) for h in range(NH)]
         yc = [kept("yc%d" % h, [P, I], U32) for h in range(NH)]
-        ys = kept("ys", [P, I], U8)
+        ys = kept("ys", [P, NH, I], U8)
         live = {}
+        on_vector, on_scalar, on_gpsimd = nc.vector.tensor_copy, nc.scalar.copy, nc.gpsimd.tensor_copy
 
         def load_u(g, t0, t1):
             rows = U[512 * g : 512 * (g + 1), :].rearrange("(m t) k -> m t k", t=4)
@@ -76,37 +78,40 @@ def tile_siglip_image_feature_gradient_k4_kernel(
                 u_raw[g, t] = raw[:, t - t0, :]
 
         def load_w(h0, h1):
+            load_scales(ws[h0], w_scales, slice(512 * h0, 512 * h1))
             src = w_words[:, :, N * h0 : N * h1].rearrange("g p n -> p g n")
             raw = kept("ww%d" % h0, [P, DG, N * (h1 - h0)], U8)
             nc.sync.dma_start(out=raw[:].bitcast(I32), in_=src.bitcast(I32))
             for h in range(h0, h1):
                 ww[h] = raw[:, :, N * (h - h0) : N * (h - h0 + 1)]
 
-        def load_z(g):
-            nc.sync.dma_start(
-                out=z_raw[g][:], in_=Z[:, 512 * g : 512 * (g + 1)].rearrange("(r p) j -> p r j", p=P)
-            )
+        def load_z(g, i0, i1):
+            raw = kept("z_raw%d_%d" % (g, i0), [P, 2 * (i1 - i0), 512], BF16)
+            src = Z[HALF * i0 : HALF * i1, 512 * g : 512 * (g + 1)]
+            nc.sync.dma_start(out=raw[:], in_=src.rearrange("(r p) j -> p r j", p=P))
+            z_raw[g, i0] = raw
 
-        def load_scales(plane, src):
+        def load_scales(plane, src, cols):
             for q in range(4):
                 nc.sync.dma_start(
                     out=plane[32 * q : 32 * q + 4, :, :].bitcast(I32),
-                    in_=src[:, 4 * q : 4 * q + 4, :].rearrange("g r n -> r g n").bitcast(I32),
+                    in_=src[:, 4 * q : 4 * q + 4, cols].rearrange("g r n -> r g n").bitcast(I32),
                 )
 
-        def load_x():
-            load_scales(xs, x_scales)
-            nc.sync.dma_start(
-                out=xw[:].bitcast(I32), in_=x_words.rearrange("g p n t -> p g (n t)").bitcast(I32)
-            )
+        def load_x(ih):
+            src = x_words[:, :, HALF * ih : HALF * (ih + 1), :].rearrange("g p n t -> p g (n t)")
+            nc.sync.dma_start(out=xw[ih][:].bitcast(I32), in_=src.bitcast(I32))
 
         def load_cb():
             nc.gpsimd.dma_start(out=cb_rows[0:G, :], in_=c.rearrange("(g j) -> g j", g=G))
             nc.gpsimd.dma_start(out=cb_rows[G : 2 * G, :], in_=b.rearrange("(g j) -> g j", g=G))
 
-        def u_sort(g, t0, t1, copy=nc.vector.tensor_copy):
+        def u_sort(g, t0, t1, copy=on_vector, slot=None):
             n = t1 - t0
-            srt = work.tile([P, n * DG, 2, P], F32, name="srt", tag="srt", bufs=3, align_bytes=64)
+            if slot:
+                srt = kept(slot, [P, n * DG, 2, P], F32)
+            else:
+                srt = work.tile([P, n * DG, 2, P], F32, name="srt", tag="srt", bufs=3, align_bytes=64)
             words = u_pack[g, t0][:, 0:n, :].rearrange("q t k -> q (t k)").bitcast(F32)
             copy(
                 out=srt[:].rearrange("q s u (x i) -> q s x u i", i=4),
@@ -130,7 +135,7 @@ def tile_siglip_image_feature_gradient_k4_kernel(
 
         def u_copy(g, t, copy=nc.scalar.copy):
             if t % 2 == 0:
-                live["ug", g, t // 2] = work.tile([P, 2, D], BF16, name="ug", tag="ug", bufs=2, align_bytes=64)
+                live["ug", g, t // 2] = kept("ug%d" % (t // 2), [P, 2, D], BF16)
             copy(
                 out=live["ug", g, t // 2][:, t % 2, :].bitcast(F32).rearrange("p (d m u) -> p d m u", d=DG, u=2),
                 in_=live["u_bank", g, t][:].rearrange("p (d u m) -> p d m u", d=DG, u=2),
@@ -143,93 +148,88 @@ def tile_siglip_image_feature_gradient_k4_kernel(
                 in_=live["ug", g, t0 // 2][:, t0 % 2 : t0 % 2 + t1 - t0, :].rearrange("p t k -> p (t k)"),
             )
 
-        def z_sort(g, on_scalar):
-            zs = work.tile([P, IT, 2, P], F32, name="zs", tag="zs", bufs=1, align_bytes=64)
-            words = z_raw[g][:].rearrange("q r j -> q (r j)").bitcast(F32)
-            copy = nc.scalar.copy if on_scalar else nc.vector.tensor_copy
+        def z_sort(g, i0, i1, copy=on_vector):
+            n = 2 * (i1 - i0)
+            zs = work.tile([P, n, 2, P], F32, name="zs", tag="zs", bufs=4, align_bytes=64)
+            words = z_raw[g, i0][:].rearrange("q r j -> q (r j)").bitcast(F32)
             copy(
                 out=zs[:].rearrange("q r u (x i) -> q r x u i", i=4),
-                in_=words.rearrange("q (r x i u) -> q r x u i", r=IT, i=4, u=2),
+                in_=words.rearrange("q (r x i u) -> q r x u i", r=n, i=4, u=2),
             )
-            live["zs", g] = zs
+            for ih in range(i0, i1):
+                live["zs", g, ih] = zs[:, 2 * (ih - i0) : 2 * (ih - i0 + 1)]
 
         def z_turn(g, ih):
             bk = bank("bk_z")
             for r in range(2):
                 for u in range(2):
-                    col = 256 * u + P * r
-                    if ("zs", g) in live:
-                        src = live["zs", g][:, 2 * ih + r, u, :]
-                    else:
-                        src = z_raw[g][:, 2 * ih + r, :].bitcast(F32)[:, u:256:2]
-                    nc.tensor.transpose(bk[:, col : col + P], src, ident[:])
+                    col = HALF * u + P * r
+                    nc.tensor.transpose(bk[:, col : col + P], live["zs", g, ih][:, r, u, :], ident[:])
             live["z_bank", g, ih] = bk
 
         def z_scale(g, ih):
             nc.vector.tensor_tensor(
-                out=zc[g][:, :, 256 * ih : 256 * (ih + 1), :],
+                out=zc[g][ih][:],
                 in0=live["z_bank", g, ih][:].bitcast(BF16).rearrange("p (u i e) -> p u i e", u=2, e=2),
                 in1=c_neg[:, g, :].rearrange("p (u e) -> p u e", u=2).unsqueeze(2).broadcast_to([P, 2, 256, 2]),
                 op=ALU.mult,
             )
 
-        def logits(g, t):
+        def logits(g, ih, u):
             bk = bank("bk_l")
-            for d in range(DG):
-                nc.tensor.matmul_mx(
-                    out=bk[:],
-                    lhsT=uc[g][:, t, P * d : P * (d + 1)].bitcast(FP8X4),
-                    lhsT_scale=us[g][:, t, P * d : P * (d + 1)],
-                    rhs=xw[:, d, :].bitcast(FP8X4),
-                    rhs_scale=xs[:, d, :],
-                    start=(d == 0),
-                    stop=(d == DG - 1),
+            for e in range(2):
+                t = 2 * u + e
+                for d in range(DG):
+                    nc.tensor.matmul_mx(
+                        out=bk[:, HALF * e : HALF * (e + 1)],
+                        lhsT=uc[g][:, t, P * d : P * (d + 1)].bitcast(FP8X4),
+                        lhsT_scale=us[g][:, t, P * d : P * (d + 1)],
+                        rhs=xw[ih][:, d, :].bitcast(FP8X4),
+                        rhs_scale=xs[:, d, HALF * ih : HALF * (ih + 1)],
+                        start=(d == 0),
+                        stop=(d == DG - 1),
+                    )
+            live["l_bank", g, ih, u] = bk
+
+        def margin(g, ih, u):
+            mg = work.tile([P, 2, HALF], F32, name="mg", tag="mg", bufs=3, align_bytes=64)
+            for e in range(2):
+                t = 2 * u + e
+                nc.vector.scalar_tensor_tensor(
+                    out=mg[:, e, :],
+                    in0=live["l_bank", g, ih, u][:, HALF * e : HALF * (e + 1)],
+                    scalar=b_over_c[:, g, t : t + 1],
+                    in1=zc[g][ih][:, u, :, e],
+                    op0=ALU.subtract,
+                    op1=ALU.mult,
                 )
-            live["l_bank", g, t] = bk
+            live["mg", g, ih, u] = mg
 
-        def margin(g, t, cols=slice(0, I)):
-            u, e = divmod(t, 2)
-            if e == 0:
-                live["mg", g, u] = work.tile([P, 2, I], F32, name="mg", tag="mg", bufs=2, align_bytes=64)
-            nc.vector.scalar_tensor_tensor(
-                out=live["mg", g, u][:, e, cols],
-                in0=live["l_bank", g, t][:, cols],
-                scalar=b_over_c[:, g, t : t + 1],
-                in1=zc[g][:, u, cols, e],
-                op0=ALU.subtract,
-                op1=ALU.mult,
-            )
-
-        def sigmoid(g, u, half):
-            cols = slice(256 * half, 256 * (half + 1))
-            if u == 0 and half == 0:
-                live["sg", g] = work.tile([P, 2, I, 2], F32, name="sg", tag="sg", bufs=2, align_bytes=64)
+        def sigmoid(g, ih, u):
+            if u == 0:
+                live["sg", g, ih] = work.tile([P, 2, HALF, 2], F32, name="sg", tag="sg", bufs=4, align_bytes=64)
             nc.scalar.activation(
-                out=live["sg", g][:, u, cols, :],
-                in_=live["mg", g, u][:, :, cols].rearrange("p e i -> p i e"),
+                out=live["sg", g, ih][:, u],
+                in_=live["mg", g, ih, u][:].rearrange("p e i -> p i e"),
                 func=ACT.Sigmoid,
             )
 
-        def r_make(g, half, engine=nc.vector, tag="rb", part=slice(0, 256)):
-            cols = slice(256 * half + part.start, 256 * half + part.stop)
-            if ("rb", g, half) not in live:
-                if tag == "rb":
-                    live["rb", g, half] = work.tile([P, 256, 4], BF16, name="rb", tag=tag, bufs=3, align_bytes=64)
-                else:
-                    live["rb", g, half] = kept(tag, [P, 256, 4], BF16)
+        def r_make(g, ih, engine, slot, part=slice(0, HALF)):
+            rb = kept(slot, [P, part.stop - part.start, 4], BF16)
             engine.tensor_tensor(
-                out=live["rb", g, half][:, part, :].rearrange("p i (u e) -> p i u e", u=2),
-                in0=live["sg", g][:, :, cols, :].rearrange("p u i e -> p i u e"),
-                in1=zc[g][:, :, cols, :].rearrange("p u i e -> p i u e"),
+                out=rb[:].rearrange("p i (u e) -> p i u e", u=2),
+                in0=live["sg", g, ih][:, :, part, :].rearrange("p u i e -> p i u e"),
+                in1=zc[g][ih][:, :, part, :].rearrange("p u i e -> p i u e"),
                 op=ALU.mult,
             )
+            live["rb", g, ih, part.start] = rb
 
-        def r_quant(g, half):
-            cols = slice(256 * half, 256 * (half + 1))
+        def r_quant(g, ih, part=slice(0, HALF)):
+            cols = slice(HALF * ih + part.start, HALF * ih + part.stop)
             nc.vector.quantize_mx(
                 out=rc[g][:, cols].bitcast(FP8X4),
                 scales=rs[g][:, cols],
-                in_=live["rb", g, half][:].rearrange("p i t -> p (i t)"),
+                in_=live["rb", g, ih, part.start][:].rearrange("p i t -> p (i t)"),
             )
 
         def b_pass(bk, g, h, s, t, d):
@@ -238,7 +238,7 @@ def tile_siglip_image_feature_gradient_k4_kernel(
                 lhsT=uc[g][:, t, P * d : P * (d + 1)].bitcast(FP8X4),
                 lhsT_scale=us[g][:, t, P * d : P * (d + 1)],
                 rhs=ww[h][:, d, 256 * s : 256 * (s + 1)].bitcast(FP4X4),
-                rhs_scale=ws[:, d, 512 * h + P * s : 512 * h + P * (s + 1)],
+                rhs_scale=ws[h][:, d, P * s : P * (s + 1)],
                 start=(d == 0),
                 stop=(d == DG - 1),
             )
@@ -250,16 +250,6 @@ def tile_siglip_image_feature_gradient_k4_kernel(
                     b_pass(bk, g, h, s, t, d)
             live["b_bank", g, h, s] = bk
 
-        def b_group(g, h, banks):
-            for s in banks:
-                live["b_bank", g, h, s] = bank("bk_b")
-            for t in range(4):
-                for d in range(DG):
-                    for s in banks:
-                        b_pass(live["b_bank", g, h, s], g, h, s, t, d)
-            for s in banks:
-                b_copy(g, h, s)
-
         def b_slice(g, h, t):
             for s in range(4):
                 if t == 0:
@@ -268,11 +258,8 @@ def tile_siglip_image_feature_gradient_k4_kernel(
                     b_pass(live["b_bank", g, h, s], g, h, s, t, d)
 
         def b_copy(g, h, s, copy=nc.scalar.copy):
-            if s == 0:
-                if h == 0 and g < G - 1:
-                    live["bb", g, h] = kept("bb_first", [P, 512, 4], BF16)
-                else:
-                    live["bb", g, h] = work.tile([P, 512, 4], BF16, name="bb", tag="bb", bufs=3, align_bytes=64)
+            if ("bb", g, h) not in live:
+                live["bb", g, h] = kept("bb%d" % ((2 * g + h) % 3), [P, 512, 4], BF16)
             dst = live["bb", g, h][:, P * s : P * (s + 1), :]
             copy(out=dst, in_=live["b_bank", g, h, s][:].rearrange("p (t n) -> p n t", t=4))
 
@@ -314,14 +301,11 @@ def tile_siglip_image_feature_gradient_k4_kernel(
             nc.sync.dma_start(out=out_0[P * r : P * (r + 1), 512 * h : 512 * (h + 1)], in_=yf[:])
             live["yf", h, r] = yf
 
-        def y_round(h, r, on_scalar):
+        def y_round(h, r, copy=nc.scalar.copy):
             yb = work.tile([P, 512], BF16, name="yb", tag="yb", bufs=8, align_bytes=64)
             dst = yb[:].rearrange("q (u x p e) -> q x u p e", u=2, p=4, e=2)
             src = live["yf", h, r][:].rearrange("q (x p u e) -> q x u p e", p=4, u=2, e=2)
-            if on_scalar:
-                nc.scalar.copy(out=dst, in_=src)
-            else:
-                nc.vector.tensor_copy(out=dst, in_=src)
+            copy(out=dst, in_=src)
             live["yb", h, r] = yb
 
         def y_round_from_bank(h, r):
@@ -339,18 +323,17 @@ def tile_siglip_image_feature_gradient_k4_kernel(
                 )
             live["yb", h, r] = yb
 
-        def y_turn(h, rows):
+        def y_turn(*tiles):
             bk = bank("bk_t")
-            for k, r in enumerate(rows):
+            for k, (h, r) in enumerate(tiles):
                 words = live["yb", h, r][:].bitcast(F32)
                 for u in range(2):
                     col = P * (2 * k + u)
                     nc.tensor.transpose(bk[:, col : col + P], words[:, P * u : P * (u + 1)], ident[:])
-            live["t_bank", h, rows[0]] = bk
+                live["t_bank", h, r] = bk[:, 2 * P * k :]
 
-        def y_copy(h, rows, on_scalar=True):
+        def y_copy(h, rows, copy=on_scalar):
             n = len(rows)
-            copy = nc.scalar.copy if on_scalar else nc.vector.tensor_copy
             dst = yg[h][:, P * rows[0] : P * (rows[0] + n), :].rearrange("p i t -> p (i t)").bitcast(F32)
             copy(
                 out=dst.rearrange("p (k i u) -> p k i u", k=n, u=2),
@@ -361,7 +344,7 @@ def tile_siglip_image_feature_gradient_k4_kernel(
             cols = slice(P * rows[0], P * (rows[0] + len(rows)))
             nc.vector.quantize_mx(
                 out=yc[h][:, cols].bitcast(FP8X4),
-                scales=ys[4 * h :, cols],
+                scales=ys[:, h, cols],
                 in_=yg[h][:, cols, :].rearrange("p i t -> p (i t)"),
             )
 
@@ -374,7 +357,8 @@ def tile_siglip_image_feature_gradient_k4_kernel(
             for q in range(4):
                 queue = nc.scalar if q % 2 == 0 else nc.sync
                 queue.dma_start(
-                    out=out_2[:, 4 * q : 4 * q + 4, :].bitcast(I32), in_=ys[32 * q : 32 * q + 8, :].bitcast(I32)
+                    out=out_2[:, 4 * q : 4 * q + 4, :].rearrange("h r m -> r h m").bitcast(I32),
+                    in_=ys[32 * q : 32 * q + 4].bitcast(I32),
                 )
 
         split = "p g (u e) -> p g u e"
@@ -407,166 +391,196 @@ def tile_siglip_image_feature_gradient_k4_kernel(
                 op=ALU.mult,
             )
 
+        last = G - 1
+        nc.vector.memset(ws[0][:].rearrange("p g n -> p (g n)").bitcast(I32), 0)
         nc.vector.memset(cb_rows[:].bitcast(I32), 0)
         nc.vector.memset(xs[:].rearrange("p g n -> p (g n)").bitcast(I32), 0)
-        nc.vector.memset(ws[:].rearrange("p g n -> p (g n)").bitcast(I32), 0)
+        nc.vector.memset(ws[1][:].rearrange("p g n -> p (g n)").bitcast(I32), 0)
         make_identity(nc, ident[:])
-        load_u(0, 0, 1)
-        load_u(0, 1, 2)
-        load_u(0, 2, 3)
-        load_u(0, 3, 4)
+        for t in range(4):
+            load_u(0, t, t + 1)
         load_cb()
-        load_scales(ws, w_scales)
         load_w(0, 1)
-        load_z(0)
-        load_x()
-        load_w(1, 2)
+        load_z(0, 0, 1)
+        load_scales(xs, x_scales, slice(0, I))
+        load_x(0)
         load_u(1, 0, 2)
+        load_w(1, 2)
         load_u(1, 2, 4)
-        load_z(1)
+        load_z(0, 1, 2)
+        load_x(1)
+        load_z(1, 0, 1)
         load_u(2, 0, 2)
-        load_z(2)
         load_u(2, 2, 4)
+        load_z(1, 1, 2)
+        load_z(2, 0, 1)
+        load_z(2, 1, 2)
         with nc.allow_non_contiguous_dma(reason="one value of a to each partition"):
             nc.sync.dma_start(out=a_sb[:, :, 0], in_=a.rearrange("(r p) -> p r", p=P))
         nc.sync.dma_start(out=gain_sb[:], in_=gain.partition_broadcast(P))
 
-        every = slice(0, I)
-        lo, hi = slice(0, 256), slice(256, I)
-
-        def r_front(g):
-            for t in range(4):
-                logits(g, t)
-                if t % 2 == 0:
-                    margin(g, t)
-                else:
-                    for half in range(2):
-                        margin(g, t, slice(256 * half, 256 * (half + 1)))
-                        sigmoid(g, t // 2, half)
-
         nc.scalar.activation(out=warm[:], in_=ident[:, 0:1], func=ACT.Sigmoid)
+        def r_front(g, ih):
+            for u in range(2):
+                logits(g, ih, u)
+                margin(g, ih, u)
+                sigmoid(g, ih, u)
+
+        lo, hi = slice(0, P), slice(P, HALF)
         u_turn(0, 0)
         u_copy(0, 0)
         for t in range(1, 4):
             u_sort(0, t, t + 1)
             u_turn(0, t)
             u_copy(0, t)
-        for t in range(3):
+        for t in range(2):
             u_quant(0, t, t + 1)
             b_slice(0, 0, t)
+        z_sort(0, 0, 1)
+        u_quant(0, 2, 3)
         u_quant(0, 3, 4)
-        z_sort(0, False)
         c_turn()
-        for ih in range(2):
-            z_turn(0, ih)
-        b_slice(0, 0, 3)
+        z_turn(0, 0)
+        for t in range(2, 4):
+            b_slice(0, 0, t)
         for s in range(4):
             b_copy(0, 0, s)
         c_negate()
+        u_sort(1, 0, 2)
         c_guard()
         z_scale(0, 0)
         c_invert()
-        z_scale(0, 1)
         b_divide()
-        u_sort(1, 0, 2, nc.gpsimd.tensor_copy)
-        r_front(0)
-        u_sort(1, 2, 4)
-        b_mul(0, 1, 0)
-        b_mul(0, 1, 1)
+        u_sort(1, 2, 4, on_gpsimd, "c_inv")
+        r_front(0, 0)
+        for s in range(2):
+            b_mul(0, 1, s)
+            b_copy(0, 1, s, on_vector)
+        z_sort(0, 1, 2)
+        b_quant(0, 0)
         for t in range(4):
             u_turn(1, t)
             u_copy(1, t)
-        z_sort(1, False)
-        b_copy(0, 1, 0, nc.vector.tensor_copy)
-        b_copy(0, 1, 1, nc.vector.tensor_copy)
-        for ih in range(2):
-            z_turn(1, ih)
-        b_mul(0, 1, 2)
-        b_mul(0, 1, 3)
-        r_make(0, 0, nc.gpsimd, "z_raw1", slice(0, P))
-        z_scale(1, 0)
+        z_turn(0, 1)
+        z_sort(1, 0, 1)
+        z_scale(0, 1)
         u_quant(1, 0, 2)
-        z_scale(1, 1)
+        b_bank(0, 1, 2)
+        b_bank(0, 1, 3)
+        z_sort(1, 1, 2, on_scalar)
+        u_sort(2, 0, 2)
         u_quant(1, 2, 4)
-        b_quant(0, 0)
-        r_make(0, 1, nc.gpsimd, "bb_first")
-        b_copy(0, 1, 2)
-        b_copy(0, 1, 3)
-        u_sort(2, 0, 2, nc.scalar.copy)
-        u_sort(2, 2, 4, nc.scalar.copy)
-        r_front(1)
-        for ih in range(2):
-            z_turn(2, ih)
-            z_scale(2, ih)
-        for t in range(4):
+        u_sort(2, 2, 4, on_gpsimd, "ug1")
+        r_make(0, 0, nc.gpsimd, "rb0")
+        r_front(0, 1)
+        z_turn(1, 0)
+        for t in range(2):
             u_turn(2, t)
             u_copy(2, t)
-        r_quant(0, 1)
-        r_make(0, 0, part=slice(P, 256))
-        r_make(1, 0)
-        r_quant(0, 0)
-        u_quant(2, 0, 2)
-        r_quant(1, 0)
-        u_quant(2, 2, 4)
-        b_quant(0, 1)
-        for s in range(4):
+        z_scale(1, 0)
+        z_sort(2, 0, 1, on_scalar)
+        r_front(1, 0)
+        b_mul(1, 0, 0)
+        b_copy(1, 0, 0, on_vector)
+        z_sort(2, 1, 2, on_scalar)
+        for s in range(1, 4):
             b_bank(1, 0, s)
-        b_quant(1, 0)
-        r_make(1, 1, nc.gpsimd, "bb_first")
+        b_quant(0, 1)
+        u_quant(2, 0, 2)
+        r_make(1, 0, nc.vector, "rb1", lo)
+        r_quant(0, 0)
+        r_make(0, 1, nc.gpsimd, "rb0")
+        z_turn(1, 1)
+        for t in range(2, 4):
+            u_turn(2, t)
+            u_copy(2, t)
+        z_turn(2, 0)
+        z_turn(2, 1)
+        z_scale(1, 1)
+        z_scale(2, 0)
+        r_front(1, 1)
         for s in range(4):
             b_bank(1, 1, s)
-        last = G - 1
-        r_front(last)
+        u_quant(2, 2, 4)
+        b_quant(1, 0)
+        r_make(1, 0, nc.vector, "rb2", hi)
+        r_quant(0, 1)
+        r_make(1, 1, nc.gpsimd, "rb0")
+        r_front(2, 0)
+        z_scale(2, 1)
+        b_mul(2, 0, 0)
+        b_copy(2, 0, 0, on_vector)
+        for s in range(1, 4):
+            b_bank(2, 0, s)
+        r_quant(1, 0, lo)
+        r_quant(1, 0, hi)
         b_quant(1, 1)
         r_quant(1, 1)
-        for s in range(4):
-            b_mul(last, 0, s)
-        r_make(last, 0)
-        for s in range(4):
-            b_copy(last, 0, s, nc.vector.tensor_copy if s == 9 else nc.scalar.copy)
-        r_make(last, 1, part=slice(0, P))
-        r_quant(last, 0)
-        b_quant(last, 0)
-        r_make(last, 1, part=slice(P, 256))
-        for s in range(4):
-            b_bank(last, 1, s)
-        r_quant(last, 1)
-
-        y_mul(0, 0, range(last))
-        y_mul(0, 1, range(last))
-        for r in range(IT):
-            y_mul(0, r, range(last, G) if r < 2 else range(G))
-            y_scale(0, r)
-            if r == 1:
-                b_quant(last, 1)
-            y_round(0, r, True)
-        y_mul(1, 0)
-        y_scale(1, 0)
-        y_mul(1, 1)
-        y_round(1, 0, False)
-        y_turn(0, [0, 1])
-        y_turn(0, [2, 3])
-        y_scale(1, 1)
-        y_copy(0, [0, 1])
-        y_copy(0, [2, 3])
+        r_make(2, 0, nc.gpsimd, "rb0", hi)
+        for u in range(2):
+            logits(2, 1, u)
+            margin(2, 1, u)
+        b_bank(2, 1, 0)
+        for u in range(2):
+            sigmoid(2, 1, u)
+        r_make(2, 0, nc.vector, "rb1", lo)
+        b_quant(2, 0)
+        r_quant(2, 0, lo)
+        r_quant(2, 0, hi)
+        r_make(last, 1, nc.gpsimd, "rb0", lo)
+        b_bank(2, 1, 1)
+        b_mul(2, 1, 2)
+        b_copy(2, 1, 2, on_vector)
+        b_bank(2, 1, 3)
+        early, late = range(last), range(last, G)
+        for r in range(2):
+            y_mul(0, r, early)
+        for r in range(2):
+            y_mul(0, r, late)
+        y_scale(0, 0)
+        y_round(0, 0)
+        b_quant(last, 1)
+        r_quant(last, 1, lo)
+        r_make(last, 1, nc.gpsimd, "rb0", hi)
+        y_scale(0, 1)
+        y_round(0, 1)
+        for h, r in ((1, 0), (1, 1), (0, 2)):
+            y_mul(h, r, early)
+        for r in range(2):
+            y_mul(1, r, late)
+            y_scale(1, r)
+            y_round(1, r)
+        r_quant(last, 1, hi)
+        y_mul(0, 2, late)
+        y_scale(0, 2)
+        y_round(0, 2)
         y_mul(1, 2)
-        y_round(1, 1, True)
-        y_quant(0, [0, 1])
         y_scale(1, 2)
+        y_round(1, 2, on_vector)
+        y_mul(0, 3, early)
+        for h in range(NH):
+            y_turn((h, 0), (h, 1))
+            y_copy(h, [0, 1])
+        y_mul(0, 3, late)
+        y_scale(0, 3)
+        y_round(0, 3)
+        y_quant(0, [0, 1])
+        store_words(0, [0, 1])
         y_mul(1, 3)
-        y_turn(1, [0, 1])
-        y_round(1, 2, True)
-        y_quant(0, [2, 3])
-        store_words(0, [0, 1, 2, 3])
+        y_turn((0, 2), (1, 2))
         y_round_from_bank(1, 3)
-        y_copy(1, [0, 1])
-        y_turn(1, [2])
-        y_turn(1, [3])
-        y_scale(1, 3)
+        y_copy(0, [2])
         y_copy(1, [2])
-        y_copy(1, [3], False)
+        y_turn((0, 3))
+        y_turn((1, 3))
         y_quant(1, [0, 1])
         store_words(1, [0, 1])
-        y_quant(1, [2, 3])
+        y_scale(1, 3)
+        y_copy(0, [3])
+        y_copy(1, [3])
+        y_quant(1, [2])
+        y_quant(0, [2, 3])
+        store_words(0, [2, 3])
+        y_quant(1, [3])
         store_words(1, [2, 3])
         store_scales()

@@ -192,7 +192,7 @@ def tile_siglip_image_feature_gradient_k4_kernel(
             live["l_bank", g, ih, u] = bk
 
         def margin(g, ih, u):
-            mg = work.tile([P, 2, HALF], F32, name="mg", tag="mg", bufs=3, align_bytes=64)
+            mg = work.tile([P, 2, HALF], F32, name="mg", tag="mg", bufs=4, align_bytes=64)
             for e in range(2):
                 t = 2 * u + e
                 nc.vector.scalar_tensor_tensor(
@@ -391,16 +391,46 @@ def tile_siglip_image_feature_gradient_k4_kernel(
                 op=ALU.mult,
             )
 
+        def warm_codes():
+            zero = kept("warm_in", [P, 1024], BF16)
+            live["wc"] = kept("warm_c", [P, 512], U32)
+            live["wsc"] = kept("warm_s", [P, 512], U8)
+            nc.vector.memset(zero[:].bitcast(I32), 0)
+            live["wz"] = zero
+
+        def warm_quant(k):
+            cols = slice(256 * k, 256 * (k + 1))
+            nc.vector.quantize_mx(out=live["wc"][:, cols].bitcast(FP8X4), scales=live["wsc"][:, cols], in_=live["wz"][:])
+
+        def warm_pass(widths):
+            bk = bank("bk_w")
+            for n in widths:
+                nc.tensor.matmul_mx(
+                    out=bk[:, 0:n],
+                    lhsT=live["wc"][:, 0:P].bitcast(FP8X4),
+                    lhsT_scale=live["wsc"][:, 0:P],
+                    rhs=live["wc"][:, 0:n].bitcast(FP8X4),
+                    rhs_scale=live["wsc"][:, 0:n],
+                    start=True,
+                    stop=True,
+                )
+
         last = G - 1
-        nc.vector.memset(ws[0][:].rearrange("p g n -> p (g n)").bitcast(I32), 0)
-        nc.vector.memset(cb_rows[:].bitcast(I32), 0)
-        nc.vector.memset(xs[:].rearrange("p g n -> p (g n)").bitcast(I32), 0)
-        nc.vector.memset(ws[1][:].rearrange("p g n -> p (g n)").bitcast(I32), 0)
         make_identity(nc, ident[:])
+        nc.gpsimd.memset(cb_rows[:].bitcast(I32), 0)
+        warm_codes()
+        nc.vector.memset(ws[0][:].rearrange("p g n -> p (g n)").bitcast(I32), 0)
+        warm_quant(0)
+        warm_quant(1)
         for t in range(4):
             load_u(0, t, t + 1)
         load_cb()
         load_w(0, 1)
+        u_sort(0, 1, 2)
+        nc.vector.memset(xs[:].rearrange("p g n -> p (g n)").bitcast(I32), 0)
+        u_sort(0, 2, 3)
+        nc.vector.memset(ws[1][:].rearrange("p g n -> p (g n)").bitcast(I32), 0)
+        u_sort(0, 3, 4)
         load_z(0, 0, 1)
         load_scales(xs, x_scales, slice(0, I))
         load_x(0)
@@ -427,10 +457,11 @@ def tile_siglip_image_feature_gradient_k4_kernel(
                 sigmoid(g, ih, u)
 
         lo, hi = slice(0, P), slice(P, HALF)
-        u_turn(0, 0)
-        u_copy(0, 0)
-        for t in range(1, 4):
-            u_sort(0, t, t + 1)
+        for t in range(4):
+            if t == 0:
+                warm_pass((256, 256, 512, 256))
+            if t == 2:
+                warm_pass((512, 512))
             u_turn(0, t)
             u_copy(0, t)
         for t in range(2):
@@ -439,25 +470,27 @@ def tile_siglip_image_feature_gradient_k4_kernel(
         z_sort(0, 0, 1)
         u_quant(0, 2, 3)
         u_quant(0, 3, 4)
-        c_turn()
         z_turn(0, 0)
+        c_turn()
         for t in range(2, 4):
             b_slice(0, 0, t)
         for s in range(4):
             b_copy(0, 0, s)
         c_negate()
-        u_sort(1, 0, 2)
         c_guard()
         z_scale(0, 0)
         c_invert()
         b_divide()
-        u_sort(1, 2, 4, on_gpsimd, "c_inv")
+        u_sort(1, 0, 2, on_gpsimd, "c_inv")
         r_front(0, 0)
-        for s in range(2):
-            b_mul(0, 1, s)
-            b_copy(0, 1, s, on_vector)
+        u_sort(1, 2, 4)
+        b_mul(0, 1, 0)
+        b_copy(0, 1, 0, on_vector)
         z_sort(0, 1, 2)
+        b_mul(0, 1, 1)
+        b_copy(0, 1, 1, on_vector)
         b_quant(0, 0)
+        b_bank(0, 1, 2)
         for t in range(4):
             u_turn(1, t)
             u_copy(1, t)
@@ -465,97 +498,96 @@ def tile_siglip_image_feature_gradient_k4_kernel(
         z_sort(1, 0, 1)
         z_scale(0, 1)
         u_quant(1, 0, 2)
-        b_bank(0, 1, 2)
         b_bank(0, 1, 3)
-        z_sort(1, 1, 2, on_scalar)
         u_sort(2, 0, 2)
+        u_sort(2, 2, 4, on_scalar)
         u_quant(1, 2, 4)
-        u_sort(2, 2, 4, on_gpsimd, "ug1")
-        r_make(0, 0, nc.gpsimd, "rb0")
-        r_front(0, 1)
+        r_make(0, 0, nc.gpsimd, "ug1")
+        for u in range(2):
+            logits(0, 1, u)
         z_turn(1, 0)
         for t in range(2):
             u_turn(2, t)
             u_copy(2, t)
         z_scale(1, 0)
-        z_sort(2, 0, 1, on_scalar)
-        r_front(1, 0)
-        b_mul(1, 0, 0)
-        b_copy(1, 0, 0, on_vector)
-        z_sort(2, 1, 2, on_scalar)
-        for s in range(1, 4):
+        for u in range(2):
+            margin(0, 1, u)
+            sigmoid(0, 1, u)
+        for u in range(2):
+            logits(1, 0, u)
+            margin(1, 0, u)
+        z_sort(1, 1, 2)
+        for s in range(3):
             b_bank(1, 0, s)
+        b_mul(1, 0, 3)
         b_quant(0, 1)
-        u_quant(2, 0, 2)
-        r_make(1, 0, nc.vector, "rb1", lo)
         r_quant(0, 0)
-        r_make(0, 1, nc.gpsimd, "rb0")
+        u_quant(2, 0, 2)
+        r_make(0, 1, nc.gpsimd, "ug0")
+        sigmoid(1, 0, 0)
         z_turn(1, 1)
         for t in range(2, 4):
             u_turn(2, t)
             u_copy(2, t)
-        z_turn(2, 0)
-        z_turn(2, 1)
         z_scale(1, 1)
-        z_scale(2, 0)
+        b_copy(1, 0, 3, on_vector)
+        sigmoid(1, 0, 1)
         r_front(1, 1)
         for s in range(4):
             b_bank(1, 1, s)
+        z_sort(2, 0, 1)
+        z_sort(2, 1, 2)
         u_quant(2, 2, 4)
         b_quant(1, 0)
-        r_make(1, 0, nc.vector, "rb2", hi)
         r_quant(0, 1)
-        r_make(1, 1, nc.gpsimd, "rb0")
-        r_front(2, 0)
+        r_make(1, 0, nc.gpsimd, "ug0")
+        z_turn(2, 0)
+        z_turn(2, 1)
+        z_scale(2, 0)
         z_scale(2, 1)
-        b_mul(2, 0, 0)
-        b_copy(2, 0, 0, on_vector)
-        for s in range(1, 4):
+        r_front(2, 0)
+        for s in range(4):
             b_bank(2, 0, s)
-        r_quant(1, 0, lo)
-        r_quant(1, 0, hi)
         b_quant(1, 1)
-        r_quant(1, 1)
-        r_make(2, 0, nc.gpsimd, "rb0", hi)
+        r_make(1, 1, nc.vector, "rb1", lo)
+        r_quant(1, 0)
+        r_make(2, 0, nc.gpsimd, "ug0", hi)
+        r_quant(1, 1, lo)
         for u in range(2):
             logits(2, 1, u)
             margin(2, 1, u)
-        b_bank(2, 1, 0)
-        for u in range(2):
-            sigmoid(2, 1, u)
+        sigmoid(2, 1, 0)
         r_make(2, 0, nc.vector, "rb1", lo)
         b_quant(2, 0)
         r_quant(2, 0, lo)
         r_quant(2, 0, hi)
-        r_make(last, 1, nc.gpsimd, "rb0", lo)
-        b_bank(2, 1, 1)
-        b_mul(2, 1, 2)
-        b_copy(2, 1, 2, on_vector)
-        b_bank(2, 1, 3)
+        r_make(1, 1, nc.vector, "rb1", hi)
+        for s in range(4):
+            b_bank(2, 1, s)
+        sigmoid(2, 1, 1)
+        r_quant(1, 1, hi)
+        b_quant(last, 1)
+        r_make(last, 1, nc.gpsimd, "bb2", lo)
         early, late = range(last), range(last, G)
         for r in range(2):
-            y_mul(0, r, early)
-        for r in range(2):
-            y_mul(0, r, late)
-        y_scale(0, 0)
-        y_round(0, 0)
-        b_quant(last, 1)
+            y_mul(0, r)
+            y_scale(0, r)
+            y_round(0, r)
+        y_mul(1, 0)
+        y_scale(1, 0)
+        y_round(1, 0)
         r_quant(last, 1, lo)
-        r_make(last, 1, nc.gpsimd, "rb0", hi)
-        y_scale(0, 1)
-        y_round(0, 1)
-        for h, r in ((1, 0), (1, 1), (0, 2)):
-            y_mul(h, r, early)
-        for r in range(2):
-            y_mul(1, r, late)
-            y_scale(1, r)
-            y_round(1, r)
+        r_make(last, 1, nc.gpsimd, "bb2", hi)
+        y_mul(1, 1)
+        y_scale(1, 1)
+        y_round(1, 1)
+        for h in range(NH):
+            y_mul(h, 2, early)
+        for h in range(NH):
+            y_mul(h, 2, late)
+            y_scale(h, 2)
         r_quant(last, 1, hi)
-        y_mul(0, 2, late)
-        y_scale(0, 2)
         y_round(0, 2)
-        y_mul(1, 2)
-        y_scale(1, 2)
         y_round(1, 2, on_vector)
         y_mul(0, 3, early)
         for h in range(NH):

@@ -64,7 +64,7 @@ def tile_siglip_image_feature_gradient_k4_kernel(
         bc = [[kept("bc%d_%d" % (g, h), [P, 512], U32) for h in range(NH)] for g in range(G)]
         bs = [[kept("bs%d_%d" % (g, h), [P, 512], U8) for h in range(NH)] for g in range(G)]
         yg = [kept("yg%d" % h, [P, I, 4], BF16) for h in range(NH)]
-        yc = [kept("yc%d" % h, [P, I], U32) for h in range(NH)]
+        yc = kept("yc", [P, NH, I], U32)
         ys = kept("ys", [P, NH, I], U8)
         live = {}
         on_vector, on_scalar, on_gpsimd = nc.vector.tensor_copy, nc.scalar.copy, nc.gpsimd.tensor_copy
@@ -288,24 +288,28 @@ def tile_siglip_image_feature_gradient_k4_kernel(
                     stop=(g == G - 1),
                 )
 
-        def y_scale(h, r):
+        def y_scale(h, r, parts=1):
             yf = work.tile([P, 512], F32, name="yf", tag="yf", bufs=8, align_bytes=64)
-            nc.vector.scalar_tensor_tensor(
-                out=yf[:],
-                in0=live["y_bank", h, r][:],
-                scalar=a_sb[:, r, 0:1],
-                in1=gain_sb[:, 512 * h : 512 * (h + 1)],
-                op0=ALU.mult,
-                op1=ALU.mult,
-            )
+            for k in range(parts):
+                n0, n1 = 512 * k // parts, 512 * (k + 1) // parts
+                nc.vector.scalar_tensor_tensor(
+                    out=yf[:, n0:n1],
+                    in0=live["y_bank", h, r][:, n0:n1],
+                    scalar=a_sb[:, r, 0:1],
+                    in1=gain_sb[:, 512 * h + n0 : 512 * h + n1],
+                    op0=ALU.mult,
+                    op1=ALU.mult,
+                )
             nc.sync.dma_start(out=out_0[P * r : P * (r + 1), 512 * h : 512 * (h + 1)], in_=yf[:])
             live["yf", h, r] = yf
 
-        def y_round(h, r, copy=nc.scalar.copy):
+        def y_round(h, r, copy=nc.scalar.copy, parts=1):
             yb = work.tile([P, 512], BF16, name="yb", tag="yb", bufs=8, align_bytes=64)
             dst = yb[:].rearrange("q (u x p e) -> q x u p e", u=2, p=4, e=2)
             src = live["yf", h, r][:].rearrange("q (x p u e) -> q x u p e", p=4, u=2, e=2)
-            copy(out=dst, in_=src)
+            for k in range(parts):
+                x = slice(32 * k // parts, 32 * (k + 1) // parts)
+                copy(out=dst[:, x], in_=src[:, x])
             live["yb", h, r] = yb
 
         def y_round_from_bank(h, r):
@@ -343,15 +347,15 @@ def tile_siglip_image_feature_gradient_k4_kernel(
         def y_quant(h, rows):
             cols = slice(P * rows[0], P * (rows[0] + len(rows)))
             nc.vector.quantize_mx(
-                out=yc[h][:, cols].bitcast(FP8X4),
+                out=yc[:, h, cols].bitcast(FP8X4),
                 scales=ys[:, h, cols],
                 in_=yg[h][:, cols, :].rearrange("p i t -> p (i t)"),
             )
 
-        def store_words(h, rows):
+        def store_words(rows):
             cols = slice(P * rows[0], P * (rows[0] + len(rows)))
-            dst = out_1[h].rearrange("p m t -> p (m t)").bitcast(I32)
-            nc.sync.dma_start(out=dst[:, cols], in_=yc[h][:, cols].bitcast(I32))
+            dst = out_1.rearrange("h p m t -> p h (m t)").bitcast(I32)
+            nc.sync.dma_start(out=dst[:, :, cols], in_=yc[:, :, cols].bitcast(I32))
 
         def store_scales():
             for q in range(4):
@@ -392,14 +396,14 @@ def tile_siglip_image_feature_gradient_k4_kernel(
             )
 
         def warm_codes():
-            zero = kept("warm_in", [P, 1024], BF16)
+            zero = kept("warm_in", [P, 512], BF16)
             live["wc"] = kept("warm_c", [P, 512], U32)
             live["wsc"] = kept("warm_s", [P, 512], U8)
             nc.vector.memset(zero[:].bitcast(I32), 0)
             live["wz"] = zero
 
         def warm_quant(k):
-            cols = slice(256 * k, 256 * (k + 1))
+            cols = slice(P * k, P * (k + 1))
             nc.vector.quantize_mx(out=live["wc"][:, cols].bitcast(FP8X4), scales=live["wsc"][:, cols], in_=live["wz"][:])
 
         def warm_pass(widths):
@@ -417,11 +421,13 @@ def tile_siglip_image_feature_gradient_k4_kernel(
 
         last = G - 1
         make_identity(nc, ident[:])
-        nc.gpsimd.memset(cb_rows[:].bitcast(I32), 0)
         warm_codes()
         nc.vector.memset(ws[0][:].rearrange("p g n -> p (g n)").bitcast(I32), 0)
         warm_quant(0)
         warm_quant(1)
+        nc.vector.memset(cb_rows[:].bitcast(I32), 0)
+        warm_quant(2)
+        warm_quant(3)
         for t in range(4):
             load_u(0, t, t + 1)
         load_cb()
@@ -541,78 +547,79 @@ def tile_siglip_image_feature_gradient_k4_kernel(
         b_quant(1, 0)
         r_quant(0, 1)
         r_make(1, 0, nc.gpsimd, "ug0")
+        r_make(1, 1, nc.gpsimd, "rb2", lo)
         z_turn(2, 0)
         z_turn(2, 1)
         z_scale(2, 0)
         z_scale(2, 1)
         r_front(2, 0)
-        for s in range(4):
-            b_bank(2, 0, s)
-        b_quant(1, 1)
-        r_make(1, 1, nc.vector, "rb1", lo)
-        r_quant(1, 0)
-        r_make(2, 0, nc.gpsimd, "ug0", hi)
-        r_quant(1, 1, lo)
+        b_mul(2, 0, 0)
+        b_copy(2, 0, 0, on_vector)
+        b_bank(2, 0, 1)
         for u in range(2):
             logits(2, 1, u)
             margin(2, 1, u)
         sigmoid(2, 1, 0)
-        r_make(2, 0, nc.vector, "rb1", lo)
-        b_quant(2, 0)
-        r_quant(2, 0, lo)
-        r_quant(2, 0, hi)
-        r_make(1, 1, nc.vector, "rb1", hi)
-        for s in range(4):
-            b_bank(2, 1, s)
+        for s in range(2, 4):
+            b_bank(2, 0, s)
         sigmoid(2, 1, 1)
-        r_quant(1, 1, hi)
+        r_make(2, 0, nc.vector, "rb1")
+        r_quant(1, 0)
+        r_quant(2, 0)
+        b_quant(2, 0)
+        r_quant(1, 1, lo)
+        r_make(2, 1, nc.vector, "rb1", lo)
+        b_quant(1, 1)
+        for s in range(3):
+            b_bank(2, 1, s)
+        b_mul(2, 1, 3)
+        b_copy(2, 1, 3, on_vector)
+        r_quant(2, 1, lo)
         b_quant(last, 1)
-        r_make(last, 1, nc.gpsimd, "bb2", lo)
-        early, late = range(last), range(last, G)
+        r_make(1, 1, nc.gpsimd, "bb2", hi)
+        r_make(2, 1, nc.gpsimd, "rb2", hi)
         for r in range(2):
             y_mul(0, r)
             y_scale(0, r)
             y_round(0, r)
-        y_mul(1, 0)
-        y_scale(1, 0)
-        y_round(1, 0)
-        r_quant(last, 1, lo)
-        r_make(last, 1, nc.gpsimd, "bb2", hi)
-        y_mul(1, 1)
-        y_scale(1, 1)
-        y_round(1, 1)
-        for h in range(NH):
-            y_mul(h, 2, early)
-        for h in range(NH):
-            y_mul(h, 2, late)
-            y_scale(h, 2)
-        r_quant(last, 1, hi)
+        for r in range(2):
+            y_mul(1, r, range(last))
+        for r in range(2):
+            y_mul(1, r, range(last, G))
+            y_scale(1, r)
+            y_round(1, r)
+        y_mul(0, 2)
+        y_scale(0, 2)
         y_round(0, 2)
-        y_round(1, 2, on_vector)
-        y_mul(0, 3, early)
+        y_mul(1, 2)
+        r_quant(1, 1, hi)
+        r_quant(last, 1, hi)
+        y_scale(1, 2)
         for h in range(NH):
             y_turn((h, 0), (h, 1))
             y_copy(h, [0, 1])
-        y_mul(0, 3, late)
-        y_scale(0, 3)
-        y_round(0, 3)
+        y_round(1, 2)
         y_quant(0, [0, 1])
-        store_words(0, [0, 1])
+        y_mul(0, 3)
+        y_scale(0, 3, 2)
+        y_round(0, 3, on_scalar, 2)
+        y_quant(1, [0, 1])
+        store_words([0, 1])
         y_mul(1, 3)
-        y_turn((0, 2), (1, 2))
+        y_turn((0, 2))
+        y_turn((1, 2))
         y_round_from_bank(1, 3)
         y_copy(0, [2])
         y_copy(1, [2])
         y_turn((0, 3))
         y_turn((1, 3))
-        y_quant(1, [0, 1])
-        store_words(1, [0, 1])
         y_scale(1, 3)
         y_copy(0, [3])
         y_copy(1, [3])
+        y_quant(0, [2])
         y_quant(1, [2])
-        y_quant(0, [2, 3])
-        store_words(0, [2, 3])
+        store_words([2])
+        y_quant(0, [3])
         y_quant(1, [3])
-        store_words(1, [2, 3])
+        store_words([3])
         store_scales()

@@ -553,16 +553,13 @@ def tile_siglip_image_feature_gradient_k4_kernel(
         z_scale(2, 0)
         z_scale(2, 1)
         r_front(2, 0)
+        r_front(2, 1)
         b_mul(2, 0, 0)
         b_copy(2, 0, 0, on_vector)
-        b_bank(2, 0, 1)
-        for u in range(2):
-            logits(2, 1, u)
-            margin(2, 1, u)
-        sigmoid(2, 1, 0)
+        b_mul(2, 0, 1)
+        b_copy(2, 0, 1, on_vector)
         for s in range(2, 4):
             b_bank(2, 0, s)
-        sigmoid(2, 1, 1)
         r_make(2, 0, nc.vector, "rb1")
         r_quant(1, 0)
         r_quant(2, 0)
@@ -570,11 +567,9 @@ def tile_siglip_image_feature_gradient_k4_kernel(
         r_quant(1, 1, lo)
         r_make(2, 1, nc.vector, "rb1", lo)
         b_quant(1, 1)
-        for s in range(3):
-            b_bank(2, 1, s)
-        b_mul(2, 1, 3)
-        b_copy(2, 1, 3, on_vector)
         r_quant(2, 1, lo)
+        for s in range(4):
+            b_bank(2, 1, s)
         b_quant(last, 1)
         r_make(1, 1, nc.gpsimd, "bb2", hi)
         r_make(2, 1, nc.gpsimd, "rb2", hi)
@@ -583,9 +578,7 @@ def tile_siglip_image_feature_gradient_k4_kernel(
             y_scale(0, r)
             y_round(0, r)
         for r in range(2):
-            y_mul(1, r, range(last))
-        for r in range(2):
-            y_mul(1, r, range(last, G))
+            y_mul(1, r)
             y_scale(1, r)
             y_round(1, r)
         y_mul(0, 2)
@@ -595,10 +588,10 @@ def tile_siglip_image_feature_gradient_k4_kernel(
         r_quant(1, 1, hi)
         r_quant(last, 1, hi)
         y_scale(1, 2)
+        y_round(1, 2, on_vector)
         for h in range(NH):
             y_turn((h, 0), (h, 1))
             y_copy(h, [0, 1])
-        y_round(1, 2)
         y_quant(0, [0, 1])
         y_mul(0, 3)
         y_scale(0, 3, 2)

@@ -444,9 +444,9 @@ def tile_siglip_image_feature_gradient_k4_kernel(
         load_w(1, 2)
         load_u(1, 2, 4)
         load_z(0, 1, 2)
+        load_u(2, 0, 2)
         load_x(1)
         load_z(1, 0, 1)
-        load_u(2, 0, 2)
         load_u(2, 2, 4)
         load_z(1, 1, 2)
         load_z(2, 0, 1)
@@ -490,22 +490,21 @@ def tile_siglip_image_feature_gradient_k4_kernel(
         u_sort(1, 0, 2, on_gpsimd, "c_inv")
         r_front(0, 0)
         u_sort(1, 2, 4)
-        b_mul(0, 1, 0)
-        b_copy(0, 1, 0, on_vector)
         z_sort(0, 1, 2)
-        b_mul(0, 1, 1)
-        b_copy(0, 1, 1, on_vector)
         b_quant(0, 0)
+        u_sort(2, 0, 2, on_gpsimd, "bb0")
+        for s in range(2):
+            b_mul(0, 1, s)
+            b_copy(0, 1, s, on_vector)
         b_bank(0, 1, 2)
         for t in range(4):
             u_turn(1, t)
             u_copy(1, t)
         z_turn(0, 1)
-        z_sort(1, 0, 1)
         z_scale(0, 1)
+        z_sort(1, 0, 1)
         u_quant(1, 0, 2)
         b_bank(0, 1, 3)
-        u_sort(2, 0, 2)
         u_sort(2, 2, 4, on_scalar)
         u_quant(1, 2, 4)
         r_make(0, 0, nc.gpsimd, "ug1")
@@ -523,34 +522,34 @@ def tile_siglip_image_feature_gradient_k4_kernel(
             logits(1, 0, u)
             margin(1, 0, u)
         z_sort(1, 1, 2)
+        z_sort(2, 0, 1)
+        z_sort(2, 1, 2)
         for s in range(3):
             b_bank(1, 0, s)
         b_mul(1, 0, 3)
         b_quant(0, 1)
-        r_quant(0, 0)
         u_quant(2, 0, 2)
         r_make(0, 1, nc.gpsimd, "ug0")
+        r_quant(0, 0)
         sigmoid(1, 0, 0)
         z_turn(1, 1)
         for t in range(2, 4):
             u_turn(2, t)
             u_copy(2, t)
-        z_scale(1, 1)
+        z_turn(2, 0)
+        z_turn(2, 1)
         b_copy(1, 0, 3, on_vector)
+        z_scale(1, 1)
+        z_scale(2, 0)
         sigmoid(1, 0, 1)
         r_front(1, 1)
         for s in range(4):
             b_bank(1, 1, s)
-        z_sort(2, 0, 1)
-        z_sort(2, 1, 2)
         u_quant(2, 2, 4)
-        b_quant(1, 0)
         r_quant(0, 1)
         r_make(1, 0, nc.gpsimd, "ug0")
+        b_quant(1, 0)
         r_make(1, 1, nc.gpsimd, "rb2", lo)
-        z_turn(2, 0)
-        z_turn(2, 1)
-        z_scale(2, 0)
         z_scale(2, 1)
         r_front(2, 0)
         r_front(2, 1)
@@ -567,11 +566,11 @@ def tile_siglip_image_feature_gradient_k4_kernel(
         r_quant(1, 1, lo)
         r_make(2, 1, nc.vector, "rb1", lo)
         b_quant(1, 1)
-        r_quant(2, 1, lo)
         for s in range(4):
             b_bank(2, 1, s)
         b_quant(last, 1)
         r_make(1, 1, nc.gpsimd, "bb2", hi)
+        r_quant(2, 1, lo)
         r_make(2, 1, nc.gpsimd, "rb2", hi)
         for r in range(2):
             y_mul(0, r)

@@ -35,7 +35,7 @@ def tile_siglip_image_feature_gradient_k4_kernel(
         ctx.enter_context(tc.manual_schedule())
 
         def kept(name, shape, dtype):
-            return keep.tile(shape, dtype, name=name, align_bytes=64)
+            return keep.tile(shape, dtype, name=name, align_bytes=256)
 
         def bank(name):
             return psum.tile([P, 512], F32, name=name, tag="bank")
@@ -111,7 +111,7 @@ def tile_siglip_image_feature_gradient_k4_kernel(
             if slot:
                 srt = kept(slot, [P, n * DG, 2, P], F32)
             else:
-                srt = work.tile([P, n * DG, 2, P], F32, name="srt", tag="srt", bufs=3, align_bytes=64)
+                srt = work.tile([P, n * DG, 2, P], F32, name="srt", tag="srt", bufs=3, align_bytes=256)
             words = u_pack[g, t0][:, 0:n, :].rearrange("q t k -> q (t k)").bitcast(F32)
             copy(
                 out=srt[:].rearrange("q s u (x i) -> q s x u i", i=4),
@@ -150,7 +150,7 @@ def tile_siglip_image_feature_gradient_k4_kernel(
 
         def z_sort(g, i0, i1, copy=on_vector):
             n = 2 * (i1 - i0)
-            zs = work.tile([P, n, 2, P], F32, name="zs", tag="zs", bufs=4, align_bytes=64)
+            zs = work.tile([P, n, 2, P], F32, name="zs", tag="zs", bufs=4, align_bytes=256)
             words = z_raw[g, i0][:].rearrange("q r j -> q (r j)").bitcast(F32)
             copy(
                 out=zs[:].rearrange("q r u (x i) -> q r x u i", i=4),
@@ -192,7 +192,7 @@ def tile_siglip_image_feature_gradient_k4_kernel(
             live["l_bank", g, ih, u] = bk
 
         def margin(g, ih, u):
-            mg = work.tile([P, 2, HALF], F32, name="mg", tag="mg", bufs=4, align_bytes=64)
+            mg = work.tile([P, 2, HALF], F32, name="mg", tag="mg", bufs=4, align_bytes=256)
             for e in range(2):
                 t = 2 * u + e
                 nc.vector.scalar_tensor_tensor(
@@ -207,7 +207,7 @@ def tile_siglip_image_feature_gradient_k4_kernel(
 
         def sigmoid(g, ih, u):
             if u == 0:
-                live["sg", g, ih] = work.tile([P, 2, HALF, 2], F32, name="sg", tag="sg", bufs=4, align_bytes=64)
+                live["sg", g, ih] = work.tile([P, 2, HALF, 2], F32, name="sg", tag="sg", bufs=4, align_bytes=256)
             nc.scalar.activation(
                 out=live["sg", g, ih][:, u],
                 in_=live["mg", g, ih, u][:].rearrange("p e i -> p i e"),
@@ -289,7 +289,7 @@ def tile_siglip_image_feature_gradient_k4_kernel(
                 )
 
         def y_scale(h, r, parts=1):
-            yf = work.tile([P, 512], F32, name="yf", tag="yf", bufs=8, align_bytes=64)
+            yf = work.tile([P, 512], F32, name="yf", tag="yf", bufs=8, align_bytes=256)
             for k in range(parts):
                 n0, n1 = 512 * k // parts, 512 * (k + 1) // parts
                 nc.vector.scalar_tensor_tensor(
@@ -304,7 +304,7 @@ def tile_siglip_image_feature_gradient_k4_kernel(
             live["yf", h, r] = yf
 
         def y_round(h, r, copy=nc.scalar.copy, parts=1):
-            yb = work.tile([P, 512], BF16, name="yb", tag="yb", bufs=8, align_bytes=64)
+            yb = work.tile([P, 512], BF16, name="yb", tag="yb", bufs=8, align_bytes=256)
             dst = yb[:].rearrange("q (u x p e) -> q x u p e", u=2, p=4, e=2)
             src = live["yf", h, r][:].rearrange("q (x p u e) -> q x u p e", p=4, u=2, e=2)
             for k in range(parts):
@@ -313,7 +313,7 @@ def tile_siglip_image_feature_gradient_k4_kernel(
             live["yb", h, r] = yb
 
         def y_round_from_bank(h, r):
-            yb = work.tile([P, 512], BF16, name="yb", tag="yb", bufs=8, align_bytes=64)
+            yb = work.tile([P, 512], BF16, name="yb", tag="yb", bufs=8, align_bytes=256)
             src = live["y_bank", h, r][:].rearrange("q (p u e) -> q u p e", u=2, e=2)
             gn = gain_sb[:, 512 * h : 512 * (h + 1)].rearrange("q (p u e) -> q u p e", u=2, e=2)
             for u in range(2):
@@ -478,9 +478,10 @@ def tile_siglip_image_feature_gradient_k4_kernel(
         u_quant(0, 3, 4)
         z_turn(0, 0)
         c_turn()
-        for t in range(2, 4):
-            b_slice(0, 0, t)
         for s in range(4):
+            for t in range(2, 4):
+                for d in range(DG):
+                    b_pass(live["b_bank", 0, 0, s], 0, 0, s, t, d)
             b_copy(0, 0, s)
         c_negate()
         c_guard()
@@ -489,14 +490,14 @@ def tile_siglip_image_feature_gradient_k4_kernel(
         b_divide()
         u_sort(1, 0, 2, on_gpsimd, "c_inv")
         r_front(0, 0)
+        b_quant(0, 0)
         u_sort(1, 2, 4)
         z_sort(0, 1, 2)
-        b_quant(0, 0)
-        u_sort(2, 0, 2, on_gpsimd, "bb0")
-        for s in range(2):
+        u_sort(2, 0, 2, on_gpsimd, "z_raw0_1")
+        b_bank(0, 1, 0)
+        for s in range(1, 3):
             b_mul(0, 1, s)
             b_copy(0, 1, s, on_vector)
-        b_bank(0, 1, 2)
         for t in range(4):
             u_turn(1, t)
             u_copy(1, t)

@@ -67,7 +67,7 @@ def tile_siglip_image_feature_gradient_k4_kernel(
         yc = kept("yc", [P, NH, I], U32)
         ys = kept("ys", [P, NH, I], U8)
         live = {}
-        on_vector, on_scalar, on_gpsimd = nc.vector.tensor_copy, nc.scalar.copy, nc.gpsimd.tensor_copy
+        on_vector, on_scalar = nc.vector.tensor_copy, nc.scalar.copy
 
         def load_u(g, t0, t1):
             rows = U[512 * g : 512 * (g + 1), :].rearrange("(m t) k -> m t k", t=4)
@@ -77,19 +77,16 @@ def tile_siglip_image_feature_gradient_k4_kernel(
             for t in range(t0, t1):
                 u_raw[g, t] = raw[:, t - t0, :]
 
-        def load_w(h0, h1):
-            load_scales(ws[h0], w_scales, slice(512 * h0, 512 * h1))
-            src = w_words[:, :, N * h0 : N * h1].rearrange("g p n -> p g n")
-            raw = kept("ww%d" % h0, [P, DG, N * (h1 - h0)], U8)
-            nc.sync.dma_start(out=raw[:].bitcast(I32), in_=src.bitcast(I32))
-            for h in range(h0, h1):
-                ww[h] = raw[:, :, N * (h - h0) : N * (h - h0 + 1)]
+        def load_w(h):
+            load_scales(ws[h], w_scales, slice(512 * h, 512 * (h + 1)))
+            src = w_words[:, :, N * h : N * (h + 1)].rearrange("g p n -> p g n")
+            ww[h] = kept("ww%d" % h, [P, DG, N], U8)
+            nc.sync.dma_start(out=ww[h][:].bitcast(I32), in_=src.bitcast(I32))
 
-        def load_z(g, i0, i1):
-            raw = kept("z_raw%d_%d" % (g, i0), [P, 2 * (i1 - i0), 512], BF16)
-            src = Z[HALF * i0 : HALF * i1, 512 * g : 512 * (g + 1)]
-            nc.sync.dma_start(out=raw[:], in_=src.rearrange("(r p) j -> p r j", p=P))
-            z_raw[g, i0] = raw
+        def load_z(g, ih):
+            z_raw[g, ih] = kept("z_raw%d_%d" % (g, ih), [P, 2, 512], BF16)
+            src = Z[HALF * ih : HALF * (ih + 1), 512 * g : 512 * (g + 1)]
+            nc.sync.dma_start(out=z_raw[g, ih][:], in_=src.rearrange("(r p) j -> p r j", p=P))
 
         def load_scales(plane, src, cols):
             for q in range(4):
@@ -106,12 +103,9 @@ def tile_siglip_image_feature_gradient_k4_kernel(
             nc.gpsimd.dma_start(out=cb_rows[0:G, :], in_=c.rearrange("(g j) -> g j", g=G))
             nc.gpsimd.dma_start(out=cb_rows[G : 2 * G, :], in_=b.rearrange("(g j) -> g j", g=G))
 
-        def u_sort(g, t0, t1, copy=on_vector, slot=None):
+        def u_sort(g, t0, t1, copy=on_vector):
             n = t1 - t0
-            if slot:
-                srt = kept(slot, [P, n * DG, 2, P], F32)
-            else:
-                srt = work.tile([P, n * DG, 2, P], F32, name="srt", tag="srt", bufs=3, align_bytes=256)
+            srt = work.tile([P, n * DG, 2, P], F32, name="srt", tag="srt", bufs=3, align_bytes=256)
             words = u_pack[g, t0][:, 0:n, :].rearrange("q t k -> q (t k)").bitcast(F32)
             copy(
                 out=srt[:].rearrange("q s u (x i) -> q s x u i", i=4),
@@ -133,10 +127,10 @@ def tile_siglip_image_feature_gradient_k4_kernel(
                     nc.tensor.transpose(bk[:, P * s : P * (s + 1)], src, ident[:])
             live["u_bank", g, t] = bk
 
-        def u_copy(g, t, copy=nc.scalar.copy):
+        def u_copy(g, t):
             if t % 2 == 0:
                 live["ug", g, t // 2] = kept("ug%d" % (t // 2), [P, 2, D], BF16)
-            copy(
+            on_scalar(
                 out=live["ug", g, t // 2][:, t % 2, :].bitcast(F32).rearrange("p (d m u) -> p d m u", d=DG, u=2),
                 in_=live["u_bank", g, t][:].rearrange("p (d u m) -> p d m u", d=DG, u=2),
             )
@@ -148,16 +142,14 @@ def tile_siglip_image_feature_gradient_k4_kernel(
                 in_=live["ug", g, t0 // 2][:, t0 % 2 : t0 % 2 + t1 - t0, :].rearrange("p t k -> p (t k)"),
             )
 
-        def z_sort(g, i0, i1, copy=on_vector):
-            n = 2 * (i1 - i0)
-            zs = work.tile([P, n, 2, P], F32, name="zs", tag="zs", bufs=4, align_bytes=256)
-            words = z_raw[g, i0][:].rearrange("q r j -> q (r j)").bitcast(F32)
-            copy(
+        def z_sort(g, ih):
+            zs = work.tile([P, 2, 2, P], F32, name="zs", tag="zs", bufs=4, align_bytes=256)
+            words = z_raw[g, ih][:].rearrange("q r j -> q (r j)").bitcast(F32)
+            on_vector(
                 out=zs[:].rearrange("q r u (x i) -> q r x u i", i=4),
-                in_=words.rearrange("q (r x i u) -> q r x u i", r=n, i=4, u=2),
+                in_=words.rearrange("q (r x i u) -> q r x u i", r=2, i=4, u=2),
             )
-            for ih in range(i0, i1):
-                live["zs", g, ih] = zs[:, 2 * (ih - i0) : 2 * (ih - i0 + 1)]
+            live["zs", g, ih] = zs
 
         def z_turn(g, ih):
             bk = bank("bk_z")
@@ -171,7 +163,7 @@ def tile_siglip_image_feature_gradient_k4_kernel(
             nc.vector.tensor_tensor(
                 out=zc[g][ih][:],
                 in0=live["z_bank", g, ih][:].bitcast(BF16).rearrange("p (u i e) -> p u i e", u=2, e=2),
-                in1=c_neg[:, g, :].rearrange("p (u e) -> p u e", u=2).unsqueeze(2).broadcast_to([P, 2, 256, 2]),
+                in1=c_neg[:, g, :].rearrange("p (u e) -> p u e", u=2).unsqueeze(2).broadcast_to([P, 2, HALF, 2]),
                 op=ALU.mult,
             )
 
@@ -214,6 +206,12 @@ def tile_siglip_image_feature_gradient_k4_kernel(
                 func=ACT.Sigmoid,
             )
 
+        def r_front(g, ih):
+            for u in range(2):
+                logits(g, ih, u)
+                margin(g, ih, u)
+                sigmoid(g, ih, u)
+
         def r_make(g, ih, engine, slot, part=slice(0, HALF)):
             rb = kept(slot, [P, part.stop - part.start, 4], BF16)
             engine.tensor_tensor(
@@ -232,40 +230,30 @@ def tile_siglip_image_feature_gradient_k4_kernel(
                 in_=live["rb", g, ih, part.start][:].rearrange("p i t -> p (i t)"),
             )
 
-        def b_pass(bk, g, h, s, t, d):
-            nc.tensor.matmul_mx(
-                out=bk[:, P * t : P * (t + 1)],
-                lhsT=uc[g][:, t, P * d : P * (d + 1)].bitcast(FP8X4),
-                lhsT_scale=us[g][:, t, P * d : P * (d + 1)],
-                rhs=ww[h][:, d, 256 * s : 256 * (s + 1)].bitcast(FP4X4),
-                rhs_scale=ws[h][:, d, P * s : P * (s + 1)],
-                start=(d == 0),
-                stop=(d == DG - 1),
-            )
-
-        def b_mul(g, h, s):
-            bk = bank("bk_b")
-            for t in range(4):
+        def b_mul(g, h, s, slots=range(4)):
+            if slots[0] == 0:
+                live["b_bank", g, h, s] = bank("bk_b")
+            for t in slots:
                 for d in range(DG):
-                    b_pass(bk, g, h, s, t, d)
-            live["b_bank", g, h, s] = bk
+                    nc.tensor.matmul_mx(
+                        out=live["b_bank", g, h, s][:, P * t : P * (t + 1)],
+                        lhsT=uc[g][:, t, P * d : P * (d + 1)].bitcast(FP8X4),
+                        lhsT_scale=us[g][:, t, P * d : P * (d + 1)],
+                        rhs=ww[h][:, d, 256 * s : 256 * (s + 1)].bitcast(FP4X4),
+                        rhs_scale=ws[h][:, d, P * s : P * (s + 1)],
+                        start=(d == 0),
+                        stop=(d == DG - 1),
+                    )
 
-        def b_slice(g, h, t):
-            for s in range(4):
-                if t == 0:
-                    live["b_bank", g, h, s] = bank("bk_b")
-                for d in range(DG):
-                    b_pass(live["b_bank", g, h, s], g, h, s, t, d)
-
-        def b_copy(g, h, s, copy=nc.scalar.copy):
+        def b_copy(g, h, s, copy=on_scalar):
             if ("bb", g, h) not in live:
                 live["bb", g, h] = kept("bb%d" % ((2 * g + h) % 3), [P, 512, 4], BF16)
             dst = live["bb", g, h][:, P * s : P * (s + 1), :]
             copy(out=dst, in_=live["b_bank", g, h, s][:].rearrange("p (t n) -> p n t", t=4))
 
-        def b_bank(g, h, s):
+        def b_bank(g, h, s, copy=on_scalar):
             b_mul(g, h, s)
-            b_copy(g, h, s)
+            b_copy(g, h, s, copy)
 
         def b_quant(g, h):
             nc.vector.quantize_mx(
@@ -274,12 +262,11 @@ def tile_siglip_image_feature_gradient_k4_kernel(
                 in_=live["bb", g, h][:].rearrange("p n t -> p (n t)"),
             )
 
-        def y_mul(h, r, groups=range(G)):
-            if groups[0] == 0:
-                live["y_bank", h, r] = bank("bk_y")
-            for g in groups:
+        def y_mul(h, r):
+            bk = bank("bk_y")
+            for g in range(G):
                 nc.tensor.matmul_mx(
-                    out=live["y_bank", h, r][:],
+                    out=bk[:],
                     lhsT=rc[g][:, P * r : P * (r + 1)].bitcast(FP8X4),
                     lhsT_scale=rs[g][:, P * r : P * (r + 1)],
                     rhs=bc[g][h][:].bitcast(FP8X4),
@@ -287,6 +274,7 @@ def tile_siglip_image_feature_gradient_k4_kernel(
                     start=(g == 0),
                     stop=(g == G - 1),
                 )
+            live["y_bank", h, r] = bk
 
         def y_scale(h, r, parts=1):
             yf = work.tile([P, 512], F32, name="yf", tag="yf", bufs=8, align_bytes=256)
@@ -303,7 +291,7 @@ def tile_siglip_image_feature_gradient_k4_kernel(
             nc.sync.dma_start(out=out_0[P * r : P * (r + 1), 512 * h : 512 * (h + 1)], in_=yf[:])
             live["yf", h, r] = yf
 
-        def y_round(h, r, copy=nc.scalar.copy, parts=1):
+        def y_round(h, r, copy=on_scalar, parts=1):
             yb = work.tile([P, 512], BF16, name="yb", tag="yb", bufs=8, align_bytes=256)
             dst = yb[:].rearrange("q (u x p e) -> q x u p e", u=2, p=4, e=2)
             src = live["yf", h, r][:].rearrange("q (x p u e) -> q x u p e", p=4, u=2, e=2)
@@ -311,6 +299,11 @@ def tile_siglip_image_feature_gradient_k4_kernel(
                 x = slice(32 * k // parts, 32 * (k + 1) // parts)
                 copy(out=dst[:, x], in_=src[:, x])
             live["yb", h, r] = yb
+
+        def y_tile(h, r, parts=1):
+            y_mul(h, r)
+            y_scale(h, r, parts)
+            y_round(h, r, on_scalar, parts)
 
         def y_round_from_bank(h, r):
             yb = work.tile([P, 512], BF16, name="yb", tag="yb", bufs=8, align_bytes=256)
@@ -336,10 +329,10 @@ def tile_siglip_image_feature_gradient_k4_kernel(
                     nc.tensor.transpose(bk[:, col : col + P], words[:, P * u : P * (u + 1)], ident[:])
                 live["t_bank", h, r] = bk[:, 2 * P * k :]
 
-        def y_copy(h, rows, copy=on_scalar):
+        def y_copy(h, rows):
             n = len(rows)
             dst = yg[h][:, P * rows[0] : P * (rows[0] + n), :].rearrange("p i t -> p (i t)").bitcast(F32)
-            copy(
+            on_scalar(
                 out=dst.rearrange("p (k i u) -> p k i u", k=n, u=2),
                 in_=live["t_bank", h, rows[0]][:, 0 : 256 * n].rearrange("p (k u i) -> p k i u", k=n, u=2),
             )
@@ -395,141 +388,136 @@ def tile_siglip_image_feature_gradient_k4_kernel(
                 op=ALU.mult,
             )
 
-        def warm_codes():
-            zero = kept("warm_in", [P, 512], BF16)
-            live["wc"] = kept("warm_c", [P, 512], U32)
-            live["wsc"] = kept("warm_s", [P, 512], U8)
-            nc.vector.memset(zero[:].bitcast(I32), 0)
-            live["wz"] = zero
-
         def warm_quant(k):
             cols = slice(P * k, P * (k + 1))
-            nc.vector.quantize_mx(out=live["wc"][:, cols].bitcast(FP8X4), scales=live["wsc"][:, cols], in_=live["wz"][:])
+            nc.vector.quantize_mx(out=warm_c[:, cols].bitcast(FP8X4), scales=warm_s[:, cols], in_=warm_in[:])
 
-        def warm_pass(widths):
+        def warm_pass(*widths):
             bk = bank("bk_w")
             for n in widths:
                 nc.tensor.matmul_mx(
                     out=bk[:, 0:n],
-                    lhsT=live["wc"][:, 0:P].bitcast(FP8X4),
-                    lhsT_scale=live["wsc"][:, 0:P],
-                    rhs=live["wc"][:, 0:n].bitcast(FP8X4),
-                    rhs_scale=live["wsc"][:, 0:n],
+                    lhsT=warm_c[:, 0:P].bitcast(FP8X4),
+                    lhsT_scale=warm_s[:, 0:P],
+                    rhs=warm_c[:, 0:n].bitcast(FP8X4),
+                    rhs_scale=warm_s[:, 0:n],
                     start=True,
                     stop=True,
                 )
 
-        last = G - 1
+        def clear(tile_ap):
+            nc.vector.memset(tile_ap.bitcast(I32), 0)
+
+        lo, hi = slice(0, P), slice(P, HALF)
+
         make_identity(nc, ident[:])
-        warm_codes()
-        nc.vector.memset(ws[0][:].rearrange("p g n -> p (g n)").bitcast(I32), 0)
+        warm_in = kept("warm_in", [P, 512], BF16)
+        warm_c = kept("warm_c", [P, 512], U32)
+        warm_s = kept("warm_s", [P, 512], U8)
+        clear(warm_in[:])
+        clear(ws[0][:].rearrange("p g n -> p (g n)"))
         warm_quant(0)
         warm_quant(1)
-        nc.vector.memset(cb_rows[:].bitcast(I32), 0)
+        clear(cb_rows[:])
         warm_quant(2)
         warm_quant(3)
         for t in range(4):
             load_u(0, t, t + 1)
         load_cb()
-        load_w(0, 1)
+        load_w(0)
         u_sort(0, 1, 2)
-        nc.vector.memset(xs[:].rearrange("p g n -> p (g n)").bitcast(I32), 0)
+        clear(xs[:].rearrange("p g n -> p (g n)"))
         u_sort(0, 2, 3)
-        nc.vector.memset(ws[1][:].rearrange("p g n -> p (g n)").bitcast(I32), 0)
+        clear(ws[1][:].rearrange("p g n -> p (g n)"))
         u_sort(0, 3, 4)
-        load_z(0, 0, 1)
+        load_z(0, 0)
         load_scales(xs, x_scales, slice(0, I))
         load_x(0)
         load_u(1, 0, 2)
-        load_w(1, 2)
+        load_w(1)
         load_u(1, 2, 4)
-        load_z(0, 1, 2)
+        load_z(0, 1)
         load_u(2, 0, 2)
         load_x(1)
-        load_z(1, 0, 1)
+        load_z(1, 0)
         load_u(2, 2, 4)
-        load_z(1, 1, 2)
-        load_z(2, 0, 1)
-        load_z(2, 1, 2)
+        load_z(1, 1)
+        load_z(2, 0)
+        load_z(2, 1)
         with nc.allow_non_contiguous_dma(reason="one value of a to each partition"):
             nc.sync.dma_start(out=a_sb[:, :, 0], in_=a.rearrange("(r p) -> p r", p=P))
         nc.sync.dma_start(out=gain_sb[:], in_=gain.partition_broadcast(P))
 
         nc.scalar.activation(out=warm[:], in_=ident[:, 0:1], func=ACT.Sigmoid)
-        def r_front(g, ih):
-            for u in range(2):
-                logits(g, ih, u)
-                margin(g, ih, u)
-                sigmoid(g, ih, u)
 
-        lo, hi = slice(0, P), slice(P, HALF)
         for t in range(4):
             if t == 0:
-                warm_pass((256, 256, 512, 256))
+                warm_pass(256, 256, 512, 256)
             if t == 2:
-                warm_pass((512, 512))
+                warm_pass(512, 512)
             u_turn(0, t)
             u_copy(0, t)
         for t in range(2):
             u_quant(0, t, t + 1)
-            b_slice(0, 0, t)
-        z_sort(0, 0, 1)
+            for s in range(4):
+                b_mul(0, 0, s, [t])
+        z_sort(0, 0)
         u_quant(0, 2, 3)
         u_quant(0, 3, 4)
         z_turn(0, 0)
         c_turn()
         for s in range(4):
-            for t in range(2, 4):
-                for d in range(DG):
-                    b_pass(live["b_bank", 0, 0, s], 0, 0, s, t, d)
+            b_mul(0, 0, s, [2, 3])
             b_copy(0, 0, s)
         c_negate()
         c_guard()
         z_scale(0, 0)
         c_invert()
+        u_sort(1, 0, 2)
         b_divide()
-        u_sort(1, 0, 2, on_gpsimd, "c_inv")
         r_front(0, 0)
         b_quant(0, 0)
         u_sort(1, 2, 4)
-        z_sort(0, 1, 2)
-        u_sort(2, 0, 2, on_gpsimd, "z_raw0_1")
+        z_sort(0, 1)
         b_bank(0, 1, 0)
-        for s in range(1, 3):
-            b_mul(0, 1, s)
-            b_copy(0, 1, s, on_vector)
+        b_bank(0, 1, 1, on_vector)
+        b_bank(0, 1, 2, on_vector)
+
         for t in range(4):
             u_turn(1, t)
             u_copy(1, t)
         z_turn(0, 1)
+        u_sort(2, 0, 2)
         z_scale(0, 1)
-        z_sort(1, 0, 1)
         u_quant(1, 0, 2)
+        z_sort(1, 0)
         b_bank(0, 1, 3)
         u_sort(2, 2, 4, on_scalar)
         u_quant(1, 2, 4)
         r_make(0, 0, nc.gpsimd, "ug1")
         for u in range(2):
             logits(0, 1, u)
-        z_turn(1, 0)
         for t in range(2):
             u_turn(2, t)
             u_copy(2, t)
+        z_turn(1, 0)
+        margin(0, 1, 0)
+        sigmoid(0, 1, 0)
         z_scale(1, 0)
-        for u in range(2):
-            margin(0, 1, u)
-            sigmoid(0, 1, u)
+        margin(0, 1, 1)
+        sigmoid(0, 1, 1)
         for u in range(2):
             logits(1, 0, u)
             margin(1, 0, u)
-        z_sort(1, 1, 2)
-        z_sort(2, 0, 1)
-        z_sort(2, 1, 2)
+        z_sort(1, 1)
+        z_sort(2, 0)
+        z_sort(2, 1)
         for s in range(3):
             b_bank(1, 0, s)
         b_mul(1, 0, 3)
         b_quant(0, 1)
         u_quant(2, 0, 2)
+
         r_make(0, 1, nc.gpsimd, "ug0")
         r_quant(0, 0)
         sigmoid(1, 0, 0)
@@ -548,18 +536,15 @@ def tile_siglip_image_feature_gradient_k4_kernel(
             b_bank(1, 1, s)
         u_quant(2, 2, 4)
         r_quant(0, 1)
+
         r_make(1, 0, nc.gpsimd, "ug0")
         b_quant(1, 0)
         r_make(1, 1, nc.gpsimd, "rb2", lo)
         z_scale(2, 1)
         r_front(2, 0)
         r_front(2, 1)
-        b_mul(2, 0, 0)
-        b_copy(2, 0, 0, on_vector)
-        b_mul(2, 0, 1)
-        b_copy(2, 0, 1, on_vector)
-        for s in range(2, 4):
-            b_bank(2, 0, s)
+        for s in range(4):
+            b_bank(2, 0, s, on_vector if s < 2 else on_scalar)
         r_make(2, 0, nc.vector, "rb1")
         r_quant(1, 0)
         r_quant(2, 0)
@@ -569,33 +554,23 @@ def tile_siglip_image_feature_gradient_k4_kernel(
         b_quant(1, 1)
         for s in range(4):
             b_bank(2, 1, s)
-        b_quant(last, 1)
+        b_quant(2, 1)
+
         r_make(1, 1, nc.gpsimd, "bb2", hi)
         r_quant(2, 1, lo)
         r_make(2, 1, nc.gpsimd, "rb2", hi)
-        for r in range(2):
-            y_mul(0, r)
-            y_scale(0, r)
-            y_round(0, r)
-        for r in range(2):
-            y_mul(1, r)
-            y_scale(1, r)
-            y_round(1, r)
-        y_mul(0, 2)
-        y_scale(0, 2)
-        y_round(0, 2)
+        for h, r in ((0, 0), (0, 1), (1, 0), (1, 1), (0, 2)):
+            y_tile(h, r)
         y_mul(1, 2)
         r_quant(1, 1, hi)
-        r_quant(last, 1, hi)
+        r_quant(2, 1, hi)
         y_scale(1, 2)
         y_round(1, 2, on_vector)
         for h in range(NH):
             y_turn((h, 0), (h, 1))
             y_copy(h, [0, 1])
         y_quant(0, [0, 1])
-        y_mul(0, 3)
-        y_scale(0, 3, 2)
-        y_round(0, 3, on_scalar, 2)
+        y_tile(0, 3, 2)
         y_quant(1, [0, 1])
         store_words([0, 1])
         y_mul(1, 3)
@@ -609,10 +584,8 @@ def tile_siglip_image_feature_gradient_k4_kernel(
         y_scale(1, 3)
         y_copy(0, [3])
         y_copy(1, [3])
-        y_quant(0, [2])
-        y_quant(1, [2])
-        store_words([2])
-        y_quant(0, [3])
-        y_quant(1, [3])
-        store_words([3])
+        for r in range(2, IT):
+            for h in range(NH):
+                y_quant(h, [r])
+            store_words([r])
         store_scales()

@@ -67,7 +67,7 @@ def tile_siglip_image_feature_gradient_k4_kernel(
         yc = kept("yc", [P, NH, I], U32)
         ys = kept("ys", [P, NH, I], U8)
         live = {}
-        on_vector, on_scalar = nc.vector.tensor_copy, nc.scalar.copy
+        on_vector, on_scalar, on_gpsimd = nc.vector.tensor_copy, nc.scalar.copy, nc.gpsimd.tensor_copy
 
         def load_u(g, t0, t1):
             rows = U[512 * g : 512 * (g + 1), :].rearrange("(m t) k -> m t k", t=4)
@@ -127,10 +127,10 @@ def tile_siglip_image_feature_gradient_k4_kernel(
                     nc.tensor.transpose(bk[:, P * s : P * (s + 1)], src, ident[:])
             live["u_bank", g, t] = bk
 
-        def u_copy(g, t):
+        def u_copy(g, t, copy=on_scalar):
             if t % 2 == 0:
                 live["ug", g, t // 2] = kept("ug%d" % (t // 2), [P, 2, D], BF16)
-            on_scalar(
+            copy(
                 out=live["ug", g, t // 2][:, t % 2, :].bitcast(F32).rearrange("p (d m u) -> p d m u", d=DG, u=2),
                 in_=live["u_bank", g, t][:].rearrange("p (d u m) -> p d m u", d=DG, u=2),
             )
@@ -142,10 +142,10 @@ def tile_siglip_image_feature_gradient_k4_kernel(
                 in_=live["ug", g, t0 // 2][:, t0 % 2 : t0 % 2 + t1 - t0, :].rearrange("p t k -> p (t k)"),
             )
 
-        def z_sort(g, ih):
+        def z_sort(g, ih, copy=on_vector):
             zs = work.tile([P, 2, 2, P], F32, name="zs", tag="zs", bufs=4, align_bytes=256)
             words = z_raw[g, ih][:].rearrange("q r j -> q (r j)").bitcast(F32)
-            on_vector(
+            copy(
                 out=zs[:].rearrange("q r u (x i) -> q r x u i", i=4),
                 in_=words.rearrange("q (r x i u) -> q r x u i", r=2, i=4, u=2),
             )
@@ -262,9 +262,11 @@ def tile_siglip_image_feature_gradient_k4_kernel(
                 in_=live["bb", g, h][:].rearrange("p n t -> p (n t)"),
             )
 
-        def y_mul(h, r):
-            bk = bank("bk_y")
-            for g in range(G):
+        def y_mul(h, r, groups=range(G)):
+            if groups[0] == 0:
+                live["y_bank", h, r] = bank("bk_y")
+            bk = live["y_bank", h, r]
+            for g in groups:
                 nc.tensor.matmul_mx(
                     out=bk[:],
                     lhsT=rc[g][:, P * r : P * (r + 1)].bitcast(FP8X4),
@@ -274,9 +276,8 @@ def tile_siglip_image_feature_gradient_k4_kernel(
                     start=(g == 0),
                     stop=(g == G - 1),
                 )
-            live["y_bank", h, r] = bk
 
-        def y_scale(h, r, parts=1):
+        def y_scale(h, r, parts=1, stores=1):
             yf = work.tile([P, 512], F32, name="yf", tag="yf", bufs=8, align_bytes=256)
             for k in range(parts):
                 n0, n1 = 512 * k // parts, 512 * (k + 1) // parts
@@ -288,7 +289,9 @@ def tile_siglip_image_feature_gradient_k4_kernel(
                     op0=ALU.mult,
                     op1=ALU.mult,
                 )
-            nc.sync.dma_start(out=out_0[P * r : P * (r + 1), 512 * h : 512 * (h + 1)], in_=yf[:])
+                if stores > 1 or k == parts - 1:
+                    n0 = n0 if stores > 1 else 0
+                    nc.sync.dma_start(out=out_0[P * r : P * (r + 1), 512 * h + n0 : 512 * h + n1], in_=yf[:, n0:n1])
             live["yf", h, r] = yf
 
         def y_round(h, r, copy=on_scalar, parts=1):
@@ -345,17 +348,17 @@ def tile_siglip_image_feature_gradient_k4_kernel(
                 in_=yg[h][:, cols, :].rearrange("p i t -> p (i t)"),
             )
 
-        def store_words(rows):
+        def store_words(rows, groups=slice(0, NH), queue=nc.sync):
             cols = slice(P * rows[0], P * (rows[0] + len(rows)))
             dst = out_1.rearrange("h p m t -> p h (m t)").bitcast(I32)
-            nc.sync.dma_start(out=dst[:, :, cols], in_=yc[:, :, cols].bitcast(I32))
+            queue.dma_start(out=dst[:, groups, cols], in_=yc[:, groups, cols].bitcast(I32))
 
-        def store_scales():
+        def store_scales(rows, queues):
+            cols = slice(P * rows[0], P * (rows[0] + len(rows)))
             for q in range(4):
-                queue = nc.scalar if q % 2 == 0 else nc.sync
-                queue.dma_start(
-                    out=out_2[:, 4 * q : 4 * q + 4, :].rearrange("h r m -> r h m").bitcast(I32),
-                    in_=ys[32 * q : 32 * q + 4].bitcast(I32),
+                queues[q % len(queues)].dma_start(
+                    out=out_2[:, 4 * q : 4 * q + 4, cols].rearrange("h r m -> r h m").bitcast(I32),
+                    in_=ys[32 * q : 32 * q + 4, :, cols].bitcast(I32),
                 )
 
         split = "p g (u e) -> p g u e"
@@ -444,12 +447,11 @@ def tile_siglip_image_feature_gradient_k4_kernel(
         load_z(1, 1)
         load_z(2, 0)
         load_z(2, 1)
+
         with nc.allow_non_contiguous_dma(reason="one value of a to each partition"):
             nc.sync.dma_start(out=a_sb[:, :, 0], in_=a.rearrange("(r p) -> p r", p=P))
         nc.sync.dma_start(out=gain_sb[:], in_=gain.partition_broadcast(P))
-
         nc.scalar.activation(out=warm[:], in_=ident[:, 0:1], func=ACT.Sigmoid)
-
         for t in range(4):
             if t == 0:
                 warm_pass(256, 256, 512, 256)
@@ -479,22 +481,22 @@ def tile_siglip_image_feature_gradient_k4_kernel(
         b_quant(0, 0)
         u_sort(1, 2, 4)
         z_sort(0, 1)
+        r_make(0, 0, nc.gpsimd, "u_raw1_2", lo)
         b_bank(0, 1, 0)
         b_bank(0, 1, 1, on_vector)
         b_bank(0, 1, 2, on_vector)
-
         for t in range(4):
             u_turn(1, t)
             u_copy(1, t)
         z_turn(0, 1)
-        u_sort(2, 0, 2)
         z_scale(0, 1)
+        u_sort(2, 0, 2)
         u_quant(1, 0, 2)
         z_sort(1, 0)
         b_bank(0, 1, 3)
-        u_sort(2, 2, 4, on_scalar)
+        r_make(0, 0, nc.gpsimd, "z_raw1_0", hi)
+        u_sort(2, 2, 4, on_gpsimd)
         u_quant(1, 2, 4)
-        r_make(0, 0, nc.gpsimd, "ug1")
         for u in range(2):
             logits(0, 1, u)
         for t in range(2):
@@ -503,89 +505,112 @@ def tile_siglip_image_feature_gradient_k4_kernel(
         z_turn(1, 0)
         margin(0, 1, 0)
         sigmoid(0, 1, 0)
+        z_sort(1, 1, on_scalar)
         z_scale(1, 0)
         margin(0, 1, 1)
         sigmoid(0, 1, 1)
         for u in range(2):
             logits(1, 0, u)
             margin(1, 0, u)
-        z_sort(1, 1)
         z_sort(2, 0)
         z_sort(2, 1)
-        for s in range(3):
-            b_bank(1, 0, s)
+        b_bank(1, 0, 0)
+        sigmoid(1, 0, 0)
+        b_bank(1, 0, 1)
+        sigmoid(1, 0, 1)
+        b_bank(1, 0, 2)
         b_mul(1, 0, 3)
         b_quant(0, 1)
         u_quant(2, 0, 2)
-
+        r_quant(0, 0, lo)
         r_make(0, 1, nc.gpsimd, "ug0")
-        r_quant(0, 0)
-        sigmoid(1, 0, 0)
+        r_quant(0, 0, hi)
         z_turn(1, 1)
         for t in range(2, 4):
             u_turn(2, t)
+        b_copy(1, 0, 3)
+        for t in range(2, 4):
             u_copy(2, t)
         z_turn(2, 0)
         z_turn(2, 1)
-        b_copy(1, 0, 3, on_vector)
         z_scale(1, 1)
         z_scale(2, 0)
-        sigmoid(1, 0, 1)
+        z_scale(2, 1)
         r_front(1, 1)
         for s in range(4):
             b_bank(1, 1, s)
         u_quant(2, 2, 4)
         r_quant(0, 1)
-
         r_make(1, 0, nc.gpsimd, "ug0")
         b_quant(1, 0)
-        r_make(1, 1, nc.gpsimd, "rb2", lo)
-        z_scale(2, 1)
+
         r_front(2, 0)
-        r_front(2, 1)
+        for u in range(2):
+            logits(2, 1, u)
+            margin(2, 1, u)
         for s in range(4):
-            b_bank(2, 0, s, on_vector if s < 2 else on_scalar)
+            b_bank(2, 0, s, on_vector if s < 1 else on_scalar)
         r_make(2, 0, nc.vector, "rb1")
         r_quant(1, 0)
+        r_make(1, 1, nc.vector, "rb2", lo)
         r_quant(2, 0)
-        b_quant(2, 0)
         r_quant(1, 1, lo)
-        r_make(2, 1, nc.vector, "rb1", lo)
+        b_quant(2, 0)
+        r_make(1, 1, nc.gpsimd, "bb1", hi)
         b_quant(1, 1)
-        for s in range(4):
+        for s in range(3):
             b_bank(2, 1, s)
+        sigmoid(2, 1, 0)
+        b_bank(2, 1, 3)
+        sigmoid(2, 1, 1)
+        y_tile(0, 0)
+        y_tile(0, 1)
+        y_mul(1, 0, [0, 1])
+        y_mul(1, 1, [0, 1])
+        y_mul(0, 2, [0, 1])
         b_quant(2, 1)
-
-        r_make(1, 1, nc.gpsimd, "bb2", hi)
-        r_quant(2, 1, lo)
-        r_make(2, 1, nc.gpsimd, "rb2", hi)
-        for h, r in ((0, 0), (0, 1), (1, 0), (1, 1), (0, 2)):
-            y_tile(h, r)
-        y_mul(1, 2)
+        r_make(2, 1, nc.vector, "rb1", lo)
         r_quant(1, 1, hi)
+        r_make(2, 1, nc.gpsimd, "bb1", hi)
+        r_quant(2, 1, lo)
+        y_mul(1, 0, [2])
+        y_scale(1, 0)
+        y_round(1, 0)
+        y_mul(1, 1, [2])
+        y_scale(1, 1)
+        y_mul(1, 2, [0, 1])
+        y_mul(0, 2, [2])
+        y_scale(0, 2)
+        y_mul(1, 2, [2])
+        y_turn((0, 0), (0, 1))
+        y_turn((1, 0))
+        y_copy(0, [0, 1])
+        y_copy(1, [0])
+        y_round(1, 1)
         r_quant(2, 1, hi)
+        y_round(0, 2, on_gpsimd)
         y_scale(1, 2)
-        y_round(1, 2, on_vector)
-        for h in range(NH):
-            y_turn((h, 0), (h, 1))
-            y_copy(h, [0, 1])
+        y_mul(0, 3)
+        y_round(1, 2)
         y_quant(0, [0, 1])
-        y_tile(0, 3, 2)
-        y_quant(1, [0, 1])
-        store_words([0, 1])
+        y_quant(1, [0])
+        store_words([0, 1], slice(0, 1))
+        y_scale(0, 3)
+        y_round(0, 3, on_gpsimd)
         y_mul(1, 3)
         y_turn((0, 2))
-        y_turn((1, 2))
-        y_round_from_bank(1, 3)
         y_copy(0, [2])
-        y_copy(1, [2])
-        y_turn((0, 3))
+        y_turn((1, 1), (1, 2))
+        y_copy(1, [1, 2])
+        y_round_from_bank(1, 3)
         y_turn((1, 3))
+        y_turn((0, 3))
         y_scale(1, 3)
-        y_copy(0, [3])
         y_copy(1, [3])
-        for r in range(2, IT):
-            for h in range(NH):
-                y_quant(h, [r])
-            store_words([r])
-        store_scales()
+        y_copy(0, [3])
+        y_quant(1, [1, 2])
+        y_quant(1, [3])
+        store_words([0, 1, 2, 3], slice(1, 2))
+        y_quant(0, [2, 3])
+        store_words([2, 3], slice(0, 1))
+        store_scales([0, 1, 2, 3], [nc.scalar, nc.sync])

@@ -105,8 +105,9 @@ def tile_siglip_image_feature_gradient_k4_kernel(
 
         def u_sort(g, t0, t1, copy=on_vector):
             n = t1 - t0
-            srt = work.tile([P, n * DG, 2, P], F32, name="srt", tag="srt", bufs=3, align_bytes=256)
-            words = u_pack[g, t0][:, 0:n, :].rearrange("q t k -> q (t k)").bitcast(F32)
+            srt = work.tile([P, n * DG, 2, P], F32, name="srt", tag="srt", bufs=4, align_bytes=256)
+            first = t0 if (g, t0) in u_pack else t0 - 1
+            words = u_pack[g, first][:, t0 - first : t1 - first, :].rearrange("q t k -> q (t k)").bitcast(F32)
             copy(
                 out=srt[:].rearrange("q s u (x i) -> q s x u i", i=4),
                 in_=words.rearrange("q (s x i u) -> q s x u i", x=P // 4, i=4, u=2),
@@ -156,7 +157,11 @@ def tile_siglip_image_feature_gradient_k4_kernel(
             for r in range(2):
                 for u in range(2):
                     col = HALF * u + P * r
-                    nc.tensor.transpose(bk[:, col : col + P], live["zs", g, ih][:, r, u, :], ident[:])
+                    if ("zs", g, ih) in live:
+                        src = live["zs", g, ih][:, r, u, :]
+                    else:
+                        src = z_raw[g, ih][:, r, :].bitcast(F32)[:, u:256:2]
+                    nc.tensor.transpose(bk[:, col : col + P], src, ident[:])
             live["z_bank", g, ih] = bk
 
         def z_scale(g, ih):
@@ -206,6 +211,11 @@ def tile_siglip_image_feature_gradient_k4_kernel(
                 func=ACT.Sigmoid,
             )
 
+        def margins(g, ih):
+            for u in range(2):
+                logits(g, ih, u)
+                margin(g, ih, u)
+
         def r_front(g, ih):
             for u in range(2):
                 logits(g, ih, u)
@@ -221,6 +231,16 @@ def tile_siglip_image_feature_gradient_k4_kernel(
                 op=ALU.mult,
             )
             live["rb", g, ih, part.start] = rb
+
+        def r_share(g, ih, engine, n0, n1, slot=None):
+            if slot:
+                live["rb", g, ih, 0] = kept(slot, [P, HALF, 4], BF16)
+            engine.tensor_tensor(
+                out=live["rb", g, ih, 0][:, n0:n1, :].rearrange("p i (u e) -> p i u e", u=2),
+                in0=live["sg", g, ih][:, :, n0:n1, :].rearrange("p u i e -> p i u e"),
+                in1=zc[g][ih][:, :, n0:n1, :].rearrange("p u i e -> p i u e"),
+                op=ALU.mult,
+            )
 
         def r_quant(g, ih, part=slice(0, HALF)):
             cols = slice(HALF * ih + part.start, HALF * ih + part.stop)
@@ -278,7 +298,7 @@ def tile_siglip_image_feature_gradient_k4_kernel(
                 )
 
         def y_scale(h, r, parts=1, stores=1):
-            yf = work.tile([P, 512], F32, name="yf", tag="yf", bufs=8, align_bytes=256)
+            yf = work.tile([P, 512], F32, name="yf", tag="yf", bufs=6, align_bytes=256)
             for k in range(parts):
                 n0, n1 = 512 * k // parts, 512 * (k + 1) // parts
                 nc.vector.scalar_tensor_tensor(
@@ -475,8 +495,9 @@ def tile_siglip_image_feature_gradient_k4_kernel(
         c_guard()
         z_scale(0, 0)
         c_invert()
-        u_sort(1, 0, 2)
+        u_sort(1, 0, 1)
         b_divide()
+        u_sort(1, 1, 2)
         r_front(0, 0)
         b_quant(0, 0)
         u_sort(1, 2, 4)
@@ -543,74 +564,51 @@ def tile_siglip_image_feature_gradient_k4_kernel(
         r_quant(0, 1)
         r_make(1, 0, nc.gpsimd, "ug0")
         b_quant(1, 0)
-
+        r_make(1, 1, nc.gpsimd, "rb2", lo)
         r_front(2, 0)
-        for u in range(2):
-            logits(2, 1, u)
-            margin(2, 1, u)
+        r_front(2, 1)
         for s in range(4):
-            b_bank(2, 0, s, on_vector if s < 1 else on_scalar)
+            b_bank(2, 0, s, on_vector if s < 2 else on_scalar)
         r_make(2, 0, nc.vector, "rb1")
         r_quant(1, 0)
-        r_make(1, 1, nc.vector, "rb2", lo)
         r_quant(2, 0)
-        r_quant(1, 1, lo)
         b_quant(2, 0)
-        r_make(1, 1, nc.gpsimd, "bb1", hi)
-        b_quant(1, 1)
-        for s in range(3):
-            b_bank(2, 1, s)
-        sigmoid(2, 1, 0)
-        b_bank(2, 1, 3)
-        sigmoid(2, 1, 1)
-        y_tile(0, 0)
-        y_tile(0, 1)
-        y_mul(1, 0, [0, 1])
-        y_mul(1, 1, [0, 1])
-        y_mul(0, 2, [0, 1])
-        b_quant(2, 1)
+        r_quant(1, 1, lo)
         r_make(2, 1, nc.vector, "rb1", lo)
-        r_quant(1, 1, hi)
-        r_make(2, 1, nc.gpsimd, "bb1", hi)
+        b_quant(1, 1)
+        for s in range(4):
+            b_bank(2, 1, s)
+        b_quant(2, 1)
+        r_make(1, 1, nc.gpsimd, "bb2", hi)
         r_quant(2, 1, lo)
-        y_mul(1, 0, [2])
-        y_scale(1, 0)
-        y_round(1, 0)
-        y_mul(1, 1, [2])
-        y_scale(1, 1)
-        y_mul(1, 2, [0, 1])
-        y_mul(0, 2, [2])
-        y_scale(0, 2)
-        y_mul(1, 2, [2])
-        y_turn((0, 0), (0, 1))
-        y_turn((1, 0))
-        y_copy(0, [0, 1])
-        y_copy(1, [0])
-        y_round(1, 1)
+        r_make(2, 1, nc.gpsimd, "rb2", hi)
+        for h, r in ((0, 0), (0, 1), (1, 0), (1, 1), (0, 2)):
+            y_tile(h, r)
+        y_mul(1, 2)
+        r_quant(1, 1, hi)
         r_quant(2, 1, hi)
-        y_round(0, 2, on_gpsimd)
         y_scale(1, 2)
-        y_mul(0, 3)
-        y_round(1, 2)
+        y_round(1, 2, on_vector)
+        for h in range(NH):
+            y_turn((h, 0), (h, 1))
+            y_copy(h, [0, 1])
         y_quant(0, [0, 1])
-        y_quant(1, [0])
-        store_words([0, 1], slice(0, 1))
-        y_scale(0, 3)
-        y_round(0, 3, on_gpsimd)
+        y_tile(0, 3, 2)
+        y_quant(1, [0, 1])
+        store_words([0, 1])
         y_mul(1, 3)
         y_turn((0, 2))
-        y_copy(0, [2])
-        y_turn((1, 1), (1, 2))
-        y_copy(1, [1, 2])
+        y_turn((1, 2))
         y_round_from_bank(1, 3)
-        y_turn((1, 3))
+        y_copy(0, [2])
+        y_copy(1, [2])
         y_turn((0, 3))
+        y_turn((1, 3))
         y_scale(1, 3)
-        y_copy(1, [3])
         y_copy(0, [3])
-        y_quant(1, [1, 2])
-        y_quant(1, [3])
-        store_words([0, 1, 2, 3], slice(1, 2))
-        y_quant(0, [2, 3])
-        store_words([2, 3], slice(0, 1))
+        y_copy(1, [3])
+        for r in range(2, IT):
+            for h in range(NH):
+                y_quant(h, [r])
+            store_words([r])
         store_scales([0, 1, 2, 3], [nc.scalar, nc.sync])

from contextlib import ExitStack

import concourse.mybir as mybir
from concourse.masks import make_identity

I, J, D, N = 512, 1536, 1024, 1024
FLOPS = 2 * I * J * D + 2 * J * D * N + 2 * I * J * N

F32 = mybir.dt.float32
BF16 = mybir.dt.bfloat16
I32 = mybir.dt.int32
U32 = mybir.dt.uint32
U8 = mybir.dt.uint8
FP8X4 = mybir.dt.float8_e4m3fn_x4
FP4X4 = mybir.dt.float4_e2m1fn_x4
ALU = mybir.AluOpType
ACT = mybir.ActivationFunctionType

P = 128
G = J // 512
DG = D // 512
NH = N // 512
IT = I // P
HALF = I // 2


def tile_siglip_image_feature_gradient_k4_kernel(
    tc, x_words, x_scales, U, w_words, w_scales, Z, c, b, a, gain, out_0, out_1, out_2
):
    nc = tc.nc
    with ExitStack() as ctx:
        keep = ctx.enter_context(tc.tile_pool(name="keep", bufs=1))
        work = ctx.enter_context(tc.tile_pool(name="work", bufs=2))
        psum = ctx.enter_context(tc.psum_pool(name="psum", bufs=8))
        ctx.enter_context(tc.manual_schedule())

        def kept(name, shape, dtype):
            return keep.tile(shape, dtype, name=name, align_bytes=256)

        def bank(name):
            return psum.tile([P, 512], F32, name=name, tag="bank")

        ident = kept("ident", [P, P], F32)
        cb_rows = kept("cb_rows", [P, 512], BF16)
        a_sb = kept("a_sb", [P, IT, 2], BF16)
        warm = kept("warm", [P, 1], F32)
        c_neg = kept("c_neg", [P, G, 4], BF16)
        c_safe = kept("c_safe", [P, G, 4], F32)
        c_inv = kept("c_inv", [P, G, 4], F32)
        b_over_c = kept("b_over_c", [P, G, 4], F32)
        gain_sb = kept("gain_sb", [P, N], BF16)
        xw = [kept("xw%d" % ih, [P, DG, HALF], U32) for ih in range(2)]
        xs = kept("xs", [P, DG, I], U8)
        ww = {}
        ws = [kept("ws%d" % h, [P, DG, 512], U8) for h in range(NH)]
        u_raw = {}
        u_pack = {}
        z_raw = {}
        uc = [kept("uc%d" % g, [P, 4, DG * P], U32) for g in range(G)]
        us = [kept("us%d" % g, [P, 4, DG * P], U8) for g in range(G)]
        zc = [[kept("zc%d_%d" % (g, ih), [P, 2, HALF, 2], BF16) for ih in range(2)] for g in range(G)]
        rc = [kept("rc%d" % g, [P, I], U32) for g in range(G)]
        rs = [kept("rs%d" % g, [P, I], U8) for g in range(G)]
        bc = [[kept("bc%d_%d" % (g, h), [P, 512], U32) for h in range(NH)] for g in range(G)]
        bs = [[kept("bs%d_%d" % (g, h), [P, 512], U8) for h in range(NH)] for g in range(G)]
        yg = [kept("yg%d" % h, [P, I, 4], BF16) for h in range(NH)]
        yc = kept("yc", [P, NH, I], U32)
        ys = kept("ys", [P, NH, I], U8)
        live = {}
        on_vector, on_scalar, on_gpsimd = nc.vector.tensor_copy, nc.scalar.copy, nc.gpsimd.tensor_copy

        def load_u(g, t0, t1):
            rows = U[512 * g : 512 * (g + 1), :].rearrange("(m t) k -> m t k", t=4)
            raw = kept("u_raw%d_%d" % (g, t0), [P, t1 - t0, D], BF16)
            nc.sync.dma_start(out=raw[:], in_=rows[:, t0:t1, :])
            u_pack[g, t0] = raw
            for t in range(t0, t1):
                u_raw[g, t] = raw[:, t - t0, :]

        def load_w(h):
            load_scales(ws[h], w_scales, slice(512 * h, 512 * (h + 1)))
            src = w_words[:, :, N * h : N * (h + 1)].rearrange("g p n -> p g n")
            ww[h] = kept("ww%d" % h, [P, DG, N], U8)
            nc.sync.dma_start(out=ww[h][:].bitcast(I32), in_=src.bitcast(I32))

        def load_z(g, ih):
            z_raw[g, ih] = kept("z_raw%d_%d" % (g, ih), [P, 2, 512], BF16)
            src = Z[HALF * ih : HALF * (ih + 1), 512 * g : 512 * (g + 1)]
            nc.sync.dma_start(out=z_raw[g, ih][:], in_=src.rearrange("(r p) j -> p r j", p=P))

        def load_scales(plane, src, cols):
            for q in range(4):
                nc.sync.dma_start(
                    out=plane[32 * q : 32 * q + 4, :, :].bitcast(I32),
                    in_=src[:, 4 * q : 4 * q + 4, cols].rearrange("g r n -> r g n").bitcast(I32),
                )

        def load_x(ih):
            src = x_words[:, :, HALF * ih : HALF * (ih + 1), :].rearrange("g p n t -> p g (n t)")
            nc.sync.dma_start(out=xw[ih][:].bitcast(I32), in_=src.bitcast(I32))

        def load_cb():
            nc.gpsimd.dma_start(out=cb_rows[0:G, :], in_=c.rearrange("(g j) -> g j", g=G))
            nc.gpsimd.dma_start(out=cb_rows[G : 2 * G, :], in_=b.rearrange("(g j) -> g j", g=G))

        def u_sort(g, t0, t1, copy=on_vector):
            n = t1 - t0
            srt = work.tile([P, n * DG, 2, P], F32, name="srt", tag="srt", bufs=4, align_bytes=256)
            first = t0 if (g, t0) in u_pack else t0 - 1
            words = u_pack[g, first][:, t0 - first : t1 - first, :].rearrange("q t k -> q (t k)").bitcast(F32)
            copy(
                out=srt[:].rearrange("q s u (x i) -> q s x u i", i=4),
                in_=words.rearrange("q (s x i u) -> q s x u i", x=P // 4, i=4, u=2),
            )
            for t in range(t0, t1):
                live["srt", g, t] = srt[:, DG * (t - t0) : DG * (t - t0 + 1)]

        def u_turn(g, t):
            bk = bank("bk_u")
            words = u_raw[g, t].bitcast(F32)
            for d in range(DG):
                for u in range(2):
                    s = 2 * d + u
                    if ("srt", g, t) in live:
                        src = live["srt", g, t][:, d, u, :]
                    else:
                        src = words[:, 256 * d + u : 256 * (d + 1) : 2]
                    nc.tensor.transpose(bk[:, P * s : P * (s + 1)], src, ident[:])
            live["u_bank", g, t] = bk

        def u_copy(g, t, copy=on_scalar):
            if t % 2 == 0:
                live["ug", g, t // 2] = kept("ug%d" % (t // 2), [P, 2, D], BF16)
            copy(
                out=live["ug", g, t // 2][:, t % 2, :].bitcast(F32).rearrange("p (d m u) -> p d m u", d=DG, u=2),
                in_=live["u_bank", g, t][:].rearrange("p (d u m) -> p d m u", d=DG, u=2),
            )

        def u_quant(g, t0, t1):
            nc.vector.quantize_mx(
                out=uc[g][:, t0:t1, :].rearrange("p t m -> p (t m)").bitcast(FP8X4),
                scales=us[g][:, t0:t1, :].rearrange("p t m -> p (t m)"),
                in_=live["ug", g, t0 // 2][:, t0 % 2 : t0 % 2 + t1 - t0, :].rearrange("p t k -> p (t k)"),
            )

        def z_sort(g, ih, copy=on_vector):
            zs = work.tile([P, 2, 2, P], F32, name="zs", tag="zs", bufs=4, align_bytes=256)
            words = z_raw[g, ih][:].rearrange("q r j -> q (r j)").bitcast(F32)
            copy(
                out=zs[:].rearrange("q r u (x i) -> q r x u i", i=4),
                in_=words.rearrange("q (r x i u) -> q r x u i", r=2, i=4, u=2),
            )
            live["zs", g, ih] = zs

        def z_turn(g, ih):
            bk = bank("bk_z")
            for r in range(2):
                for u in range(2):
                    col = HALF * u + P * r
                    if ("zs", g, ih) in live:
                        src = live["zs", g, ih][:, r, u, :]
                    else:
                        src = z_raw[g, ih][:, r, :].bitcast(F32)[:, u:256:2]
                    nc.tensor.transpose(bk[:, col : col + P], src, ident[:])
            live["z_bank", g, ih] = bk

        def z_scale(g, ih):
            nc.vector.tensor_tensor(
                out=zc[g][ih][:],
                in0=live["z_bank", g, ih][:].bitcast(BF16).rearrange("p (u i e) -> p u i e", u=2, e=2),
                in1=c_neg[:, g, :].rearrange("p (u e) -> p u e", u=2).unsqueeze(2).broadcast_to([P, 2, HALF, 2]),
                op=ALU.mult,
            )

        def logits(g, ih, u):
            bk = bank("bk_l")
            for e in range(2):
                t = 2 * u + e
                for d in range(DG):
                    nc.tensor.matmul_mx(
                        out=bk[:, HALF * e : HALF * (e + 1)],
                        lhsT=uc[g][:, t, P * d : P * (d + 1)].bitcast(FP8X4),
                        lhsT_scale=us[g][:, t, P * d : P * (d + 1)],
                        rhs=xw[ih][:, d, :].bitcast(FP8X4),
                        rhs_scale=xs[:, d, HALF * ih : HALF * (ih + 1)],
                        start=(d == 0),
                        stop=(d == DG - 1),
                    )
            live["l_bank", g, ih, u] = bk

        def margin(g, ih, u):
            mg = work.tile([P, 2, HALF], F32, name="mg", tag="mg", bufs=4, align_bytes=256)
            for e in range(2):
                t = 2 * u + e
                nc.vector.scalar_tensor_tensor(
                    out=mg[:, e, :],
                    in0=live["l_bank", g, ih, u][:, HALF * e : HALF * (e + 1)],
                    scalar=b_over_c[:, g, t : t + 1],
                    in1=zc[g][ih][:, u, :, e],
                    op0=ALU.subtract,
                    op1=ALU.mult,
                )
            live["mg", g, ih, u] = mg

        def sigmoid(g, ih, u):
            if u == 0:
                live["sg", g, ih] = work.tile([P, 2, HALF, 2], F32, name="sg", tag="sg", bufs=4, align_bytes=256)
            nc.scalar.activation(
                out=live["sg", g, ih][:, u],
                in_=live["mg", g, ih, u][:].rearrange("p e i -> p i e"),
                func=ACT.Sigmoid,
            )

        def margins(g, ih):
            for u in range(2):
                logits(g, ih, u)
                margin(g, ih, u)

        def r_front(g, ih):
            for u in range(2):
                logits(g, ih, u)
                margin(g, ih, u)
                sigmoid(g, ih, u)

        def r_make(g, ih, engine, slot, part=slice(0, HALF)):
            rb = kept(slot, [P, part.stop - part.start, 4], BF16)
            engine.tensor_tensor(
                out=rb[:].rearrange("p i (u e) -> p i u e", u=2),
                in0=live["sg", g, ih][:, :, part, :].rearrange("p u i e -> p i u e"),
                in1=zc[g][ih][:, :, part, :].rearrange("p u i e -> p i u e"),
                op=ALU.mult,
            )
            live["rb", g, ih, part.start] = rb

        def r_share(g, ih, engine, n0, n1, slot=None):
            if slot:
                live["rb", g, ih, 0] = kept(slot, [P, HALF, 4], BF16)
            engine.tensor_tensor(
                out=live["rb", g, ih, 0][:, n0:n1, :].rearrange("p i (u e) -> p i u e", u=2),
                in0=live["sg", g, ih][:, :, n0:n1, :].rearrange("p u i e -> p i u e"),
                in1=zc[g][ih][:, :, n0:n1, :].rearrange("p u i e -> p i u e"),
                op=ALU.mult,
            )

        def r_quant(g, ih, part=slice(0, HALF)):
            cols = slice(HALF * ih + part.start, HALF * ih + part.stop)
            nc.vector.quantize_mx(
                out=rc[g][:, cols].bitcast(FP8X4),
                scales=rs[g][:, cols],
                in_=live["rb", g, ih, part.start][:].rearrange("p i t -> p (i t)"),
            )

        def b_mul(g, h, s, slots=range(4)):
            if slots[0] == 0:
                live["b_bank", g, h, s] = bank("bk_b")
            for t in slots:
                for d in range(DG):
                    nc.tensor.matmul_mx(
                        out=live["b_bank", g, h, s][:, P * t : P * (t + 1)],
                        lhsT=uc[g][:, t, P * d : P * (d + 1)].bitcast(FP8X4),
                        lhsT_scale=us[g][:, t, P * d : P * (d + 1)],
                        rhs=ww[h][:, d, 256 * s : 256 * (s + 1)].bitcast(FP4X4),
                        rhs_scale=ws[h][:, d, P * s : P * (s + 1)],
                        start=(d == 0),
                        stop=(d == DG - 1),
                    )

        def b_copy(g, h, s, copy=on_scalar):
            if ("bb", g, h) not in live:
                live["bb", g, h] = kept("bb%d" % ((2 * g + h) % 3), [P, 512, 4], BF16)
            dst = live["bb", g, h][:, P * s : P * (s + 1), :]
            copy(out=dst, in_=live["b_bank", g, h, s][:].rearrange("p (t n) -> p n t", t=4))

        def b_bank(g, h, s, copy=on_scalar):
            b_mul(g, h, s)
            b_copy(g, h, s, copy)

        def b_quant(g, h):
            nc.vector.quantize_mx(
                out=bc[g][h][:].bitcast(FP8X4),
                scales=bs[g][h][:],
                in_=live["bb", g, h][:].rearrange("p n t -> p (n t)"),
            )

        def y_mul(h, r, groups=range(G)):
            if groups[0] == 0:
                live["y_bank", h, r] = bank("bk_y")
            bk = live["y_bank", h, r]
            for g in groups:
                nc.tensor.matmul_mx(
                    out=bk[:],
                    lhsT=rc[g][:, P * r : P * (r + 1)].bitcast(FP8X4),
                    lhsT_scale=rs[g][:, P * r : P * (r + 1)],
                    rhs=bc[g][h][:].bitcast(FP8X4),
                    rhs_scale=bs[g][h][:],
                    start=(g == 0),
                    stop=(g == G - 1),
                )

        def y_scale(h, r, parts=1, stores=1):
            yf = work.tile([P, 512], F32, name="yf", tag="yf", bufs=6, align_bytes=256)
            for k in range(parts):
                n0, n1 = 512 * k // parts, 512 * (k + 1) // parts
                nc.vector.scalar_tensor_tensor(
                    out=yf[:, n0:n1],
                    in0=live["y_bank", h, r][:, n0:n1],
                    scalar=a_sb[:, r, 0:1],
                    in1=gain_sb[:, 512 * h + n0 : 512 * h + n1],
                    op0=ALU.mult,
                    op1=ALU.mult,
                )
                if stores > 1 or k == parts - 1:
                    n0 = n0 if stores > 1 else 0
                    nc.sync.dma_start(out=out_0[P * r : P * (r + 1), 512 * h + n0 : 512 * h + n1], in_=yf[:, n0:n1])
            live["yf", h, r] = yf

        def y_round(h, r, copy=on_scalar, parts=1):
            yb = work.tile([P, 512], BF16, name="yb", tag="yb", bufs=8, align_bytes=256)
            dst = yb[:].rearrange("q (u x p e) -> q x u p e", u=2, p=4, e=2)
            src = live["yf", h, r][:].rearrange("q (x p u e) -> q x u p e", p=4, u=2, e=2)
            for k in range(parts):
                x = slice(32 * k // parts, 32 * (k + 1) // parts)
                copy(out=dst[:, x], in_=src[:, x])
            live["yb", h, r] = yb

        def y_tile(h, r, parts=1):
            y_mul(h, r)
            y_scale(h, r, parts)
            y_round(h, r, on_scalar, parts)

        def y_round_from_bank(h, r):
            yb = work.tile([P, 512], BF16, name="yb", tag="yb", bufs=8, align_bytes=256)
            src = live["y_bank", h, r][:].rearrange("q (p u e) -> q u p e", u=2, e=2)
            gn = gain_sb[:, 512 * h : 512 * (h + 1)].rearrange("q (p u e) -> q u p e", u=2, e=2)
            for u in range(2):
                nc.vector.scalar_tensor_tensor(
                    out=yb[:, 256 * u : 256 * (u + 1)].rearrange("q (p e) -> q p e", e=2),
                    in0=src[:, u],
                    scalar=a_sb[:, r, 0:1],
                    in1=gn[:, u],
                    op0=ALU.mult,
                    op1=ALU.mult,
                )
            live["yb", h, r] = yb

        def y_turn(*tiles):
            bk = bank("bk_t")
            for k, (h, r) in enumerate(tiles):
                words = live["yb", h, r][:].bitcast(F32)
                for u in range(2):
                    col = P * (2 * k + u)
                    nc.tensor.transpose(bk[:, col : col + P], words[:, P * u : P * (u + 1)], ident[:])
                live["t_bank", h, r] = bk[:, 2 * P * k :]

        def y_copy(h, rows):
            n = len(rows)
            dst = yg[h][:, P * rows[0] : P * (rows[0] + n), :].rearrange("p i t -> p (i t)").bitcast(F32)
            on_scalar(
                out=dst.rearrange("p (k i u) -> p k i u", k=n, u=2),
                in_=live["t_bank", h, rows[0]][:, 0 : 256 * n].rearrange("p (k u i) -> p k i u", k=n, u=2),
            )

        def y_quant(h, rows):
            cols = slice(P * rows[0], P * (rows[0] + len(rows)))
            nc.vector.quantize_mx(
                out=yc[:, h, cols].bitcast(FP8X4),
                scales=ys[:, h, cols],
                in_=yg[h][:, cols, :].rearrange("p i t -> p (i t)"),
            )

        def store_words(rows, groups=slice(0, NH), queue=nc.sync):
            cols = slice(P * rows[0], P * (rows[0] + len(rows)))
            dst = out_1.rearrange("h p m t -> p h (m t)").bitcast(I32)
            queue.dma_start(out=dst[:, groups, cols], in_=yc[:, groups, cols].bitcast(I32))

        def store_scales(rows, queues):
            cols = slice(P * rows[0], P * (rows[0] + len(rows)))
            for q in range(4):
                queues[q % len(queues)].dma_start(
                    out=out_2[:, 4 * q : 4 * q + 4, cols].rearrange("h r m -> r h m").bitcast(I32),
                    in_=ys[32 * q : 32 * q + 4, :, cols].bitcast(I32),
                )

        split = "p g (u e) -> p g u e"

        def c_turn():
            bk = bank("bk_c")
            words = cb_rows[:].bitcast(F32)
            for u in range(2):
                nc.tensor.transpose(bk[:, P * u : P * (u + 1)], words[:, u:256:2], ident[:])
            live["cb"] = bk[:, 0 : 2 * P].bitcast(BF16).rearrange("p (u r e) -> p r u e", u=2, e=2)

        def c_negate():
            nc.vector.tensor_scalar(
                out=c_neg[:].rearrange(split, u=2), in0=live["cb"][:, 0:G], scalar1=-1.0, scalar2=None, op0=ALU.mult
            )

        def c_guard():
            nc.vector.scalar_tensor_tensor(
                out=c_safe[:], in0=c_neg[:], scalar=0.0, in1=c_neg[:], op0=ALU.is_equal, op1=ALU.add
            )

        def c_invert():
            nc.vector.reciprocal(out=c_inv[:], in_=c_safe[:])

        def b_divide():
            nc.vector.tensor_tensor(
                out=b_over_c[:].rearrange(split, u=2),
                in0=live["cb"][:, G : 2 * G],
                in1=c_inv[:].rearrange(split, u=2),
                op=ALU.mult,
            )

        def warm_quant(k):
            cols = slice(P * k, P * (k + 1))
            nc.vector.quantize_mx(out=warm_c[:, cols].bitcast(FP8X4), scales=warm_s[:, cols], in_=warm_in[:])

        def warm_pass(*widths):
            bk = bank("bk_w")
            for n in widths:
                nc.tensor.matmul_mx(
                    out=bk[:, 0:n],
                    lhsT=warm_c[:, 0:P].bitcast(FP8X4),
                    lhsT_scale=warm_s[:, 0:P],
                    rhs=warm_c[:, 0:n].bitcast(FP8X4),
                    rhs_scale=warm_s[:, 0:n],
                    start=True,
                    stop=True,
                )

        def clear(tile_ap):
            nc.vector.memset(tile_ap.bitcast(I32), 0)

        lo, hi = slice(0, P), slice(P, HALF)

        make_identity(nc, ident[:])
        warm_in = kept("warm_in", [P, 512], BF16)
        warm_c = kept("warm_c", [P, 512], U32)
        warm_s = kept("warm_s", [P, 512], U8)
        clear(warm_in[:])
        clear(ws[0][:].rearrange("p g n -> p (g n)"))
        warm_quant(0)
        warm_quant(1)
        clear(cb_rows[:])
        warm_quant(2)
        warm_quant(3)
        for t in range(4):
            load_u(0, t, t + 1)
        load_cb()
        load_w(0)
        u_sort(0, 1, 2)
        clear(xs[:].rearrange("p g n -> p (g n)"))
        u_sort(0, 2, 3)
        clear(ws[1][:].rearrange("p g n -> p (g n)"))
        u_sort(0, 3, 4)
        load_z(0, 0)
        load_scales(xs, x_scales, slice(0, I))
        load_x(0)
        load_u(1, 0, 2)
        load_w(1)
        load_u(1, 2, 4)
        load_z(0, 1)
        load_u(2, 0, 2)
        load_x(1)
        load_z(1, 0)
        load_u(2, 2, 4)
        load_z(1, 1)
        load_z(2, 0)
        load_z(2, 1)

        with nc.allow_non_contiguous_dma(reason="one value of a to each partition"):
            nc.sync.dma_start(out=a_sb[:, :, 0], in_=a.rearrange("(r p) -> p r", p=P))
        nc.sync.dma_start(out=gain_sb[:], in_=gain.partition_broadcast(P))
        nc.scalar.activation(out=warm[:], in_=ident[:, 0:1], func=ACT.Sigmoid)
        for t in range(4):
            if t == 0:
                warm_pass(256, 256, 512, 256)
            if t == 2:
                warm_pass(512, 512)
            u_turn(0, t)
            u_copy(0, t)
        for t in range(2):
            u_quant(0, t, t + 1)
            for s in range(4):
                b_mul(0, 0, s, [t])
        z_sort(0, 0)
        u_quant(0, 2, 3)
        u_quant(0, 3, 4)
        z_turn(0, 0)
        c_turn()
        for s in range(4):
            b_mul(0, 0, s, [2, 3])
            b_copy(0, 0, s)
        c_negate()
        c_guard()
        z_scale(0, 0)
        c_invert()
        u_sort(1, 0, 1)
        b_divide()
        u_sort(1, 1, 2)
        r_front(0, 0)
        b_quant(0, 0)
        u_sort(1, 2, 4)
        z_sort(0, 1)
        r_make(0, 0, nc.gpsimd, "u_raw1_2", lo)
        b_bank(0, 1, 0)
        b_bank(0, 1, 1, on_vector)
        b_bank(0, 1, 2, on_vector)
        for t in range(4):
            u_turn(1, t)
            u_copy(1, t)
        z_turn(0, 1)
        z_scale(0, 1)
        u_sort(2, 0, 2)
        u_quant(1, 0, 2)
        z_sort(1, 0)
        b_bank(0, 1, 3)
        r_make(0, 0, nc.gpsimd, "z_raw1_0", hi)
        u_sort(2, 2, 4, on_gpsimd)
        u_quant(1, 2, 4)
        for u in range(2):
            logits(0, 1, u)
        for t in range(2):
            u_turn(2, t)
            u_copy(2, t)
        z_turn(1, 0)
        margin(0, 1, 0)
        sigmoid(0, 1, 0)
        z_sort(1, 1, on_scalar)
        z_scale(1, 0)
        margin(0, 1, 1)
        sigmoid(0, 1, 1)
        for u in range(2):
            logits(1, 0, u)
            margin(1, 0, u)
        z_sort(2, 0)
        z_sort(2, 1)
        b_bank(1, 0, 0)
        sigmoid(1, 0, 0)
        b_bank(1, 0, 1)
        sigmoid(1, 0, 1)
        b_bank(1, 0, 2)
        b_mul(1, 0, 3)
        b_quant(0, 1)
        u_quant(2, 0, 2)
        r_quant(0, 0, lo)
        r_make(0, 1, nc.gpsimd, "ug0")
        r_quant(0, 0, hi)
        z_turn(1, 1)
        for t in range(2, 4):
            u_turn(2, t)
        b_copy(1, 0, 3)
        for t in range(2, 4):
            u_copy(2, t)
        z_turn(2, 0)
        z_turn(2, 1)
        z_scale(1, 1)
        z_scale(2, 0)
        z_scale(2, 1)
        r_front(1, 1)
        for s in range(4):
            b_bank(1, 1, s)
        u_quant(2, 2, 4)
        r_quant(0, 1)
        r_make(1, 0, nc.gpsimd, "ug0")
        b_quant(1, 0)
        r_make(1, 1, nc.gpsimd, "rb2", lo)
        r_front(2, 0)
        r_front(2, 1)
        for s in range(4):
            b_bank(2, 0, s, on_vector if s < 2 else on_scalar)
        r_make(2, 0, nc.vector, "rb1")
        r_quant(1, 0)
        r_quant(2, 0)
        b_quant(2, 0)
        r_quant(1, 1, lo)
        r_make(2, 1, nc.vector, "rb1", lo)
        b_quant(1, 1)
        for s in range(4):
            b_bank(2, 1, s)
        b_quant(2, 1)
        r_make(1, 1, nc.gpsimd, "bb2", hi)
        r_quant(2, 1, lo)
        r_make(2, 1, nc.gpsimd, "rb2", hi)
        for h, r in ((0, 0), (0, 1), (1, 0), (1, 1), (0, 2)):
            y_tile(h, r)
        y_mul(1, 2)
        r_quant(1, 1, hi)
        r_quant(2, 1, hi)
        y_scale(1, 2)
        y_round(1, 2, on_vector)
        for h in range(NH):
            y_turn((h, 0), (h, 1))
            y_copy(h, [0, 1])
        y_quant(0, [0, 1])
        y_tile(0, 3, 2)
        y_quant(1, [0, 1])
        store_words([0, 1])
        y_mul(1, 3)
        y_turn((0, 2))
        y_turn((1, 2))
        y_round_from_bank(1, 3)
        y_copy(0, [2])
        y_copy(1, [2])
        y_turn((0, 3))
        y_turn((1, 3))
        y_scale(1, 3)
        y_copy(0, [3])
        y_copy(1, [3])
        for r in range(2, IT):
            for h in range(NH):
                y_quant(h, [r])
            store_words([r])
        store_scales([0, 1, 2, 3], [nc.scalar, nc.sync])
